import numpy as np
import ml_dtypes


def mxq(x, axis, fmt="e4m3"):
    dtype, down = {"e4m3": (ml_dtypes.float8_e4m3fn, 7), "e5m2": (ml_dtypes.float8_e5m2, 14)}[fmt]
    v = np.moveaxis(np.asarray(x, np.float32).astype(ml_dtypes.bfloat16).astype(np.float64), axis, -1)
    blocks = v.reshape(v.shape[:-1] + (-1, 32))
    amax = np.abs(blocks).max(-1, keepdims=True)
    byte = np.maximum(np.where(amax > 0, np.frexp(amax)[1] - 1 + 127, 0) - down, 1)
    scale = np.exp2(byte - 127.0)
    codes = (blocks / scale).astype(np.float32).astype(dtype).astype(np.float64)
    return np.moveaxis((codes * scale).reshape(v.shape), -1, axis)


WIDE = False


def mx_kscale(k):
    if not WIDE:
        return np.ones(k)
    levels = np.array([10, -10, 5, -5, 0])
    if k % 512:
        return np.exp2(np.random.permutation(np.resize(levels, k // 32))).repeat(32)
    a = np.empty((k // 512, 16))
    for p in range(k // 512):
        a[p, :8] = np.random.permutation(np.resize(levels, 8))
        for g in range(8):
            far = levels[np.abs(levels - a[p, g]) >= 10]
            a[p, g + 8] = far[np.random.randint(len(far))]
    return np.exp2(a.ravel()).repeat(32)


def f64(x):
    return np.asarray(x).astype(np.float64)


def striped(idx):
    return np.tile(idx.reshape(-1, 16).T, (8, 1)).astype(np.uint16)


def unstriped(offs):
    return offs[:16].T.reshape(-1).astype(np.int64)


E2M1 = np.array([0.0, 0.5, 1.0, 1.5, 2.0, 3.0, 4.0, 6.0, -0.0, -0.5, -1.0, -1.5, -2.0, -3.0, -4.0, -6.0])


def pack_weight(w, fmt):
    k, n = w.shape
    w = f64(np.asarray(w, np.float32).astype(ml_dtypes.bfloat16)).reshape(k // 32, 32, n)
    amax = np.abs(w).max(1)
    if fmt == "e4m3":
        byte = np.frexp(amax)[1] - 1 + 127 - 7
    else:
        mant, ex = np.frexp(amax / 6.0)
        byte = np.where(mant > 0.5, ex, ex - 1) + 127
    byte = np.clip(np.where(amax > 0, byte, 1), 1, 254)
    scaled = (w * np.exp2(127.0 - byte)[:, None, :]).reshape(k, n).astype(np.float32)
    by_word = np.ascontiguousarray(scaled.reshape(k // 512, 128, 4, n).transpose(0, 1, 3, 2))
    if fmt == "e4m3":
        words = by_word.astype(ml_dtypes.float8_e4m3fn).view(np.uint8)
    else:
        c = by_word.astype(ml_dtypes.float4_e2m1fn).view(np.uint8) & 0xF
        words = (c[..., 0::2] | (c[..., 1::2] << 4)).reshape(k // 512, 128, 2 * n)
    return np.ascontiguousarray(words), np.ascontiguousarray(byte.astype(np.uint8).reshape(k // 512, 16, n))


def unpack_weight(words, scales, fmt):
    g, _, n = scales.shape
    words = np.ascontiguousarray(words).reshape(g, 128, n, -1)
    if fmt == "e4m3":
        vals = words.view(ml_dtypes.float8_e4m3fn).astype(np.float64)
    else:
        nib = np.empty((g, 128, n, 4), np.uint8)
        nib[..., 0::2] = words & 0xF
        nib[..., 1::2] = words >> 4
        vals = E2M1[nib]
    vals = vals * np.repeat(np.exp2(scales.astype(np.float64) - 127.0), 8, axis=1)[..., None]
    return vals.transpose(0, 1, 3, 2).reshape(g * 512, n)


def gelu(v):
    return 0.5 * v * (1.0 + np.tanh(np.sqrt(2.0 / np.pi) * (v + 0.044715 * v**3)))


def bf(x):
    return np.asarray(x, np.float32).astype(ml_dtypes.bfloat16)


def planes(Y):
    n, m = Y.shape
    b = f64(bf(Y)).reshape(n // 32, 32, m)
    amax = np.abs(b).max(1)
    byte = np.clip(np.where(amax > 0, np.frexp(amax)[1] - 1 + 127 - 7, 1), 1, 254)
    codes = (b * np.exp2(127.0 - byte)[:, None, :]).reshape(n, m).astype(np.float32).astype(ml_dtypes.float8_e4m3fn).view(np.uint8)
    words = codes.reshape(n // 512, 128, 4, m).transpose(0, 1, 3, 2)
    return np.ascontiguousarray(words), np.ascontiguousarray(byte.astype(np.uint8).reshape(n // 512, 16, m))


K, H, N, T, S, T2 = 512, 1024, 512, 2048, 1024, 2048

def setup_inputs():
    n = np.random.standard_normal
    s = mx_kscale(K)[:, None]
    u = mx_kscale(H)[:, None]
    tab_words, tab_scales = pack_weight(n((K, T)) * s, "e4m3")
    w1 = n((K, H)) / np.sqrt(K) / s * u.T
    w2_words, w2_scales = pack_weight(n((K, H)) / np.sqrt(K) / s, "e2m1")
    w3 = n((K, H)) / np.sqrt(K) / s
    w4_words, w4_scales = pack_weight(n((H, N)) / np.sqrt(H) / u, "e4m3")
    return {
        "tab_words": tab_words, "tab_scales": tab_scales,
        "offs": striped(np.random.permutation(T)[:S]),
        "offs2": striped(np.random.permutation(T2)[:S]),
        "w1": w1.astype(np.float32),
        "w2_words": w2_words, "w2_scales": w2_scales,
        "w3": w3.astype(np.float32),
        "wgs": np.exp(0.3 * n((128, S))).astype(np.float32),
        "page0": (n((H, T2)) * u).astype(np.float32),
        "w4_words": w4_words, "w4_scales": w4_scales,
        "b4": n(N).astype(np.float32),
    }

def reference(tab_words, tab_scales, offs, offs2, w1, w2_words, w2_scales, w3, wgs, page0, w4_words, w4_scales, b4):
    v = unpack_weight(tab_words, tab_scales, "e4m3")[:, unstriped(offs)]
    a = mxq(f64(w1), 0, "e4m3").T @ v
    b = unpack_weight(w2_words, w2_scales, "e2m1").T @ v
    c = mxq(f64(w3), 0, "e4m3").T @ v
    h = a * b * c
    page = f64(page0).copy()
    page[:, unstriped(offs2)] = np.tile(f64(wgs), (H // 128, 1)) * h
    words, scales = planes(page)
    y = (unpack_weight(w4_words, w4_scales, "e4m3").T @ mxq(page, 0, "e4m3")) + f64(b4)[:, None]
    return y, page, words, scales

@@ -1,0 +1,294 @@
+from contextlib import ExitStack
+
+import concourse.mybir as mybir
+
+K, H, N, T, S, T2 = 512, 1024, 512, 2048, 1024, 2048
+FLOPS = 2 * (3 * K * H * S + H * N * T2)
+
+F32 = mybir.dt.float32
+BF16 = mybir.dt.bfloat16
+I32 = mybir.dt.int32
+U32 = mybir.dt.uint32
+U16 = mybir.dt.uint16
+U8 = mybir.dt.uint8
+FP8X4 = mybir.dt.float8_e4m3fn_x4
+FP4X4 = mybir.dt.float4_e2m1fn_x4
+MULT = mybir.AluOpType.mult
+ADD = mybir.AluOpType.add
+IDENTITY = mybir.ActivationFunctionType.Identity
+
+P = 128
+PACK = 4
+PASS = P * PACK
+BANK = 512
+GROUPS = H // PASS
+TILES = GROUPS * PACK
+HALVES = S // BANK
+CHUNKS = T2 // BANK
+N_TILES = N // P
+QUADS = 4
+PER_COLUMN = 16
+
+
+def tile_list_clue_memory_triple_kernel(
+    tc, tab_words, tab_scales, offs, offs2, w1, w2_words, w2_scales, w3, wgs, page0,
+    w4_words, w4_scales, b4, out_0, out_1, out_2, out_3,
+):
+    nc = tc.nc
+    with ExitStack() as ctx:
+        keep = ctx.enter_context(tc.tile_pool(name="keep", bufs=1))
+        raw_pool = ctx.enter_context(tc.tile_pool(name="raw", bufs=4))
+        woven_pool = ctx.enter_context(tc.tile_pool(name="woven", bufs=4))
+        rounded_pool = ctx.enter_context(tc.tile_pool(name="rounded", bufs=2))
+        psum = ctx.enter_context(tc.psum_pool(name="psum", bufs=1))
+        banks = [psum.tile([P, BANK], F32, name="bank%d" % n) for n in range(8)]
+
+        def held(name, shape, dtype):
+            return keep.tile(shape, dtype, name=name, align_bytes=64)
+
+        pick = keep.tile([P, S // PER_COLUMN], U16, name="pick")
+        place = keep.tile([P, S // PER_COLUMN], U16, name="place")
+        table_words = held("table_words", [P, T], U32)
+        table_scales = held("table_scales", [P, T], U8)
+        landed_scales = held("landed_scales", [P, T], U8)
+        picked_words = [held("picked_words%d" % h, [P, BANK], U32) for h in range(HALVES)]
+        c_bufs = [held("c%d" % n, [P, S], F32) for n in range(2)]
+        hw_bufs = [held("hw%d" % n, [P, S], F32) for n in range(3)]
+        picked_scales = [held("picked_scales%d" % h, [P, BANK], U8) for h in range(HALVES)]
+        w2_raw = held("w2_raw", [P, 2 * H], U8)
+        w2_raw_scales = held("w2_raw_scales", [P, H], U8)
+        w2_codes = held("w2_codes", [P, 2 * H], U8)
+        w2_planes = held("w2_planes", [P, H], U8)
+        w_codes = {(w, g): held("w%d_codes%d" % (w, g), [P, PASS], U32) for w in (1, 3) for g in range(GROUPS)}
+        w_planes = {(w, g): held("w%d_planes%d" % (w, g), [P, PASS], U8) for w in (1, 3) for g in range(GROUPS)}
+        w4_codes = held("w4_codes", [P, GROUPS * N], U32)
+        w4_planes = held("w4_planes", [P, GROUPS * N], U8)
+        bias = held("bias", [P, N_TILES], F32)
+        gains = [held("gain0", [P, 1, S], F32), held("gain1", [P, 1, S], F32), held("gain23", [P, 2, S], F32)]
+        pages = [held("page%d" % i, [P, T2], F32) for i in range(TILES)]
+        page_codes = [held("page_codes%d" % g, [P, T2], U32) for g in range(GROUPS)]
+        page_planes = [held("page_planes%d" % g, [P, T2], U8) for g in range(GROUPS)]
+
+        page_rows = page0.rearrange("(g p t) m -> g t p m", p=P, t=PACK)
+        out_rows = out_1.rearrange("(g p t) m -> g t p m", p=P, t=PACK)
+        gain_rows = wgs.rearrange("(u t) j -> u t j", t=PACK)
+
+        def gain(t):
+            return gains[min(t, 2)][:, max(t - 2, 0), :]
+
+        def load_scale_rows(queue, plane, rows):
+            passes = rows.shape[0]
+            for q in range(QUADS):
+                queue.dma_start(
+                    out=plane[32 * q : 32 * q + 4, :].bitcast(I32).rearrange("r (a c) -> r a c", a=passes),
+                    in_=rows[:, 4 * q : 4 * q + 4, :].bitcast(I32).rearrange("a r c -> r a c"),
+                )
+
+        def load_gain(tile, t0, t1):
+            for q in (0, 2, 1, 3):
+                nc.sync.dma_start(out=tile[32 * q : 32 * q + 32, :, :], in_=gain_rows[:, t0:t1, :])
+
+        def load_weight(w, g):
+            raw = raw_pool.tile([P, PACK, PASS], F32, name="raw")
+            nc.sync.dma_start(out=raw[:], in_=w[:, g * PASS : (g + 1) * PASS].rearrange("(p j) c -> p j c", j=PACK))
+            return raw
+
+        def load_page(i):
+            nc.sync.dma_start(out=pages[i][:], in_=page_rows[i // PACK, i % PACK])
+
+        def woven_tile():
+            return woven_pool.tile([P, PACK * PASS], BF16, name="woven", align_bytes=64)
+
+        def round_weight(raw, grouped, on_vector):
+            dst = grouped[:].rearrange("p (t m j) -> p m j t", t=PACK, j=PACK)
+            src = raw[:].rearrange("p j (m t) -> p m j t", t=PACK)
+            if on_vector:
+                nc.vector.tensor_copy(out=dst, in_=src)
+            else:
+                nc.scalar.activation(out=dst, in_=src, func=IDENTITY)
+            return grouped
+
+        def quantize_weight(grouped, w, g):
+            nc.vector.quantize_mx(out=w_codes[w, g][:].bitcast(FP8X4), scales=w_planes[w, g][:], in_=grouped[:])
+
+        def gather(picked, table, h):
+            entries = pick[:, h * BANK // PER_COLUMN : (h + 1) * BANK // PER_COLUMN]
+            nc.vector.tensor_copy(out=picked[h][:], in_=table[:].indirect(entries))
+
+        nc.vector.memset(w2_raw_scales[:].bitcast(I32), 0)
+        nc.vector.memset(table_scales[:].bitcast(I32), 0)
+        nc.vector.memset(w4_planes[:].bitcast(I32), 0)
+        nc.sync.dma_start(pick[:], offs)
+        load_scale_rows(nc.sync, landed_scales, tab_scales)
+        nc.sync.dma_start(out=w2_raw[:].bitcast(I32), in_=w2_words[0].bitcast(I32))
+        nc.sync.dma_start(out=table_words[:].bitcast(I32), in_=tab_words[0].rearrange("p t i -> p (t i)").bitcast(I32))
+        raw1 = load_weight(w1, 0)
+        load_scale_rows(nc.sync, w2_raw_scales, w2_scales)
+        raw3 = load_weight(w3, 0)
+        load_gain(gains[0], 0, 1)
+        nc.sync.dma_start(place[:], offs2)
+        load_gain(gains[1], 1, 2)
+        load_page(0)
+        load_gain(gains[2], 2, 4)
+        load_page(1)
+
+        for q in range(QUADS):
+            rows = slice(32 * q, 32 * q + 4)
+            nc.vector.tensor_copy(out=table_scales[rows, :].bitcast(I32), in_=landed_scales[rows, :].bitcast(I32))
+        gather(picked_scales, table_scales, 0)
+        gather(picked_scales, table_scales, 1)
+        nc.vector.tensor_copy(
+            out=w2_codes[:].bitcast(U16).rearrange("p (g t m) -> p g m t", g=GROUPS, t=PACK),
+            in_=w2_raw[:].bitcast(U16).rearrange("p (g m t) -> p g m t", g=GROUPS, t=PACK),
+        )
+        gather(picked_words, table_words, 0)
+        gather(picked_words, table_words, 1)
+        nc.vector.tensor_copy(
+            out=w2_planes[:].rearrange("p (g t m) -> p g m t", g=GROUPS, t=PACK),
+            in_=w2_raw_scales[:].rearrange("p (g m t) -> p g m t", g=GROUPS, t=PACK),
+        )
+        w1_grouped = round_weight(raw1, woven_tile(), False)
+        w3_grouped = round_weight(raw3, woven_tile(), True)
+        quantize_weight(w1_grouped, 1, 0)
+        quantize_weight(w3_grouped, 3, 0)
+
+        raw1 = load_weight(w1, 1)
+        raw3 = load_weight(w3, 1)
+        load_page(2)
+        load_page(3)
+        for g in range(GROUPS):
+            nc.sync.dma_start(
+                out=w4_codes[:, g * N : (g + 1) * N].bitcast(I32),
+                in_=w4_words[g].rearrange("p c i -> p (c i)").bitcast(I32),
+            )
+        load_scale_rows(nc.sync, w4_planes, w4_scales)
+        for i in range(4, TILES):
+            load_page(i)
+        with nc.allow_non_contiguous_dma(reason="one bias value for each partition"):
+            nc.sync.dma_start(out=bias[:], in_=b4.rearrange("(c p) -> p c", p=P))
+
+        def product(bank, lhs_codes, lhs_plane, h):
+            nc.tensor.matmul_mx(
+                out=bank[:], lhsT=lhs_codes, lhsT_scale=lhs_plane,
+                rhs=picked_words[h][:].bitcast(FP8X4), rhs_scale=picked_scales[h][:], start=True, stop=True,
+            )
+            return bank
+
+        rounded = [rounded_pool.tile([P, PACK * T2], BF16, name="rounded") for g in range(GROUPS)]
+
+        def plane(i):
+            return rounded[i // PACK][:, (i % PACK) * T2 : (i % PACK + 1) * T2]
+
+        def products(i, h):
+            g, t = divmod(i, PACK)
+            cols = slice(t * P, (t + 1) * P)
+            bank_a = product(banks[4 + 2 * (i % 2) + h], w_codes[1, g][:, cols].bitcast(FP8X4), w_planes[1, g][:, cols], h)
+            bank_b = product(banks[h], w2_codes[:, 2 * i * P : 2 * (i + 1) * P].bitcast(FP4X4), w2_planes[:, i * P : (i + 1) * P], h)
+            bank_c = product(banks[2 + h], w_codes[3, g][:, cols].bitcast(FP8X4), w_planes[3, g][:, cols], h)
+            return bank_a, bank_b, bank_c
+
+        def triple(i, first_on_vector):
+            b, c, hw = plane((i - 1) % TILES).bitcast(F32), c_bufs[i % 2], hw_bufs[i % 3]
+            for h in range(HALVES):
+                half = slice(h * BANK, (h + 1) * BANK)
+                bank_a, bank_b, bank_c = products(i, h)
+                nc.vector.tensor_tensor(out=hw[:, half], in0=bank_a[:], in1=gain(i % PACK)[:, half], op=MULT)
+                if first_on_vector and h == 0:
+                    nc.vector.tensor_tensor(out=b[:, half], in0=bank_b[:], in1=hw[:, half], op=MULT)
+                    nc.vector.tensor_tensor(out=hw[:, half], in0=bank_c[:], in1=b[:, half], op=MULT)
+                else:
+                    nc.scalar.copy(out=b[:, half], in_=bank_b[:])
+                    nc.scalar.copy(out=c[:, half], in_=bank_c[:])
+            span = slice(BANK if first_on_vector else 0, S)
+            nc.gpsimd.tensor_tensor(out=b[:, span], in0=b[:, span], in1=c[:, span], op=MULT)
+            nc.gpsimd.tensor_tensor(out=hw[:, span], in0=b[:, span], in1=hw[:, span], op=MULT)
+
+        def scatter(i, cuts):
+            width = S // cuts
+            for h in range(cuts):
+                entries = place[:, h * width // PER_COLUMN : (h + 1) * width // PER_COLUMN]
+                nc.vector.tensor_copy(out=pages[i][:].indirect(entries), in_=hw_bufs[i % 3][:, h * width : (h + 1) * width])
+            nc.sync.dma_start(out=out_rows[i // PACK, i % PACK], in_=pages[i][:])
+
+        def round_page(i, cols):
+            nc.scalar.copy(out=plane(i)[:, cols], in_=pages[i][:, cols])
+
+        def quantize_page(g, chunk, on_vector):
+            cols = slice(chunk * BANK, (chunk + 1) * BANK)
+            woven = woven_tile()[:]
+            dst = woven.rearrange("p (c i t) -> p c t i", i=4, t=PACK)
+            src = rounded[g][:].rearrange("p (t m) -> p t m", t=PACK)[:, :, cols].rearrange("p t (c i) -> p c t i", i=4)
+            if on_vector:
+                nc.vector.tensor_copy(out=dst, in_=src)
+            else:
+                nc.scalar.copy(out=dst, in_=src)
+            nc.vector.quantize_mx(out=page_codes[g][:, cols].bitcast(FP8X4), scales=page_planes[g][:, cols], in_=woven)
+
+        def store_planes(g):
+            for q in range(QUADS):
+                nc.sync.dma_start(
+                    out=out_3[g, 4 * q : 4 * q + 4, :].bitcast(I32), in_=page_planes[g][32 * q : 32 * q + 4, :].bitcast(I32)
+                )
+
+        def store_codes(g, cols):
+            nc.sync.dma_start(
+                out=out_2[g].rearrange("p m t -> p (m t)").bitcast(I32)[:, cols], in_=page_codes[g][:, cols].bitcast(I32)
+            )
+
+        sums = {}
+
+        def read_pass(g, chunk):
+            cols = slice(chunk * BANK, (chunk + 1) * BANK)
+            for n in range(N_TILES):
+                if g == 0:
+                    sums[chunk, n] = banks[(chunk % 2) * N_TILES + n]
+                w4_cols = slice(g * N + n * P, g * N + (n + 1) * P)
+                nc.tensor.matmul_mx(
+                    out=sums[chunk, n][:], lhsT=w4_codes[:, w4_cols].bitcast(FP8X4), lhsT_scale=w4_planes[:, w4_cols],
+                    rhs=page_codes[g][:, cols].bitcast(FP8X4), rhs_scale=page_planes[g][:, cols],
+                    start=(g == 0), stop=(g == GROUPS - 1),
+                )
+
+        def store_features(chunk, staged):
+            cols = slice(chunk * BANK, (chunk + 1) * BANK)
+            for n in range(N_TILES):
+                y = staged[:, n, :]
+                if n == N_TILES - 1:
+                    nc.vector.tensor_scalar(
+                        out=y, in0=sums[chunk, n][:], scalar1=bias[:, n : n + 1], scalar2=None, op0=ADD
+                    )
+                else:
+                    nc.scalar.activation(out=y, in_=sums[chunk, n][:], func=IDENTITY, bias=bias[:, n : n + 1])
+                nc.sync.dma_start(out=out_0[n * P : (n + 1) * P, cols], in_=y)
+
+        triple(0, True)
+        triple(1, False)
+        for i in range(TILES):
+            if i == TILES - 1:
+                read_pass(0, 0)
+                read_pass(0, 1)
+            scatter(i, HALVES if i == 0 else 1)
+            if i + 2 < TILES:
+                triple(i + 2, False)
+            if i == 0:
+                quantize_weight(round_weight(raw1, woven_tile(), False), 1, 1)
+            if i == 1:
+                quantize_weight(round_weight(raw3, woven_tile(), False), 3, 1)
+            if i < TILES - 1:
+                round_page(i, slice(0, T2))
+            if 3 <= i < 3 + CHUNKS:
+                quantize_page(0, i - 3, False)
+            if i == TILES - 2:
+                store_codes(0, slice(0, T2))
+                store_planes(0)
+
+        for chunk in range(CHUNKS):
+            cols = slice(chunk * BANK, (chunk + 1) * BANK)
+            round_page(TILES - 1, cols)
+            quantize_page(1, chunk, True)
+            read_pass(1, chunk)
+            store_features(chunk, raw_pool.tile([P, N_TILES, BANK], F32, name="raw"))
+            store_codes(1, cols)
+            if chunk + 2 < CHUNKS:
+                read_pass(0, chunk + 2)
+        store_planes(1)

@@ -50,7 +50,6 @@ def tile_list_clue_memory_triple_kernel(
         place = keep.tile([P, S // PER_COLUMN], U16, name="place")
         table_words = held("table_words", [P, T], U32)
         table_scales = held("table_scales", [P, T], U8)
-        landed_scales = held("landed_scales", [P, T], U8)
         picked_words = [held("picked_words%d" % h, [P, BANK], U32) for h in range(HALVES)]
         c_bufs = [held("c%d" % n, [P, S], F32) for n in range(2)]
         hw_bufs = [held("hw%d" % n, [P, S], F32) for n in range(3)]
@@ -64,7 +63,7 @@ def tile_list_clue_memory_triple_kernel(
         w4_codes = held("w4_codes", [P, GROUPS * N], U32)
         w4_planes = held("w4_planes", [P, GROUPS * N], U8)
         bias = held("bias", [P, N_TILES], F32)
-        gains = [held("gain0", [P, 1, S], F32), held("gain1", [P, 1, S], F32), held("gain23", [P, 2, S], F32)]
+        gains = [held("gain%d" % t, [P, S], F32) for t in range(PACK)]
         pages = [held("page%d" % i, [P, T2], F32) for i in range(TILES)]
         page_codes = [held("page_codes%d" % g, [P, T2], U32) for g in range(GROUPS)]
         page_planes = [held("page_planes%d" % g, [P, T2], U8) for g in range(GROUPS)]
@@ -72,9 +71,6 @@ def tile_list_clue_memory_triple_kernel(
         page_rows = page0.rearrange("(g p t) m -> g t p m", p=P, t=PACK)
         out_rows = out_1.rearrange("(g p t) m -> g t p m", p=P, t=PACK)
         gain_rows = wgs.rearrange("(u t) j -> u t j", t=PACK)
-
-        def gain(t):
-            return gains[min(t, 2)][:, max(t - 2, 0), :]
 
         def load_scale_rows(queue, plane, rows):
             passes = rows.shape[0]
@@ -84,9 +80,20 @@ def tile_list_clue_memory_triple_kernel(
                     in_=rows[:, 4 * q : 4 * q + 4, :].bitcast(I32).rearrange("a r c -> r a c"),
                 )
 
-        def load_gain(tile, t0, t1):
+        def load_gain(queue, t):
             for q in (0, 2, 1, 3):
-                nc.sync.dma_start(out=tile[32 * q : 32 * q + 32, :, :], in_=gain_rows[:, t0:t1, :])
+                queue.dma_start(out=gains[t][32 * q : 32 * q + 32, :], in_=gain_rows[:, t, :])
+
+        def load_w4_codes():
+            for g in range(GROUPS):
+                nc.sync.dma_start(
+                    out=w4_codes[:, g * N : (g + 1) * N].bitcast(I32),
+                    in_=w4_words[g].rearrange("p c i -> p (c i)").bitcast(I32),
+                )
+
+        def load_bias():
+            with nc.allow_non_contiguous_dma(reason="one bias value for each partition"):
+                nc.sync.dma_start(out=bias[:], in_=b4.rearrange("(c p) -> p c", p=P))
 
         def load_weight(w, g):
             raw = raw_pool.tile([P, PACK, PASS], F32, name="raw")
@@ -96,11 +103,16 @@ def tile_list_clue_memory_triple_kernel(
         def load_page(i):
             nc.sync.dma_start(out=pages[i][:], in_=page_rows[i // PACK, i % PACK])
 
+        rounded = [rounded_pool.tile([P, PACK * T2], BF16, name="rounded", align_bytes=64) for g in range(GROUPS)]
+
+        def plane(i):
+            return rounded[i // PACK][:, (i % PACK) * T2 : (i % PACK + 1) * T2]
+
         def woven_tile():
             return woven_pool.tile([P, PACK * PASS], BF16, name="woven", align_bytes=64)
 
         def round_weight(raw, grouped, on_vector):
-            dst = grouped[:].rearrange("p (t m j) -> p m j t", t=PACK, j=PACK)
+            dst = grouped.rearrange("p (t m j) -> p m j t", t=PACK, j=PACK)
             src = raw[:].rearrange("p j (m t) -> p m j t", t=PACK)
             if on_vector:
                 nc.vector.tensor_copy(out=dst, in_=src)
@@ -109,32 +121,40 @@ def tile_list_clue_memory_triple_kernel(
             return grouped
 
         def quantize_weight(grouped, w, g):
-            nc.vector.quantize_mx(out=w_codes[w, g][:].bitcast(FP8X4), scales=w_planes[w, g][:], in_=grouped[:])
+            nc.vector.quantize_mx(out=w_codes[w, g][:].bitcast(FP8X4), scales=w_planes[w, g][:], in_=grouped)
 
         def gather(picked, table, h):
             entries = pick[:, h * BANK // PER_COLUMN : (h + 1) * BANK // PER_COLUMN]
             nc.vector.tensor_copy(out=picked[h][:], in_=table[:].indirect(entries))
 
-        nc.vector.memset(w2_raw_scales[:].bitcast(I32), 0)
         nc.vector.memset(table_scales[:].bitcast(I32), 0)
+        nc.vector.memset(w2_raw_scales[:].bitcast(I32), 0)
         nc.vector.memset(w4_planes[:].bitcast(I32), 0)
         nc.sync.dma_start(pick[:], offs)
-        load_scale_rows(nc.sync, landed_scales, tab_scales)
         nc.sync.dma_start(out=w2_raw[:].bitcast(I32), in_=w2_words[0].bitcast(I32))
+        load_scale_rows(nc.sync, table_scales, tab_scales)
         nc.sync.dma_start(out=table_words[:].bitcast(I32), in_=tab_words[0].rearrange("p t i -> p (t i)").bitcast(I32))
-        raw1 = load_weight(w1, 0)
         load_scale_rows(nc.sync, w2_raw_scales, w2_scales)
+        raw1 = load_weight(w1, 0)
         raw3 = load_weight(w3, 0)
-        load_gain(gains[0], 0, 1)
+        load_gain(nc.sync, 0)
         nc.sync.dma_start(place[:], offs2)
-        load_gain(gains[1], 1, 2)
+        load_gain(nc.sync, 1)
         load_page(0)
-        load_gain(gains[2], 2, 4)
+        late_raw1 = load_weight(w1, 1)
+        late_raw3 = load_weight(w3, 1)
+        load_gain(nc.sync, 2)
+        load_gain(nc.sync, 3)
         load_page(1)
+        load_page(2)
+        load_page(3)
+        load_page(4)
+        load_w4_codes()
+        load_page(5)
+        load_scale_rows(nc.sync, w4_planes, w4_scales)
+        load_page(6)
+        load_bias()
 
-        for q in range(QUADS):
-            rows = slice(32 * q, 32 * q + 4)
-            nc.vector.tensor_copy(out=table_scales[rows, :].bitcast(I32), in_=landed_scales[rows, :].bitcast(I32))
         gather(picked_scales, table_scales, 0)
         gather(picked_scales, table_scales, 1)
         nc.vector.tensor_copy(
@@ -147,25 +167,10 @@ def tile_list_clue_memory_triple_kernel(
             out=w2_planes[:].rearrange("p (g t m) -> p g m t", g=GROUPS, t=PACK),
             in_=w2_raw_scales[:].rearrange("p (g m t) -> p g m t", g=GROUPS, t=PACK),
         )
-        w1_grouped = round_weight(raw1, woven_tile(), False)
-        w3_grouped = round_weight(raw3, woven_tile(), True)
+        w1_grouped = round_weight(raw1, woven_tile()[:], False)
+        w3_grouped = round_weight(raw3, plane(TILES - 2), True)
         quantize_weight(w1_grouped, 1, 0)
         quantize_weight(w3_grouped, 3, 0)
-
-        raw1 = load_weight(w1, 1)
-        raw3 = load_weight(w3, 1)
-        load_page(2)
-        load_page(3)
-        for g in range(GROUPS):
-            nc.sync.dma_start(
-                out=w4_codes[:, g * N : (g + 1) * N].bitcast(I32),
-                in_=w4_words[g].rearrange("p c i -> p (c i)").bitcast(I32),
-            )
-        load_scale_rows(nc.sync, w4_planes, w4_scales)
-        for i in range(4, TILES):
-            load_page(i)
-        with nc.allow_non_contiguous_dma(reason="one bias value for each partition"):
-            nc.sync.dma_start(out=bias[:], in_=b4.rearrange("(c p) -> p c", p=P))
 
         def product(bank, lhs_codes, lhs_plane, h):
             nc.tensor.matmul_mx(
@@ -173,11 +178,6 @@ def tile_list_clue_memory_triple_kernel(
                 rhs=picked_words[h][:].bitcast(FP8X4), rhs_scale=picked_scales[h][:], start=True, stop=True,
             )
             return bank
-
-        rounded = [rounded_pool.tile([P, PACK * T2], BF16, name="rounded") for g in range(GROUPS)]
-
-        def plane(i):
-            return rounded[i // PACK][:, (i % PACK) * T2 : (i % PACK + 1) * T2]
 
         def products(i, h):
             g, t = divmod(i, PACK)
@@ -188,11 +188,14 @@ def tile_list_clue_memory_triple_kernel(
             return bank_a, bank_b, bank_c
 
         def triple(i, first_on_vector):
-            b, c, hw = plane((i - 1) % TILES).bitcast(F32), c_bufs[i % 2], hw_bufs[i % 3]
+            b, c, hw = plane(TILES - 2 + i % 2).bitcast(F32), c_bufs[i % 2], hw_bufs[i % 3]
             for h in range(HALVES):
                 half = slice(h * BANK, (h + 1) * BANK)
                 bank_a, bank_b, bank_c = products(i, h)
-                nc.vector.tensor_tensor(out=hw[:, half], in0=bank_a[:], in1=gain(i % PACK)[:, half], op=MULT)
+                if (i, h) in [(i, h) for i in range(4, 8) for h in range(2)]:
+                    nc.scalar.copy(out=hw[:, half], in_=bank_a[:])
+                else:
+                    nc.vector.tensor_tensor(out=hw[:, half], in0=bank_a[:], in1=gains[i % PACK][:, half], op=MULT)
                 if first_on_vector and h == 0:
                     nc.vector.tensor_tensor(out=b[:, half], in0=bank_b[:], in1=hw[:, half], op=MULT)
                     nc.vector.tensor_tensor(out=hw[:, half], in0=bank_c[:], in1=b[:, half], op=MULT)
@@ -200,8 +203,11 @@ def tile_list_clue_memory_triple_kernel(
                     nc.scalar.copy(out=b[:, half], in_=bank_b[:])
                     nc.scalar.copy(out=c[:, half], in_=bank_c[:])
             span = slice(BANK if first_on_vector else 0, S)
-            nc.gpsimd.tensor_tensor(out=b[:, span], in0=b[:, span], in1=c[:, span], op=MULT)
-            nc.gpsimd.tensor_tensor(out=hw[:, span], in0=b[:, span], in1=hw[:, span], op=MULT)
+            if i >= PACK:
+                nc.gpsimd.tensor_tensor(out=hw[:], in0=hw[:], in1=gains[i % PACK][:], op=MULT)
+            bc = plane(0 if i == 2 else PACK + i % 2).bitcast(F32)
+            nc.gpsimd.tensor_tensor(out=bc[:, span], in0=b[:, span], in1=c[:, span], op=MULT)
+            nc.gpsimd.tensor_tensor(out=hw[:, span], in0=bc[:, span], in1=hw[:, span], op=MULT)
 
         def scatter(i, cuts):
             width = S // cuts
@@ -213,9 +219,8 @@ def tile_list_clue_memory_triple_kernel(
         def round_page(i, cols):
             nc.scalar.copy(out=plane(i)[:, cols], in_=pages[i][:, cols])
 
-        def quantize_page(g, chunk, on_vector):
-            cols = slice(chunk * BANK, (chunk + 1) * BANK)
-            woven = woven_tile()[:]
+        def quantize_page(g, cols, on_vector):
+            woven = (last_woven if on_vector else woven_tile())[:, 0 : PACK * (cols.stop - cols.start)]
             dst = woven.rearrange("p (c i t) -> p c t i", i=4, t=PACK)
             src = rounded[g][:].rearrange("p (t m) -> p t m", t=PACK)[:, :, cols].rearrange("p t (c i) -> p c t i", i=4)
             if on_vector:
@@ -236,59 +241,67 @@ def tile_list_clue_memory_triple_kernel(
             )
 
         sums = {}
+        edges = [0, 512, 1024, 1536, 2048]
+        spans = [slice(lo, hi) for lo, hi in zip(edges[:-1], edges[1:])]
 
         def read_pass(g, chunk):
-            cols = slice(chunk * BANK, (chunk + 1) * BANK)
+            cols = spans[chunk]
             for n in range(N_TILES):
                 if g == 0:
-                    sums[chunk, n] = banks[(chunk % 2) * N_TILES + n]
+                    sums[chunk, n] = banks[(chunk % 2) * N_TILES + n][:, 0 : cols.stop - cols.start]
                 w4_cols = slice(g * N + n * P, g * N + (n + 1) * P)
                 nc.tensor.matmul_mx(
-                    out=sums[chunk, n][:], lhsT=w4_codes[:, w4_cols].bitcast(FP8X4), lhsT_scale=w4_planes[:, w4_cols],
+                    out=sums[chunk, n], lhsT=w4_codes[:, w4_cols].bitcast(FP8X4), lhsT_scale=w4_planes[:, w4_cols],
                     rhs=page_codes[g][:, cols].bitcast(FP8X4), rhs_scale=page_planes[g][:, cols],
                     start=(g == 0), stop=(g == GROUPS - 1),
                 )
 
         def store_features(chunk, staged):
-            cols = slice(chunk * BANK, (chunk + 1) * BANK)
+            cols = spans[chunk]
             for n in range(N_TILES):
-                y = staged[:, n, :]
-                if n == N_TILES - 1:
+                y = staged[:, n, 0 : cols.stop - cols.start]
+                if n >= N_TILES - [1, 1, 1, 1][chunk]:
                     nc.vector.tensor_scalar(
-                        out=y, in0=sums[chunk, n][:], scalar1=bias[:, n : n + 1], scalar2=None, op0=ADD
+                        out=y, in0=sums[chunk, n], scalar1=bias[:, n : n + 1], scalar2=None, op0=ADD
                     )
                 else:
-                    nc.scalar.activation(out=y, in_=sums[chunk, n][:], func=IDENTITY, bias=bias[:, n : n + 1])
+                    nc.scalar.activation(out=y, in_=sums[chunk, n], func=IDENTITY, bias=bias[:, n : n + 1])
                 nc.sync.dma_start(out=out_0[n * P : (n + 1) * P, cols], in_=y)
 
         triple(0, True)
         triple(1, False)
+        quantize_weight(round_weight(late_raw1, c_bufs[0][:].bitcast(BF16), False), 1, 1)
+        quantize_weight(round_weight(late_raw3, plane(TILES - 2), False), 3, 1)
+        triple(2, False)
         for i in range(TILES):
             if i == TILES - 1:
                 read_pass(0, 0)
                 read_pass(0, 1)
             scatter(i, HALVES if i == 0 else 1)
-            if i + 2 < TILES:
-                triple(i + 2, False)
-            if i == 0:
-                quantize_weight(round_weight(raw1, woven_tile(), False), 1, 1)
-            if i == 1:
-                quantize_weight(round_weight(raw3, woven_tile(), False), 3, 1)
+            if i == 2:
+                load_page(TILES - 1)
+            if i + 3 < TILES:
+                triple(i + 3, False)
+            if i == PACK:
+                for chunk in range(CHUNKS // 2, CHUNKS):
+                    quantize_page(0, slice(chunk * BANK, (chunk + 1) * BANK), False)
             if i < TILES - 1:
                 round_page(i, slice(0, T2))
-            if 3 <= i < 3 + CHUNKS:
-                quantize_page(0, i - 3, False)
+            if i == PACK - 1:
+                for chunk in range(CHUNKS // 2):
+                    quantize_page(0, slice(chunk * BANK, (chunk + 1) * BANK), False)
             if i == TILES - 2:
                 store_codes(0, slice(0, T2))
                 store_planes(0)
 
-        for chunk in range(CHUNKS):
-            cols = slice(chunk * BANK, (chunk + 1) * BANK)
+        last_woven = woven_tile()
+        for chunk, cols in enumerate(spans):
             round_page(TILES - 1, cols)
-            quantize_page(1, chunk, True)
+            quantize_page(1, cols, True)
+            store_codes(1, cols)
+            if cols.stop == T2:
+                store_planes(1)
             read_pass(1, chunk)
             store_features(chunk, raw_pool.tile([P, N_TILES, BANK], F32, name="raw"))
-            store_codes(1, cols)
-            if chunk + 2 < CHUNKS:
+            if chunk + 2 < len(spans):
                 read_pass(0, chunk + 2)
-        store_planes(1)

@@ -21,13 +21,19 @@ P = 128
 PACK = 4
 PASS = P * PACK
 BANK = 512
+BANKS = 8
 GROUPS = H // PASS
 TILES = GROUPS * PACK
+LAST = TILES - 1
 HALVES = S // BANK
 CHUNKS = T2 // BANK
 N_TILES = N // P
-QUADS = 4
+QUADRANT = 32
+QUADRANTS = P // QUADRANT
+SCALE_ROWS = 4
 PER_COLUMN = 16
+AHEAD = 3
+OFF_VECTOR = TILES - 2
 
 
 def tile_list_clue_memory_triple_kernel(
@@ -37,11 +43,11 @@ def tile_list_clue_memory_triple_kernel(
     nc = tc.nc
     with ExitStack() as ctx:
         keep = ctx.enter_context(tc.tile_pool(name="keep", bufs=1))
-        raw_pool = ctx.enter_context(tc.tile_pool(name="raw", bufs=4))
-        woven_pool = ctx.enter_context(tc.tile_pool(name="woven", bufs=4))
-        rounded_pool = ctx.enter_context(tc.tile_pool(name="rounded", bufs=2))
+        wide_pool = ctx.enter_context(tc.tile_pool(name="wide", bufs=4))
+        woven_pool = ctx.enter_context(tc.tile_pool(name="woven", bufs=CHUNKS))
+        rounded_pool = ctx.enter_context(tc.tile_pool(name="rounded", bufs=GROUPS))
         psum = ctx.enter_context(tc.psum_pool(name="psum", bufs=1))
-        banks = [psum.tile([P, BANK], F32, name="bank%d" % n) for n in range(8)]
+        banks = [psum.tile([P, BANK], F32, name="bank%d" % n) for n in range(BANKS)]
 
         def held(name, shape, dtype):
             return keep.tile(shape, dtype, name=name, align_bytes=64)
@@ -51,130 +57,131 @@ def tile_list_clue_memory_triple_kernel(
         table_words = held("table_words", [P, T], U32)
         table_scales = held("table_scales", [P, T], U8)
         picked_words = [held("picked_words%d" % h, [P, BANK], U32) for h in range(HALVES)]
-        c_bufs = [held("c%d" % n, [P, S], F32) for n in range(2)]
-        hw_bufs = [held("hw%d" % n, [P, S], F32) for n in range(3)]
+        c_tiles = [held("c%d" % n, [P, S], F32) for n in range(2)]
+        value_tiles = [held("values%d" % n, [P, S], F32) for n in range(AHEAD)]
         picked_scales = [held("picked_scales%d" % h, [P, BANK], U8) for h in range(HALVES)]
-        w2_raw = held("w2_raw", [P, 2 * H], U8)
-        w2_raw_scales = held("w2_raw_scales", [P, H], U8)
-        w2_codes = held("w2_codes", [P, 2 * H], U8)
-        w2_planes = held("w2_planes", [P, H], U8)
+        w2_loaded_codes = held("w2_loaded_codes", [P, 2 * H], U8)
+        w2_loaded_scales = held("w2_loaded_scales", [P, H], U8)
+        w2_dealt_codes = held("w2_dealt_codes", [P, 2 * H], U8)
+        w2_dealt_scales = held("w2_dealt_scales", [P, H], U8)
         w_codes = {(w, g): held("w%d_codes%d" % (w, g), [P, PASS], U32) for w in (1, 3) for g in range(GROUPS)}
-        w_planes = {(w, g): held("w%d_planes%d" % (w, g), [P, PASS], U8) for w in (1, 3) for g in range(GROUPS)}
+        w_scales = {(w, g): held("w%d_scales%d" % (w, g), [P, PASS], U8) for w in (1, 3) for g in range(GROUPS)}
         w4_codes = held("w4_codes", [P, GROUPS * N], U32)
-        w4_planes = held("w4_planes", [P, GROUPS * N], U8)
+        w4_scale_tile = held("w4_scale_tile", [P, GROUPS * N], U8)
         bias = held("bias", [P, N_TILES], F32)
         gains = [held("gain%d" % t, [P, S], F32) for t in range(PACK)]
         pages = [held("page%d" % i, [P, T2], F32) for i in range(TILES)]
         page_codes = [held("page_codes%d" % g, [P, T2], U32) for g in range(GROUPS)]
-        page_planes = [held("page_planes%d" % g, [P, T2], U8) for g in range(GROUPS)]
+        page_scales = [held("page_scales%d" % g, [P, T2], U8) for g in range(GROUPS)]
 
         page_rows = page0.rearrange("(g p t) m -> g t p m", p=P, t=PACK)
         out_rows = out_1.rearrange("(g p t) m -> g t p m", p=P, t=PACK)
         gain_rows = wgs.rearrange("(u t) j -> u t j", t=PACK)
 
-        def load_scale_rows(queue, plane, rows):
+        def scale_partitions(q):
+            return slice(QUADRANT * q, QUADRANT * q + SCALE_ROWS)
+
+        def load_scale_rows(scale_tile, rows):
             passes = rows.shape[0]
-            for q in range(QUADS):
-                queue.dma_start(
-                    out=plane[32 * q : 32 * q + 4, :].bitcast(I32).rearrange("r (a c) -> r a c", a=passes),
-                    in_=rows[:, 4 * q : 4 * q + 4, :].bitcast(I32).rearrange("a r c -> r a c"),
-                )
-
-        def load_gain(queue, t):
-            for q in (0, 2, 1, 3):
-                queue.dma_start(out=gains[t][32 * q : 32 * q + 32, :], in_=gain_rows[:, t, :])
-
-        def load_w4_codes():
-            for g in range(GROUPS):
+            for q in range(QUADRANTS):
                 nc.sync.dma_start(
-                    out=w4_codes[:, g * N : (g + 1) * N].bitcast(I32),
-                    in_=w4_words[g].rearrange("p c i -> p (c i)").bitcast(I32),
+                    out=scale_tile[scale_partitions(q), :].bitcast(I32).rearrange("r (a c) -> r a c", a=passes),
+                    in_=rows[:, SCALE_ROWS * q : SCALE_ROWS * (q + 1), :].bitcast(I32).rearrange("a r c -> r a c"),
                 )
 
-        def load_bias():
-            with nc.allow_non_contiguous_dma(reason="one bias value for each partition"):
-                nc.sync.dma_start(out=bias[:], in_=b4.rearrange("(c p) -> p c", p=P))
+        def load_gain(t):
+            for q in (0, 2, 1, 3):
+                nc.sync.dma_start(out=gains[t][QUADRANT * q : QUADRANT * (q + 1), :], in_=gain_rows[:, t, :])
 
         def load_weight(w, g):
-            raw = raw_pool.tile([P, PACK, PASS], F32, name="raw")
-            nc.sync.dma_start(out=raw[:], in_=w[:, g * PASS : (g + 1) * PASS].rearrange("(p j) c -> p j c", j=PACK))
-            return raw
+            loaded = wide_pool.tile([P, PACK, PASS], F32, name="wide")
+            nc.sync.dma_start(out=loaded[:], in_=w[:, g * PASS : (g + 1) * PASS].rearrange("(p j) c -> p j c", j=PACK))
+            return loaded
 
         def load_page(i):
             nc.sync.dma_start(out=pages[i][:], in_=page_rows[i // PACK, i % PACK])
 
         rounded = [rounded_pool.tile([P, PACK * T2], BF16, name="rounded", align_bytes=64) for g in range(GROUPS)]
 
-        def plane(i):
+        def rounded_row(i):
             return rounded[i // PACK][:, (i % PACK) * T2 : (i % PACK + 1) * T2]
 
         def woven_tile():
             return woven_pool.tile([P, PACK * PASS], BF16, name="woven", align_bytes=64)
 
-        def round_weight(raw, grouped, on_vector):
-            dst = grouped.rearrange("p (t m j) -> p m j t", t=PACK, j=PACK)
-            src = raw[:].rearrange("p j (m t) -> p m j t", t=PACK)
-            if on_vector:
-                nc.vector.tensor_copy(out=dst, in_=src)
-            else:
-                nc.scalar.activation(out=dst, in_=src, func=IDENTITY)
-            return grouped
+        def round_weight(loaded, woven, scalar_share):
+            dst = woven.rearrange("p (t m j) -> p m j t", t=PACK, j=PACK)
+            src = loaded[:].rearrange("p j (m t) -> p m j t", t=PACK)
+            nc.scalar.activation(out=dst[:, :, :, :scalar_share], in_=src[:, :, :, :scalar_share], func=IDENTITY)
+            if scalar_share < PACK:
+                nc.vector.tensor_copy(out=dst[:, :, :, scalar_share:], in_=src[:, :, :, scalar_share:])
+            return woven
 
-        def quantize_weight(grouped, w, g):
-            nc.vector.quantize_mx(out=w_codes[w, g][:].bitcast(FP8X4), scales=w_planes[w, g][:], in_=grouped)
+        def quantize_weight(woven, w, g):
+            nc.vector.quantize_mx(out=w_codes[w, g][:].bitcast(FP8X4), scales=w_scales[w, g][:], in_=woven)
 
-        def gather(picked, table, h):
-            entries = pick[:, h * BANK // PER_COLUMN : (h + 1) * BANK // PER_COLUMN]
-            nc.vector.tensor_copy(out=picked[h][:], in_=table[:].indirect(entries))
+        def entries(offsets, first, count):
+            return offsets[:, first // PER_COLUMN : (first + count) // PER_COLUMN]
+
+        def pick_columns(picked, table, h):
+            nc.vector.tensor_copy(out=picked[h][:], in_=table[:].indirect(entries(pick, h * BANK, BANK)))
 
         nc.vector.memset(table_scales[:].bitcast(I32), 0)
-        nc.vector.memset(w2_raw_scales[:].bitcast(I32), 0)
-        nc.vector.memset(w4_planes[:].bitcast(I32), 0)
+        nc.vector.memset(w2_loaded_scales[:].bitcast(I32), 0)
+        nc.vector.memset(w4_scale_tile[:].bitcast(I32), 0)
+
         nc.sync.dma_start(pick[:], offs)
-        nc.sync.dma_start(out=w2_raw[:].bitcast(I32), in_=w2_words[0].bitcast(I32))
-        load_scale_rows(nc.sync, table_scales, tab_scales)
+        nc.sync.dma_start(out=w2_loaded_codes[:].bitcast(I32), in_=w2_words[0].bitcast(I32))
+        load_scale_rows(table_scales, tab_scales)
         nc.sync.dma_start(out=table_words[:].bitcast(I32), in_=tab_words[0].rearrange("p t i -> p (t i)").bitcast(I32))
-        load_scale_rows(nc.sync, w2_raw_scales, w2_scales)
-        raw1 = load_weight(w1, 0)
-        raw3 = load_weight(w3, 0)
-        load_gain(nc.sync, 0)
+        load_scale_rows(w2_loaded_scales, w2_scales)
+        w1_first = load_weight(w1, 0)
+        w3_first = load_weight(w3, 0)
+        load_gain(0)
         nc.sync.dma_start(place[:], offs2)
-        load_gain(nc.sync, 1)
+        load_gain(1)
         load_page(0)
-        late_raw1 = load_weight(w1, 1)
-        late_raw3 = load_weight(w3, 1)
-        load_gain(nc.sync, 2)
-        load_gain(nc.sync, 3)
-        load_page(1)
-        load_page(2)
-        load_page(3)
-        load_page(4)
-        load_w4_codes()
-        load_page(5)
-        load_scale_rows(nc.sync, w4_planes, w4_scales)
-        load_page(6)
-        load_bias()
+        load_gain(2)
+        w1_second = load_weight(w1, 1)
+        w3_second = load_weight(w3, 1)
+        load_gain(3)
+        for i in range(1, LAST - 2):
+            load_page(i)
+        for g in range(GROUPS):
+            nc.sync.dma_start(
+                out=w4_codes[:, g * N : (g + 1) * N].bitcast(I32),
+                in_=w4_words[g].rearrange("p c i -> p (c i)").bitcast(I32),
+            )
+        load_page(LAST - 2)
+        load_scale_rows(w4_scale_tile, w4_scales)
+        load_page(LAST - 1)
+        with nc.allow_non_contiguous_dma(reason="one bias value for each partition"):
+            nc.sync.dma_start(out=bias[:], in_=b4.rearrange("(c p) -> p c", p=P))
 
-        gather(picked_scales, table_scales, 0)
-        gather(picked_scales, table_scales, 1)
+        pick_columns(picked_scales, table_scales, 0)
+        pick_columns(picked_scales, table_scales, 1)
         nc.vector.tensor_copy(
-            out=w2_codes[:].bitcast(U16).rearrange("p (g t m) -> p g m t", g=GROUPS, t=PACK),
-            in_=w2_raw[:].bitcast(U16).rearrange("p (g m t) -> p g m t", g=GROUPS, t=PACK),
+            out=w2_dealt_codes[:].bitcast(U16).rearrange("p (g t m) -> p g m t", g=GROUPS, t=PACK),
+            in_=w2_loaded_codes[:].bitcast(U16).rearrange("p (g m t) -> p g m t", g=GROUPS, t=PACK),
         )
-        gather(picked_words, table_words, 0)
-        gather(picked_words, table_words, 1)
+        pick_columns(picked_words, table_words, 0)
+        pick_columns(picked_words, table_words, 1)
         nc.vector.tensor_copy(
-            out=w2_planes[:].rearrange("p (g t m) -> p g m t", g=GROUPS, t=PACK),
-            in_=w2_raw_scales[:].rearrange("p (g m t) -> p g m t", g=GROUPS, t=PACK),
+            out=w2_dealt_scales[:].rearrange("p (g t m) -> p g m t", g=GROUPS, t=PACK),
+            in_=w2_loaded_scales[:].rearrange("p (g m t) -> p g m t", g=GROUPS, t=PACK),
         )
-        w1_grouped = round_weight(raw1, woven_tile()[:], False)
-        w3_grouped = round_weight(raw3, plane(TILES - 2), True)
-        quantize_weight(w1_grouped, 1, 0)
-        quantize_weight(w3_grouped, 3, 0)
 
-        def product(bank, lhs_codes, lhs_plane, h):
+        def b_tile(i):
+            return rounded_row(TILES - 2 + i % 2)
+
+        w1_woven = round_weight(w1_first, woven_tile()[:], PACK // 2)
+        w3_woven = round_weight(w3_first, b_tile(0), PACK // 4)
+        quantize_weight(w1_woven, 1, 0)
+        quantize_weight(w3_woven, 3, 0)
+
+        def product(bank, codes, scales, h):
             nc.tensor.matmul_mx(
-                out=bank[:], lhsT=lhs_codes, lhsT_scale=lhs_plane,
+                out=bank[:], lhsT=codes, lhsT_scale=scales,
                 rhs=picked_words[h][:].bitcast(FP8X4), rhs_scale=picked_scales[h][:], start=True, stop=True,
             )
             return bank
@@ -182,126 +189,139 @@ def tile_list_clue_memory_triple_kernel(
         def products(i, h):
             g, t = divmod(i, PACK)
             cols = slice(t * P, (t + 1) * P)
-            bank_a = product(banks[4 + 2 * (i % 2) + h], w_codes[1, g][:, cols].bitcast(FP8X4), w_planes[1, g][:, cols], h)
-            bank_b = product(banks[h], w2_codes[:, 2 * i * P : 2 * (i + 1) * P].bitcast(FP4X4), w2_planes[:, i * P : (i + 1) * P], h)
-            bank_c = product(banks[2 + h], w_codes[3, g][:, cols].bitcast(FP8X4), w_planes[3, g][:, cols], h)
-            return bank_a, bank_b, bank_c
+            a_bank, b_bank, c_bank = banks[2 * HALVES + HALVES * (i % 2) + h], banks[h], banks[HALVES + h]
+            product(a_bank, w_codes[1, g][:, cols].bitcast(FP8X4), w_scales[1, g][:, cols], h)
+            product(
+                b_bank, w2_dealt_codes[:, 2 * i * P : 2 * (i + 1) * P].bitcast(FP4X4), w2_dealt_scales[:, i * P : (i + 1) * P], h
+            )
+            product(c_bank, w_codes[3, g][:, cols].bitcast(FP8X4), w_scales[3, g][:, cols], h)
+            return a_bank, b_bank, c_bank
 
-        def triple(i, first_on_vector):
-            b, c, hw = plane(TILES - 2 + i % 2).bitcast(F32), c_bufs[i % 2], hw_bufs[i % 3]
+        def make_values(i):
+            b, c, values, gain = b_tile(i).bitcast(F32), c_tiles[i % 2], value_tiles[i % AHEAD], gains[i % PACK]
             for h in range(HALVES):
                 half = slice(h * BANK, (h + 1) * BANK)
-                bank_a, bank_b, bank_c = products(i, h)
-                if (i, h) in [(i, h) for i in range(4, 8) for h in range(2)]:
-                    nc.scalar.copy(out=hw[:, half], in_=bank_a[:])
+                a_bank, b_bank, c_bank = products(i, h)
+                if i >= OFF_VECTOR:
+                    nc.scalar.copy(out=values[:, half], in_=a_bank[:])
                 else:
-                    nc.vector.tensor_tensor(out=hw[:, half], in0=bank_a[:], in1=gains[i % PACK][:, half], op=MULT)
-                if first_on_vector and h == 0:
-                    nc.vector.tensor_tensor(out=b[:, half], in0=bank_b[:], in1=hw[:, half], op=MULT)
-                    nc.vector.tensor_tensor(out=hw[:, half], in0=bank_c[:], in1=b[:, half], op=MULT)
+                    nc.vector.tensor_tensor(out=values[:, half], in0=a_bank[:], in1=gain[:, half], op=MULT)
+                if i == 0 and h == 0:
+                    nc.vector.tensor_tensor(out=b[:, half], in0=b_bank[:], in1=values[:, half], op=MULT)
+                    nc.vector.tensor_tensor(out=values[:, half], in0=c_bank[:], in1=b[:, half], op=MULT)
                 else:
-                    nc.scalar.copy(out=b[:, half], in_=bank_b[:])
-                    nc.scalar.copy(out=c[:, half], in_=bank_c[:])
-            span = slice(BANK if first_on_vector else 0, S)
-            if i >= PACK:
-                nc.gpsimd.tensor_tensor(out=hw[:], in0=hw[:], in1=gains[i % PACK][:], op=MULT)
-            bc = plane(0 if i == 2 else PACK + i % 2).bitcast(F32)
-            nc.gpsimd.tensor_tensor(out=bc[:, span], in0=b[:, span], in1=c[:, span], op=MULT)
-            nc.gpsimd.tensor_tensor(out=hw[:, span], in0=bc[:, span], in1=hw[:, span], op=MULT)
+                    nc.scalar.copy(out=b[:, half], in_=b_bank[:])
+                    nc.scalar.copy(out=c[:, half], in_=c_bank[:])
+            span = slice(BANK if i == 0 else 0, S)
+            if i >= OFF_VECTOR:
+                nc.gpsimd.tensor_tensor(out=values[:], in0=values[:], in1=gain[:], op=MULT)
+            if i == LAST:
+                nc.gpsimd.tensor_tensor(out=b, in0=b, in1=c[:], op=MULT)
+            else:
+                bc = rounded_row(0 if i == 2 else PACK + i % 2).bitcast(F32)
+                nc.gpsimd.tensor_tensor(out=bc[:, span], in0=b[:, span], in1=c[:, span], op=MULT)
+                nc.gpsimd.tensor_tensor(out=values[:, span], in0=bc[:, span], in1=values[:, span], op=MULT)
 
-        def scatter(i, cuts):
-            width = S // cuts
-            for h in range(cuts):
-                entries = place[:, h * width // PER_COLUMN : (h + 1) * width // PER_COLUMN]
-                nc.vector.tensor_copy(out=pages[i][:].indirect(entries), in_=hw_bufs[i % 3][:, h * width : (h + 1) * width])
+        def place_values(i):
+            values = value_tiles[i % AHEAD]
+            if i == LAST:
+                nc.vector.tensor_tensor(out=pages[i][:].indirect(place[:]), in0=values[:], in1=b_tile(i).bitcast(F32), op=MULT)
+            else:
+                width = BANK if i == 0 else S
+                for first in range(0, S, width):
+                    nc.vector.tensor_copy(
+                        out=pages[i][:].indirect(entries(place, first, width)), in_=values[:, first : first + width]
+                    )
             nc.sync.dma_start(out=out_rows[i // PACK, i % PACK], in_=pages[i][:])
 
+        def chunk_columns(chunk):
+            return slice(chunk * BANK, (chunk + 1) * BANK)
+
         def round_page(i, cols):
-            nc.scalar.copy(out=plane(i)[:, cols], in_=pages[i][:, cols])
+            nc.scalar.copy(out=rounded_row(i)[:, cols], in_=pages[i][:, cols])
 
-        def quantize_page(g, cols, on_vector):
-            woven = (last_woven if on_vector else woven_tile())[:, 0 : PACK * (cols.stop - cols.start)]
-            dst = woven.rearrange("p (c i t) -> p c t i", i=4, t=PACK)
-            src = rounded[g][:].rearrange("p (t m) -> p t m", t=PACK)[:, :, cols].rearrange("p t (c i) -> p c t i", i=4)
-            if on_vector:
-                nc.vector.tensor_copy(out=dst, in_=src)
-            else:
-                nc.scalar.copy(out=dst, in_=src)
-            nc.vector.quantize_mx(out=page_codes[g][:, cols].bitcast(FP8X4), scales=page_planes[g][:, cols], in_=woven)
+        def quantize_page(g, chunk, woven, weave):
+            cols = chunk_columns(chunk)
+            rows = rounded[g][:].rearrange("p (t m) -> p t m", t=PACK)[:, :, cols]
+            weave(
+                out=woven[:].rearrange("p (c i t) -> p c t i", i=4, t=PACK), in_=rows.rearrange("p t (c i) -> p c t i", i=4)
+            )
+            nc.vector.quantize_mx(out=page_codes[g][:, cols].bitcast(FP8X4), scales=page_scales[g][:, cols], in_=woven[:])
 
-        def store_planes(g):
-            for q in range(QUADS):
+        def store_page_scales(g):
+            for q in range(QUADRANTS):
                 nc.sync.dma_start(
-                    out=out_3[g, 4 * q : 4 * q + 4, :].bitcast(I32), in_=page_planes[g][32 * q : 32 * q + 4, :].bitcast(I32)
+                    out=out_3[g, SCALE_ROWS * q : SCALE_ROWS * (q + 1), :].bitcast(I32),
+                    in_=page_scales[g][scale_partitions(q), :].bitcast(I32),
                 )
 
-        def store_codes(g, cols):
+        def store_page_codes(g, cols):
             nc.sync.dma_start(
                 out=out_2[g].rearrange("p m t -> p (m t)").bitcast(I32)[:, cols], in_=page_codes[g][:, cols].bitcast(I32)
             )
 
-        sums = {}
-        edges = [0, 512, 1024, 1536, 2048]
-        spans = [slice(lo, hi) for lo, hi in zip(edges[:-1], edges[1:])]
+        def sum_bank(chunk, n):
+            return banks[(chunk % 2) * N_TILES + n]
 
-        def read_pass(g, chunk):
-            cols = spans[chunk]
+        def read_page(g, chunk):
+            cols = chunk_columns(chunk)
             for n in range(N_TILES):
-                if g == 0:
-                    sums[chunk, n] = banks[(chunk % 2) * N_TILES + n][:, 0 : cols.stop - cols.start]
                 w4_cols = slice(g * N + n * P, g * N + (n + 1) * P)
                 nc.tensor.matmul_mx(
-                    out=sums[chunk, n], lhsT=w4_codes[:, w4_cols].bitcast(FP8X4), lhsT_scale=w4_planes[:, w4_cols],
-                    rhs=page_codes[g][:, cols].bitcast(FP8X4), rhs_scale=page_planes[g][:, cols],
+                    out=sum_bank(chunk, n)[:],
+                    lhsT=w4_codes[:, w4_cols].bitcast(FP8X4), lhsT_scale=w4_scale_tile[:, w4_cols],
+                    rhs=page_codes[g][:, cols].bitcast(FP8X4), rhs_scale=page_scales[g][:, cols],
                     start=(g == 0), stop=(g == GROUPS - 1),
                 )
 
-        def store_features(chunk, staged):
-            cols = spans[chunk]
+        def store_features(chunk):
+            features = wide_pool.tile([P, N_TILES, BANK], F32, name="wide")
             for n in range(N_TILES):
-                y = staged[:, n, 0 : cols.stop - cols.start]
-                if n >= N_TILES - [1, 1, 1, 1][chunk]:
+                if n == N_TILES - 1:
                     nc.vector.tensor_scalar(
-                        out=y, in0=sums[chunk, n], scalar1=bias[:, n : n + 1], scalar2=None, op0=ADD
+                        out=features[:, n, :], in0=sum_bank(chunk, n)[:], scalar1=bias[:, n : n + 1], scalar2=None, op0=ADD
                     )
                 else:
-                    nc.scalar.activation(out=y, in_=sums[chunk, n], func=IDENTITY, bias=bias[:, n : n + 1])
-                nc.sync.dma_start(out=out_0[n * P : (n + 1) * P, cols], in_=y)
+                    nc.scalar.activation(
+                        out=features[:, n, :], in_=sum_bank(chunk, n)[:], func=IDENTITY, bias=bias[:, n : n + 1]
+                    )
+                nc.sync.dma_start(out=out_0[n * P : (n + 1) * P, chunk_columns(chunk)], in_=features[:, n, :])
 
-        triple(0, True)
-        triple(1, False)
-        quantize_weight(round_weight(late_raw1, c_bufs[0][:].bitcast(BF16), False), 1, 1)
-        quantize_weight(round_weight(late_raw3, plane(TILES - 2), False), 3, 1)
-        triple(2, False)
+        make_values(0)
+        make_values(1)
+        quantize_weight(round_weight(w1_second, c_tiles[0][:].bitcast(BF16), PACK), 1, 1)
+        quantize_weight(round_weight(w3_second, b_tile(2), PACK), 3, 1)
+        make_values(2)
+
         for i in range(TILES):
-            if i == TILES - 1:
-                read_pass(0, 0)
-                read_pass(0, 1)
-            scatter(i, HALVES if i == 0 else 1)
-            if i == 2:
-                load_page(TILES - 1)
-            if i + 3 < TILES:
-                triple(i + 3, False)
+            if i == LAST:
+                read_page(0, 0)
+                read_page(0, 1)
+            place_values(i)
+            if i == AHEAD - 1:
+                load_page(LAST)
+            if i + AHEAD < TILES:
+                make_values(i + AHEAD)
             if i == PACK:
                 for chunk in range(CHUNKS // 2, CHUNKS):
-                    quantize_page(0, slice(chunk * BANK, (chunk + 1) * BANK), False)
-            if i < TILES - 1:
+                    quantize_page(0, chunk, woven_tile(), nc.scalar.copy)
+            if i < LAST:
                 round_page(i, slice(0, T2))
             if i == PACK - 1:
                 for chunk in range(CHUNKS // 2):
-                    quantize_page(0, slice(chunk * BANK, (chunk + 1) * BANK), False)
-            if i == TILES - 2:
-                store_codes(0, slice(0, T2))
-                store_planes(0)
+                    quantize_page(0, chunk, woven_tile(), nc.scalar.copy)
+            if i == LAST - 1:
+                store_page_codes(0, slice(0, T2))
+                store_page_scales(0)
 
         last_woven = woven_tile()
-        for chunk, cols in enumerate(spans):
-            round_page(TILES - 1, cols)
-            quantize_page(1, cols, True)
-            store_codes(1, cols)
-            if cols.stop == T2:
-                store_planes(1)
-            read_pass(1, chunk)
-            store_features(chunk, raw_pool.tile([P, N_TILES, BANK], F32, name="raw"))
-            if chunk + 2 < len(spans):
-                read_pass(0, chunk + 2)
+        for chunk in range(CHUNKS):
+            round_page(LAST, chunk_columns(chunk))
+            quantize_page(1, chunk, last_woven, nc.vector.tensor_copy)
+            store_page_codes(1, chunk_columns(chunk))
+            if chunk == CHUNKS - 1:
+                store_page_scales(1)
+            read_page(1, chunk)
+            store_features(chunk)
+            if chunk + 2 < CHUNKS:
+                read_page(0, chunk + 2)

@@ -32,8 +32,9 @@ QUADRANT = 32
 QUADRANTS = P // QUADRANT
 SCALE_ROWS = 4
 PER_COLUMN = 16
-AHEAD = 3
-OFF_VECTOR = TILES - 2
+AHEAD = 4
+OFF_VECTOR = PACK
+EARLY_GAINS = 2
 
 
 def tile_list_clue_memory_triple_kernel(
@@ -54,10 +55,11 @@ def tile_list_clue_memory_triple_kernel(
 
         pick = keep.tile([P, S // PER_COLUMN], U16, name="pick")
         place = keep.tile([P, S // PER_COLUMN], U16, name="place")
-        table_words = held("table_words", [P, T], U32)
+        table_words = keep.tile([P, T], U32, name="table_words", tag="table_words", align_bytes=64)
         table_scales = held("table_scales", [P, T], U8)
         picked_words = [held("picked_words%d" % h, [P, BANK], U32) for h in range(HALVES)]
         c_tiles = [held("c%d" % n, [P, S], F32) for n in range(2)]
+        bc_tile = held("bc", [P, S], F32)
         value_tiles = [held("values%d" % n, [P, S], F32) for n in range(AHEAD)]
         picked_scales = [held("picked_scales%d" % h, [P, BANK], U8) for h in range(HALVES)]
         w2_loaded_codes = held("w2_loaded_codes", [P, 2 * H], U8)
@@ -69,7 +71,7 @@ def tile_list_clue_memory_triple_kernel(
         w4_codes = held("w4_codes", [P, GROUPS * N], U32)
         w4_scale_tile = held("w4_scale_tile", [P, GROUPS * N], U8)
         bias = held("bias", [P, N_TILES], F32)
-        gains = [held("gain%d" % t, [P, S], F32) for t in range(PACK)]
+        late_gains = [held("gain%d" % t, [P, S], F32)[:] for t in range(EARLY_GAINS, PACK)]
         pages = [held("page%d" % i, [P, T2], F32) for i in range(TILES)]
         page_codes = [held("page_codes%d" % g, [P, T2], U32) for g in range(GROUPS)]
         page_scales = [held("page_scales%d" % g, [P, T2], U8) for g in range(GROUPS)]
@@ -91,7 +93,8 @@ def tile_list_clue_memory_triple_kernel(
 
         def load_gain(t):
             for q in (0, 2, 1, 3):
-                nc.sync.dma_start(out=gains[t][QUADRANT * q : QUADRANT * (q + 1), :], in_=gain_rows[:, t, :])
+                queue = nc.scalar if t < EARLY_GAINS and q >= QUADRANTS // 2 else nc.sync
+                queue.dma_start(out=gains[t][QUADRANT * q : QUADRANT * (q + 1), :], in_=gain_rows[:, t, :])
 
         def load_weight(w, g):
             loaded = wide_pool.tile([P, PACK, PASS], F32, name="wide")
@@ -112,7 +115,8 @@ def tile_list_clue_memory_triple_kernel(
         def round_weight(loaded, woven, scalar_share):
             dst = woven.rearrange("p (t m j) -> p m j t", t=PACK, j=PACK)
             src = loaded[:].rearrange("p j (m t) -> p m j t", t=PACK)
-            nc.scalar.activation(out=dst[:, :, :, :scalar_share], in_=src[:, :, :, :scalar_share], func=IDENTITY)
+            if scalar_share > 0:
+                nc.scalar.copy(out=dst[:, :, :, :scalar_share], in_=src[:, :, :, :scalar_share])
             if scalar_share < PACK:
                 nc.vector.tensor_copy(out=dst[:, :, :, scalar_share:], in_=src[:, :, :, scalar_share:])
             return woven
@@ -137,26 +141,6 @@ def tile_list_clue_memory_triple_kernel(
         load_scale_rows(w2_loaded_scales, w2_scales)
         w1_first = load_weight(w1, 0)
         w3_first = load_weight(w3, 0)
-        load_gain(0)
-        nc.sync.dma_start(place[:], offs2)
-        load_gain(1)
-        load_page(0)
-        load_gain(2)
-        w1_second = load_weight(w1, 1)
-        w3_second = load_weight(w3, 1)
-        load_gain(3)
-        for i in range(1, LAST - 2):
-            load_page(i)
-        for g in range(GROUPS):
-            nc.sync.dma_start(
-                out=w4_codes[:, g * N : (g + 1) * N].bitcast(I32),
-                in_=w4_words[g].rearrange("p c i -> p (c i)").bitcast(I32),
-            )
-        load_page(LAST - 2)
-        load_scale_rows(w4_scale_tile, w4_scales)
-        load_page(LAST - 1)
-        with nc.allow_non_contiguous_dma(reason="one bias value for each partition"):
-            nc.sync.dma_start(out=bias[:], in_=b4.rearrange("(c p) -> p c", p=P))
 
         pick_columns(picked_scales, table_scales, 0)
         pick_columns(picked_scales, table_scales, 1)
@@ -171,10 +155,35 @@ def tile_list_clue_memory_triple_kernel(
             in_=w2_loaded_scales[:].rearrange("p (g m t) -> p g m t", g=GROUPS, t=PACK),
         )
 
+        early_gains = keep.tile([P, EARLY_GAINS * S], F32, name="early_gains", tag="table_words", align_bytes=64)
+        gains = [early_gains[:, t * S : (t + 1) * S] for t in range(EARLY_GAINS)] + late_gains
+
+        load_gain(0)
+        nc.sync.dma_start(place[:], offs2)
+        load_gain(1)
+        load_page(0)
+        w1_second = load_weight(w1, 1)
+        w3_second = load_weight(w3, 1)
+        load_gain(2)
+        load_page(1)
+        load_gain(3)
+        for i in range(2, LAST - 2):
+            load_page(i)
+        for g in range(GROUPS):
+            nc.sync.dma_start(
+                out=w4_codes[:, g * N : (g + 1) * N].bitcast(I32),
+                in_=w4_words[g].rearrange("p c i -> p (c i)").bitcast(I32),
+            )
+        load_page(LAST - 2)
+        load_scale_rows(w4_scale_tile, w4_scales)
+        load_page(LAST - 1)
+        with nc.allow_non_contiguous_dma(reason="one bias value for each partition"):
+            nc.sync.dma_start(out=bias[:], in_=b4.rearrange("(c p) -> p c", p=P))
+
         def b_tile(i):
             return rounded_row(TILES - 2 + i % 2)
 
-        w1_woven = round_weight(w1_first, woven_tile()[:], PACK // 2)
+        w1_woven = round_weight(w1_first, woven_tile()[:], 0)
         w3_woven = round_weight(w3_first, b_tile(0), PACK // 4)
         quantize_weight(w1_woven, 1, 0)
         quantize_weight(w3_woven, 3, 0)
@@ -213,19 +222,17 @@ def tile_list_clue_memory_triple_kernel(
                     nc.scalar.copy(out=b[:, half], in_=b_bank[:])
                     nc.scalar.copy(out=c[:, half], in_=c_bank[:])
             span = slice(BANK if i == 0 else 0, S)
+            bc = rounded_row(0).bitcast(F32) if i == 2 else bc_tile[:]
+            nc.gpsimd.tensor_tensor(out=bc[:, span], in0=b[:, span], in1=c[:, span], op=MULT)
             if i >= OFF_VECTOR:
-                nc.gpsimd.tensor_tensor(out=values[:], in0=values[:], in1=gain[:], op=MULT)
-            if i == LAST:
-                nc.gpsimd.tensor_tensor(out=b, in0=b, in1=c[:], op=MULT)
-            else:
-                bc = rounded_row(0 if i == 2 else PACK + i % 2).bitcast(F32)
-                nc.gpsimd.tensor_tensor(out=bc[:, span], in0=b[:, span], in1=c[:, span], op=MULT)
+                nc.gpsimd.tensor_tensor(out=bc, in0=bc, in1=gain, op=MULT)
+            if i < LAST:
                 nc.gpsimd.tensor_tensor(out=values[:, span], in0=bc[:, span], in1=values[:, span], op=MULT)
 
         def place_values(i):
             values = value_tiles[i % AHEAD]
             if i == LAST:
-                nc.vector.tensor_tensor(out=pages[i][:].indirect(place[:]), in0=values[:], in1=b_tile(i).bitcast(F32), op=MULT)
+                nc.vector.tensor_tensor(out=pages[i][:].indirect(place[:]), in0=values[:], in1=bc_tile[:], op=MULT)
             else:
                 width = BANK if i == 0 else S
                 for first in range(0, S, width):
@@ -292,23 +299,21 @@ def tile_list_clue_memory_triple_kernel(
         quantize_weight(round_weight(w1_second, c_tiles[0][:].bitcast(BF16), PACK), 1, 1)
         quantize_weight(round_weight(w3_second, b_tile(2), PACK), 3, 1)
         make_values(2)
+        make_values(3)
 
         for i in range(TILES):
             if i == LAST:
                 read_page(0, 0)
                 read_page(0, 1)
             place_values(i)
-            if i == AHEAD - 1:
+            if i == PACK:
                 load_page(LAST)
             if i + AHEAD < TILES:
                 make_values(i + AHEAD)
-            if i == PACK:
-                for chunk in range(CHUNKS // 2, CHUNKS):
-                    quantize_page(0, chunk, woven_tile(), nc.scalar.copy)
             if i < LAST:
                 round_page(i, slice(0, T2))
             if i == PACK - 1:
-                for chunk in range(CHUNKS // 2):
+                for chunk in range(CHUNKS):
                     quantize_page(0, chunk, woven_tile(), nc.scalar.copy)
             if i == LAST - 1:
                 store_page_codes(0, slice(0, T2))

@@ -1,6 +1,7 @@
 from contextlib import ExitStack
 
 import concourse.mybir as mybir
+from concourse.masks import make_identity
 
 K, H, N, T, S, T2 = 512, 1024, 512, 2048, 1024, 2048
 FLOPS = 2 * (3 * K * H * S + H * N * T2)
@@ -21,20 +22,22 @@ P = 128
 PACK = 4
 PASS = P * PACK
 BANK = 512
-BANKS = 8
 GROUPS = H // PASS
-TILES = GROUPS * PACK
+TILES = H // P
 LAST = TILES - 1
 HALVES = S // BANK
 CHUNKS = T2 // BANK
+BLOCKS = BANK // P
 N_TILES = N // P
 QUADRANT = 32
 QUADRANTS = P // QUADRANT
 SCALE_ROWS = 4
 PER_COLUMN = 16
-AHEAD = 4
-OFF_VECTOR = PACK
-EARLY_GAINS = 2
+PIECE = 2 * P
+PIECES = H // PIECE
+RING = 6
+ON_VECTOR = 2
+AHEAD = 3
 
 
 def tile_list_clue_memory_triple_kernel(
@@ -44,41 +47,43 @@ def tile_list_clue_memory_triple_kernel(
     nc = tc.nc
     with ExitStack() as ctx:
         keep = ctx.enter_context(tc.tile_pool(name="keep", bufs=1))
-        wide_pool = ctx.enter_context(tc.tile_pool(name="wide", bufs=4))
-        woven_pool = ctx.enter_context(tc.tile_pool(name="woven", bufs=CHUNKS))
-        rounded_pool = ctx.enter_context(tc.tile_pool(name="rounded", bufs=GROUPS))
+        wide_pool = ctx.enter_context(tc.tile_pool(name="wide", bufs=2 * PIECES))
         psum = ctx.enter_context(tc.psum_pool(name="psum", bufs=1))
-        banks = [psum.tile([P, BANK], F32, name="bank%d" % n) for n in range(BANKS)]
+        ring = [psum.tile([P, BANK], F32, name="ring%d" % n) for n in range(RING)]
+        word_banks = [psum.tile([P, BANK], F32, name="word_bank%d" % n) for n in range(2)]
+        ring_turns = []
 
-        def held(name, shape, dtype):
-            return keep.tile(shape, dtype, name=name, align_bytes=64)
+        def next_bank():
+            ring_turns.append(0)
+            return ring[(len(ring_turns) - 1) % RING]
+
+        def held(name, shape, dtype, tag=None):
+            return keep.tile(shape, dtype, name=name, tag=tag or name, align_bytes=64)
 
         pick = keep.tile([P, S // PER_COLUMN], U16, name="pick")
         place = keep.tile([P, S // PER_COLUMN], U16, name="place")
-        table_words = keep.tile([P, T], U32, name="table_words", tag="table_words", align_bytes=64)
+        table_words = held("table_words", [P, T], U32)
         table_scales = held("table_scales", [P, T], U8)
         picked_words = [held("picked_words%d" % h, [P, BANK], U32) for h in range(HALVES)]
-        c_tiles = [held("c%d" % n, [P, S], F32) for n in range(2)]
-        bc_tile = held("bc", [P, S], F32)
-        value_tiles = [held("values%d" % n, [P, S], F32) for n in range(AHEAD)]
         picked_scales = [held("picked_scales%d" % h, [P, BANK], U8) for h in range(HALVES)]
-        w2_loaded_codes = held("w2_loaded_codes", [P, 2 * H], U8)
-        w2_loaded_scales = held("w2_loaded_scales", [P, H], U8)
-        w2_dealt_codes = held("w2_dealt_codes", [P, 2 * H], U8)
-        w2_dealt_scales = held("w2_dealt_scales", [P, H], U8)
-        w_codes = {(w, g): held("w%d_codes%d" % (w, g), [P, PASS], U32) for w in (1, 3) for g in range(GROUPS)}
-        w_scales = {(w, g): held("w%d_scales%d" % (w, g), [P, PASS], U8) for w in (1, 3) for g in range(GROUPS)}
+        w2_codes = held("w2_codes", [P, 2 * H], U8)
+        w2_scale_tile = held("w2_scale_tile", [P, H], U8)
         w4_codes = held("w4_codes", [P, GROUPS * N], U32)
         w4_scale_tile = held("w4_scale_tile", [P, GROUPS * N], U8)
         bias = held("bias", [P, N_TILES], F32)
-        late_gains = [held("gain%d" % t, [P, S], F32)[:] for t in range(EARLY_GAINS, PACK)]
+        gain_whole = held("gain_whole", [P, S], F32)
+        identity = held("identity", [P, P], F32)
         pages = [held("page%d" % i, [P, T2], F32) for i in range(TILES)]
-        page_codes = [held("page_codes%d" % g, [P, T2], U32) for g in range(GROUPS)]
+        a_tiles = [held("a%d" % n, [P, S], F32) for n in range(2)]
+        b_tiles = [held("b%d" % n, [P, S], F32) for n in range(2)]
+        woven = [held("woven%d" % n, [P, 2 * PACK * BANK], BF16) for n in range(2)]
+        turned = [held("turned%d" % c, [P, BLOCKS * PASS], BF16) for c in range(CHUNKS)]
         page_scales = [held("page_scales%d" % g, [P, T2], U8) for g in range(GROUPS)]
-
-        page_rows = page0.rearrange("(g p t) m -> g t p m", p=P, t=PACK)
-        out_rows = out_1.rearrange("(g p t) m -> g t p m", p=P, t=PACK)
-        gain_rows = wgs.rearrange("(u t) j -> u t j", t=PACK)
+        w_scales = [held("w_scales%d" % n, [P, 2 * PIECE], U8) for n in range(PIECES)]
+        w_codes = {}
+        page_codes = {}
+        values = {}
+        value_tags = ["values_a", "late_codes2", "late_codes3", "values_b", "values_a", "values_c", "page_codes0", "values_a"]
 
         def scale_partitions(q):
             return slice(QUADRANT * q, QUADRANT * q + SCALE_ROWS)
@@ -91,38 +96,34 @@ def tile_list_clue_memory_triple_kernel(
                     in_=rows[:, SCALE_ROWS * q : SCALE_ROWS * (q + 1), :].bitcast(I32).rearrange("a r c -> r a c"),
                 )
 
-        def load_gain(t):
-            for q in (0, 2, 1, 3):
-                queue = nc.scalar if t < EARLY_GAINS and q >= QUADRANTS // 2 else nc.sync
-                queue.dma_start(out=gains[t][QUADRANT * q : QUADRANT * (q + 1), :], in_=gain_rows[:, t, :])
-
-        def load_weight(w, g):
-            loaded = wide_pool.tile([P, PACK, PASS], F32, name="wide")
-            nc.sync.dma_start(out=loaded[:], in_=w[:, g * PASS : (g + 1) * PASS].rearrange("(p j) c -> p j c", j=PACK))
+        def load_weight(w, piece):
+            loaded = wide_pool.tile([P, PACK, PIECE], F32, name="wide")
+            nc.sync.dma_start(
+                out=loaded[:], in_=w[:, piece * PIECE : (piece + 1) * PIECE].rearrange("(p j) c -> p j c", j=PACK)
+            )
             return loaded
 
         def load_page(i):
-            nc.sync.dma_start(out=pages[i][:], in_=page_rows[i // PACK, i % PACK])
+            nc.sync.dma_start(out=pages[i][:], in_=page0[i * P : (i + 1) * P, :])
 
-        rounded = [rounded_pool.tile([P, PACK * T2], BF16, name="rounded", align_bytes=64) for g in range(GROUPS)]
+        def woven_part(n):
+            width = PACK * BANK
+            return woven[n // 2][:, (n % 2) * width : (n % 2 + 1) * width]
 
-        def rounded_row(i):
-            return rounded[i // PACK][:, (i % PACK) * T2 : (i % PACK + 1) * T2]
+        def round_weight(engine_copy, loaded, piece, which, first, count):
+            base = which * PIECE * PACK
+            dst = woven_part(piece)[:, base + first * PACK : base + (first + count) * PACK]
+            engine_copy(
+                out=dst.rearrange("p (c i j) -> p c j i", i=4, j=PACK),
+                in_=loaded[:, :, first : first + count].rearrange("p j (c i) -> p c j i", i=4),
+            )
 
-        def woven_tile():
-            return woven_pool.tile([P, PACK * PASS], BF16, name="woven", align_bytes=64)
-
-        def round_weight(loaded, woven, scalar_share):
-            dst = woven.rearrange("p (t m j) -> p m j t", t=PACK, j=PACK)
-            src = loaded[:].rearrange("p j (m t) -> p m j t", t=PACK)
-            if scalar_share > 0:
-                nc.scalar.copy(out=dst[:, :, :, :scalar_share], in_=src[:, :, :, :scalar_share])
-            if scalar_share < PACK:
-                nc.vector.tensor_copy(out=dst[:, :, :, scalar_share:], in_=src[:, :, :, scalar_share:])
-            return woven
-
-        def quantize_weight(woven, w, g):
-            nc.vector.quantize_mx(out=w_codes[w, g][:].bitcast(FP8X4), scales=w_scales[w, g][:], in_=woven)
+        def quantize_weight(piece, first, count):
+            nc.vector.quantize_mx(
+                out=w_codes[piece][:, first : first + count].bitcast(FP8X4),
+                scales=w_scales[piece][:, first : first + count],
+                in_=woven_part(piece)[:, first * PACK : (first + count) * PACK],
+            )
 
         def entries(offsets, first, count):
             return offsets[:, first // PER_COLUMN : (first + count) // PER_COLUMN]
@@ -131,129 +132,127 @@ def tile_list_clue_memory_triple_kernel(
             nc.vector.tensor_copy(out=picked[h][:], in_=table[:].indirect(entries(pick, h * BANK, BANK)))
 
         nc.vector.memset(table_scales[:].bitcast(I32), 0)
-        nc.vector.memset(w2_loaded_scales[:].bitcast(I32), 0)
+        nc.vector.memset(w2_scale_tile[:].bitcast(I32), 0)
         nc.vector.memset(w4_scale_tile[:].bitcast(I32), 0)
+        make_identity(nc, identity[:])
 
         nc.sync.dma_start(pick[:], offs)
-        nc.sync.dma_start(out=w2_loaded_codes[:].bitcast(I32), in_=w2_words[0].bitcast(I32))
+        nc.sync.dma_start(out=w2_codes[:].bitcast(I32), in_=w2_words[0].bitcast(I32))
         load_scale_rows(table_scales, tab_scales)
         nc.sync.dma_start(out=table_words[:].bitcast(I32), in_=tab_words[0].rearrange("p t i -> p (t i)").bitcast(I32))
-        load_scale_rows(w2_loaded_scales, w2_scales)
-        w1_first = load_weight(w1, 0)
-        w3_first = load_weight(w3, 0)
-
-        pick_columns(picked_scales, table_scales, 0)
-        pick_columns(picked_scales, table_scales, 1)
-        nc.vector.tensor_copy(
-            out=w2_dealt_codes[:].bitcast(U16).rearrange("p (g t m) -> p g m t", g=GROUPS, t=PACK),
-            in_=w2_loaded_codes[:].bitcast(U16).rearrange("p (g m t) -> p g m t", g=GROUPS, t=PACK),
-        )
-        pick_columns(picked_words, table_words, 0)
-        pick_columns(picked_words, table_words, 1)
-        nc.vector.tensor_copy(
-            out=w2_dealt_scales[:].rearrange("p (g t m) -> p g m t", g=GROUPS, t=PACK),
-            in_=w2_loaded_scales[:].rearrange("p (g m t) -> p g m t", g=GROUPS, t=PACK),
-        )
-
-        early_gains = keep.tile([P, EARLY_GAINS * S], F32, name="early_gains", tag="table_words", align_bytes=64)
-        gains = [early_gains[:, t * S : (t + 1) * S] for t in range(EARLY_GAINS)] + late_gains
-
-        load_gain(0)
+        load_scale_rows(w2_scale_tile, w2_scales)
+        loaded = {(0, 0): load_weight(w1, 0), (1, 0): load_weight(w3, 0)}
+        nc.sync.dma_start(out=gain_whole[:], in_=wgs)
         nc.sync.dma_start(place[:], offs2)
-        load_gain(1)
         load_page(0)
-        w1_second = load_weight(w1, 1)
-        w3_second = load_weight(w3, 1)
-        load_gain(2)
-        load_page(1)
-        load_gain(3)
-        for i in range(2, LAST - 2):
+        for piece in range(1, PIECES):
+            loaded[0, piece] = load_weight(w1, piece)
+            loaded[1, piece] = load_weight(w3, piece)
+            if piece > 1:
+                load_page(piece - 1)
+        for i in range(PIECES - 1, LAST - 1):
             load_page(i)
         for g in range(GROUPS):
             nc.sync.dma_start(
                 out=w4_codes[:, g * N : (g + 1) * N].bitcast(I32),
                 in_=w4_words[g].rearrange("p c i -> p (c i)").bitcast(I32),
             )
-        load_page(LAST - 2)
-        load_scale_rows(w4_scale_tile, w4_scales)
         load_page(LAST - 1)
+        load_scale_rows(w4_scale_tile, w4_scales)
+        load_page(LAST)
         with nc.allow_non_contiguous_dma(reason="one bias value for each partition"):
             nc.sync.dma_start(out=bias[:], in_=b4.rearrange("(c p) -> p c", p=P))
 
-        def b_tile(i):
-            return rounded_row(TILES - 2 + i % 2)
+        pick_columns(picked_scales, table_scales, 0)
+        pick_columns(picked_scales, table_scales, 1)
+        pick_columns(picked_words, table_words, 0)
+        pick_columns(picked_words, table_words, 1)
 
-        w1_woven = round_weight(w1_first, woven_tile()[:], 0)
-        w3_woven = round_weight(w3_first, b_tile(0), PACK // 4)
-        quantize_weight(w1_woven, 1, 0)
-        quantize_weight(w3_woven, 3, 0)
+        w_codes[0] = held("w_codes0", [P, 2 * PIECE], U32)
+        w_codes[1] = held("w_codes1", [P, 2 * PIECE], U32)
+        for which in range(2):
+            round_weight(nc.scalar.copy, loaded[which, 0], 0, which, 0, P)
+            round_weight(nc.vector.tensor_copy, loaded[which, 0], 0, which, P, P)
+            quantize_weight(0, which * PIECE, PIECE)
 
-        def product(bank, codes, scales, h):
+        def product(bank, i, h, name):
+            piece, cols = i // 2, slice((i % 2) * P, (i % 2 + 1) * P)
+            if name == "b":
+                codes, scales = w2_codes[:, 2 * i * P : 2 * (i + 1) * P].bitcast(FP4X4), w2_scale_tile[:, i * P : (i + 1) * P]
+            else:
+                if name == "c":
+                    cols = slice(PIECE + cols.start, PIECE + cols.stop)
+                codes, scales = w_codes[piece][:, cols].bitcast(FP8X4), w_scales[piece][:, cols]
             nc.tensor.matmul_mx(
                 out=bank[:], lhsT=codes, lhsT_scale=scales,
                 rhs=picked_words[h][:].bitcast(FP8X4), rhs_scale=picked_scales[h][:], start=True, stop=True,
             )
             return bank
 
-        def products(i, h):
-            g, t = divmod(i, PACK)
-            cols = slice(t * P, (t + 1) * P)
-            a_bank, b_bank, c_bank = banks[2 * HALVES + HALVES * (i % 2) + h], banks[h], banks[HALVES + h]
-            product(a_bank, w_codes[1, g][:, cols].bitcast(FP8X4), w_scales[1, g][:, cols], h)
-            product(
-                b_bank, w2_dealt_codes[:, 2 * i * P : 2 * (i + 1) * P].bitcast(FP4X4), w2_dealt_scales[:, i * P : (i + 1) * P], h
-            )
-            product(c_bank, w_codes[3, g][:, cols].bitcast(FP8X4), w_scales[3, g][:, cols], h)
-            return a_bank, b_bank, c_bank
+        def half(h):
+            return slice(h * BANK, (h + 1) * BANK)
+
+        def first_values():
+            values[0] = held("values0", [P, S], F32, value_tags[0])
+            for name in "abc":
+                for h in range(HALVES):
+                    bank = product(next_bank(), 0, h, name)
+                    other = gain_whole if name == "a" else values[0]
+                    nc.vector.tensor_tensor(out=values[0][:, half(h)], in0=bank[:], in1=other[:, half(h)], op=MULT)
 
         def make_values(i):
-            b, c, values, gain = b_tile(i).bitcast(F32), c_tiles[i % 2], value_tiles[i % AHEAD], gains[i % PACK]
-            for h in range(HALVES):
-                half = slice(h * BANK, (h + 1) * BANK)
-                a_bank, b_bank, c_bank = products(i, h)
-                if i >= OFF_VECTOR:
-                    nc.scalar.copy(out=values[:, half], in_=a_bank[:])
-                else:
-                    nc.vector.tensor_tensor(out=values[:, half], in0=a_bank[:], in1=gain[:, half], op=MULT)
-                if i == 0 and h == 0:
-                    nc.vector.tensor_tensor(out=b[:, half], in0=b_bank[:], in1=values[:, half], op=MULT)
-                    nc.vector.tensor_tensor(out=values[:, half], in0=c_bank[:], in1=b[:, half], op=MULT)
-                else:
-                    nc.scalar.copy(out=b[:, half], in_=b_bank[:])
-                    nc.scalar.copy(out=c[:, half], in_=c_bank[:])
-            span = slice(BANK if i == 0 else 0, S)
-            bc = rounded_row(0).bitcast(F32) if i == 2 else bc_tile[:]
-            nc.gpsimd.tensor_tensor(out=bc[:, span], in0=b[:, span], in1=c[:, span], op=MULT)
-            if i >= OFF_VECTOR:
-                nc.gpsimd.tensor_tensor(out=bc, in0=bc, in1=gain, op=MULT)
+            values[i] = held("values%d" % i, [P, S], F32, value_tags[i])
+            a, b = a_tiles[i % 2], b_tiles[i % 2]
+            for name, target in (("c", values[i]), ("a", a), ("b", b)):
+                for h in range(HALVES):
+                    bank = product(word_banks[h] if i <= ON_VECTOR and name == "c" else next_bank(), i, h, name)
+                    if i == ON_VECTOR and name == "c":
+                        nc.vector.tensor_tensor(out=target[:, half(h)], in0=bank[:], in1=gain_whole[:, half(h)], op=MULT)
+                    else:
+                        nc.scalar.copy(out=target[:, half(h)], in_=bank[:])
+            if i != ON_VECTOR:
+                nc.gpsimd.tensor_tensor(out=values[i][:], in0=values[i][:], in1=gain_whole[:], op=MULT)
+            nc.gpsimd.tensor_tensor(out=values[i][:], in0=values[i][:], in1=a[:], op=MULT)
             if i < LAST:
-                nc.gpsimd.tensor_tensor(out=values[:, span], in0=bc[:, span], in1=values[:, span], op=MULT)
+                nc.gpsimd.tensor_tensor(out=values[i][:], in0=values[i][:], in1=b[:], op=MULT)
+
+        def round_piece(piece):
+            for which in range(2):
+                round_weight(nc.scalar.copy, loaded[which, piece], piece, which, 0, PIECE)
 
         def place_values(i):
-            values = value_tiles[i % AHEAD]
             if i == LAST:
-                nc.vector.tensor_tensor(out=pages[i][:].indirect(place[:]), in0=values[:], in1=bc_tile[:], op=MULT)
+                nc.vector.tensor_tensor(out=pages[i][:].indirect(place[:]), in0=values[i][:], in1=b_tiles[i % 2][:], op=MULT)
             else:
-                width = BANK if i == 0 else S
-                for first in range(0, S, width):
-                    nc.vector.tensor_copy(
-                        out=pages[i][:].indirect(entries(place, first, width)), in_=values[:, first : first + width]
-                    )
-            nc.sync.dma_start(out=out_rows[i // PACK, i % PACK], in_=pages[i][:])
+                nc.vector.tensor_copy(out=pages[i][:].indirect(place[:]), in_=values[i][:])
+            nc.sync.dma_start(out=out_1[i * P : (i + 1) * P, :], in_=pages[i][:])
 
         def chunk_columns(chunk):
             return slice(chunk * BANK, (chunk + 1) * BANK)
 
-        def round_page(i, cols):
-            nc.scalar.copy(out=rounded_row(i)[:, cols], in_=pages[i][:, cols])
-
-        def quantize_page(g, chunk, woven, weave):
-            cols = chunk_columns(chunk)
-            rows = rounded[g][:].rearrange("p (t m) -> p t m", t=PACK)[:, :, cols]
-            weave(
-                out=woven[:].rearrange("p (c i t) -> p c t i", i=4, t=PACK), in_=rows.rearrange("p t (c i) -> p c t i", i=4)
+        def turn_page(i, chunk, bank):
+            for block in range(BLOCKS):
+                first = chunk * BANK + block * P
+                nc.tensor.transpose(bank[:, block * P : (block + 1) * P], pages[i][:, first : first + P], identity[:])
+            nc.scalar.copy(
+                out=turned[chunk][:].rearrange("p (b u q w e) -> p b u q w e", b=BLOCKS, u=2, q=QUADRANTS, e=2)[:, :, :, i % PACK],
+                in_=bank[:].rearrange("p (b w u e) -> p b u w e", b=BLOCKS, u=2, e=2),
             )
-            nc.vector.quantize_mx(out=page_codes[g][:, cols].bitcast(FP8X4), scales=page_scales[g][:, cols], in_=woven[:])
+
+        def turn_back(chunk, copies):
+            words = turned[chunk][:].bitcast(F32)
+            target = woven_part(chunk).bitcast(F32)
+            for n in range(2):
+                for m in range(4):
+                    first = (4 * n + m) * P
+                    nc.tensor.transpose(word_banks[n][:, m * P : (m + 1) * P], words[:, first : first + P], identity[:])
+                copies[n](
+                    out=target[:, n * BANK : (n + 1) * BANK].rearrange("p (b m u) -> p b m u", b=2, u=2),
+                    in_=word_banks[n][:].rearrange("p (b u m) -> p b m u", b=2, u=2),
+                )
+
+        def quantize_page(g, cols, source):
+            nc.vector.quantize_mx(out=page_codes[g][:, cols].bitcast(FP8X4), scales=page_scales[g][:, cols], in_=source)
 
         def store_page_scales(g):
             for q in range(QUADRANTS):
@@ -267,66 +266,78 @@ def tile_list_clue_memory_triple_kernel(
                 out=out_2[g].rearrange("p m t -> p (m t)").bitcast(I32)[:, cols], in_=page_codes[g][:, cols].bitcast(I32)
             )
 
-        def sum_bank(chunk, n):
-            return banks[(chunk % 2) * N_TILES + n]
-
         def read_page(g, chunk):
             cols = chunk_columns(chunk)
             for n in range(N_TILES):
                 w4_cols = slice(g * N + n * P, g * N + (n + 1) * P)
                 nc.tensor.matmul_mx(
-                    out=sum_bank(chunk, n)[:],
+                    out=sum_banks[n][:],
                     lhsT=w4_codes[:, w4_cols].bitcast(FP8X4), lhsT_scale=w4_scale_tile[:, w4_cols],
                     rhs=page_codes[g][:, cols].bitcast(FP8X4), rhs_scale=page_scales[g][:, cols],
                     start=(g == 0), stop=(g == GROUPS - 1),
                 )
 
         def store_features(chunk):
-            features = wide_pool.tile([P, N_TILES, BANK], F32, name="wide")
-            for n in range(N_TILES):
-                if n == N_TILES - 1:
-                    nc.vector.tensor_scalar(
-                        out=features[:, n, :], in0=sum_bank(chunk, n)[:], scalar1=bias[:, n : n + 1], scalar2=None, op0=ADD
-                    )
-                else:
-                    nc.scalar.activation(
-                        out=features[:, n, :], in_=sum_bank(chunk, n)[:], func=IDENTITY, bias=bias[:, n : n + 1]
-                    )
-                nc.sync.dma_start(out=out_0[n * P : (n + 1) * P, chunk_columns(chunk)], in_=features[:, n, :])
+            for pair in range(N_TILES // 2):
+                features = wide_pool.tile([P, 2, BANK], F32, name="wide")
+                for m in range(2):
+                    n = 2 * pair + m
+                    if m == 1:
+                        nc.vector.tensor_scalar(
+                            out=features[:, m, :], in0=sum_banks[n][:], scalar1=bias[:, n : n + 1], scalar2=None, op0=ADD
+                        )
+                    else:
+                        nc.scalar.activation(
+                            out=features[:, m, :], in_=sum_banks[n][:], func=IDENTITY, bias=bias[:, n : n + 1]
+                        )
+                    nc.sync.dma_start(out=out_0[n * P : (n + 1) * P, chunk_columns(chunk)], in_=features[:, m, :])
 
-        make_values(0)
+        first_values()
         make_values(1)
-        quantize_weight(round_weight(w1_second, c_tiles[0][:].bitcast(BF16), PACK), 1, 1)
-        quantize_weight(round_weight(w3_second, b_tile(2), PACK), 3, 1)
+        round_piece(1)
+        quantize_weight(1, 0, 2 * PIECE)
         make_values(2)
-        make_values(3)
+        round_piece(2)
 
-        for i in range(TILES):
-            if i == LAST:
-                read_page(0, 0)
-                read_page(0, 1)
+        for i in range(LAST):
             place_values(i)
-            if i == PACK:
-                load_page(LAST)
+            if i in (1, 2):
+                w_codes[i + 1] = held("w_codes%d" % (i + 1), [P, 2 * PIECE], U32, value_tags[i])
+                quantize_weight(i + 1, 0, 2 * PIECE)
             if i + AHEAD < TILES:
                 make_values(i + AHEAD)
-            if i < LAST:
-                round_page(i, slice(0, T2))
-            if i == PACK - 1:
+            if i == 0:
+                round_piece(3)
+            if i == PACK:
                 for chunk in range(CHUNKS):
-                    quantize_page(0, chunk, woven_tile(), nc.scalar.copy)
+                    turn_back(chunk, [nc.scalar.copy, nc.scalar.copy])
             if i == LAST - 1:
+                page_codes[0] = held("page_codes0", [P, T2], U32, value_tags[i])
+                for n in range(2):
+                    quantize_page(0, slice(n * 2 * BANK, (n + 1) * 2 * BANK), woven[n][:])
                 store_page_codes(0, slice(0, T2))
                 store_page_scales(0)
+            for chunk in range(CHUNKS):
+                turn_page(i, chunk, next_bank())
 
-        last_woven = woven_tile()
+        sum_banks = [next_bank() for n in range(N_TILES)]
+        turn_banks = [next_bank() for n in range(2)]
+        page_codes[1] = held("page_codes1", [P, T2], U32)
+        read_page(0, 0)
+        place_values(LAST)
+        turn_page(LAST, 0, turn_banks[0])
+        turn_back(0, [nc.scalar.copy, nc.vector.tensor_copy])
+        turn_page(LAST, 1, turn_banks[1])
         for chunk in range(CHUNKS):
-            round_page(LAST, chunk_columns(chunk))
-            quantize_page(1, chunk, last_woven, nc.vector.tensor_copy)
+            quantize_page(1, chunk_columns(chunk), woven_part(chunk))
+            if chunk + 1 < CHUNKS:
+                turn_back(chunk + 1, [nc.scalar.copy, nc.vector.tensor_copy])
             store_page_codes(1, chunk_columns(chunk))
             if chunk == CHUNKS - 1:
                 store_page_scales(1)
             read_page(1, chunk)
-            store_features(chunk)
             if chunk + 2 < CHUNKS:
-                read_page(0, chunk + 2)
+                turn_page(LAST, chunk + 2, turn_banks[chunk % 2])
+            store_features(chunk)
+            if chunk + 1 < CHUNKS:
+                read_page(0, chunk + 1)

@@ -34,7 +34,7 @@ QUADRANTS = P // QUADRANT
 SCALE_ROWS = 4
 PER_COLUMN = 16
 PIECE = 2 * P
-PIECES = H // PIECE
+PIECES = PASS // PIECE
 RING = 6
 ON_VECTOR = 2
 AHEAD = 3
@@ -47,7 +47,7 @@ def tile_list_clue_memory_triple_kernel(
     nc = tc.nc
     with ExitStack() as ctx:
         keep = ctx.enter_context(tc.tile_pool(name="keep", bufs=1))
-        wide_pool = ctx.enter_context(tc.tile_pool(name="wide", bufs=2 * PIECES))
+        wide_pool = ctx.enter_context(tc.tile_pool(name="wide", bufs=1))
         psum = ctx.enter_context(tc.psum_pool(name="psum", bufs=1))
         ring = [psum.tile([P, BANK], F32, name="ring%d" % n) for n in range(RING)]
         word_banks = [psum.tile([P, BANK], F32, name="word_bank%d" % n) for n in range(2)]
@@ -72,6 +72,9 @@ def tile_list_clue_memory_triple_kernel(
         w4_scale_tile = held("w4_scale_tile", [P, GROUPS * N], U8)
         bias = held("bias", [P, N_TILES], F32)
         gain_whole = held("gain_whole", [P, S], F32)
+        dealt_gains = [held("dealt_gain%d" % t, [P, S], F32) for t in range(PACK)]
+        w2_dealt_codes = held("w2_dealt_codes", [P, 2 * PASS], U8)
+        w2_dealt_scales = held("w2_dealt_scales", [P, PASS], U8)
         identity = held("identity", [P, P], F32)
         pages = [held("page%d" % i, [P, T2], F32) for i in range(TILES)]
         a_tiles = [held("a%d" % n, [P, S], F32) for n in range(2)]
@@ -79,11 +82,14 @@ def tile_list_clue_memory_triple_kernel(
         woven = [held("woven%d" % n, [P, 2 * PACK * BANK], BF16) for n in range(2)]
         turned = [held("turned%d" % c, [P, BLOCKS * PASS], BF16) for c in range(CHUNKS)]
         page_scales = [held("page_scales%d" % g, [P, T2], U8) for g in range(GROUPS)]
-        w_scales = [held("w_scales%d" % n, [P, 2 * PIECE], U8) for n in range(PIECES)]
+        w_scales = [held("w_scales%d" % n, [P, 2 * width], U8) for n, width in enumerate((PIECE, PIECE, PASS))]
         w_codes = {}
         page_codes = {}
         values = {}
-        value_tags = ["values_a", "late_codes2", "late_codes3", "values_b", "values_a", "values_c", "page_codes0", "values_a"]
+        value_tags = ["values_a", "dealt_codes", "values_b", "values_c", "values_a", "values_b", "page_codes0", "values_c"]
+        dealt_in = page0[PASS:, :].rearrange("(p t) m -> t p m", t=PACK)
+        dealt_out = out_1[PASS:, :].rearrange("(p t) m -> t p m", t=PACK)
+        gain_rows = wgs.rearrange("(u t) j -> u t j", t=PACK)
 
         def scale_partitions(q):
             return slice(QUADRANT * q, QUADRANT * q + SCALE_ROWS)
@@ -96,15 +102,23 @@ def tile_list_clue_memory_triple_kernel(
                     in_=rows[:, SCALE_ROWS * q : SCALE_ROWS * (q + 1), :].bitcast(I32).rearrange("a r c -> r a c"),
                 )
 
-        def load_weight(w, piece):
-            loaded = wide_pool.tile([P, PACK, PIECE], F32, name="wide")
+        def load_weight(which, piece):
+            first, width = piece * PIECE, PIECE if piece < PIECES else PASS
+            loaded = wide_pool.tile(
+                [P, PACK, width], F32, name="w_loaded%d_%d" % (which, piece), offset=4 * PACK * (2 * first + which * width)
+            )
             nc.sync.dma_start(
-                out=loaded[:], in_=w[:, piece * PIECE : (piece + 1) * PIECE].rearrange("(p j) c -> p j c", j=PACK)
+                out=loaded[:], in_=(w1, w3)[which][:, first : first + width].rearrange("(p j) c -> p j c", j=PACK)
             )
             return loaded
 
         def load_page(i):
-            nc.sync.dma_start(out=pages[i][:], in_=page0[i * P : (i + 1) * P, :])
+            rows = page0[i * P : (i + 1) * P, :] if i < PACK else dealt_in[i - PACK]
+            nc.sync.dma_start(out=pages[i][:], in_=rows)
+
+        def load_dealt_gain(t):
+            for q in (0, 2, 1, 3):
+                nc.sync.dma_start(out=dealt_gains[t][QUADRANT * q : QUADRANT * (q + 1), :], in_=gain_rows[:, t, :])
 
         def woven_part(n):
             width = PACK * BANK
@@ -141,17 +155,17 @@ def tile_list_clue_memory_triple_kernel(
         load_scale_rows(table_scales, tab_scales)
         nc.sync.dma_start(out=table_words[:].bitcast(I32), in_=tab_words[0].rearrange("p t i -> p (t i)").bitcast(I32))
         load_scale_rows(w2_scale_tile, w2_scales)
-        loaded = {(0, 0): load_weight(w1, 0), (1, 0): load_weight(w3, 0)}
+        loaded = {(0, 0): load_weight(0, 0), (1, 0): load_weight(1, 0)}
         nc.sync.dma_start(out=gain_whole[:], in_=wgs)
         nc.sync.dma_start(place[:], offs2)
         load_page(0)
-        for piece in range(1, PIECES):
-            loaded[0, piece] = load_weight(w1, piece)
-            loaded[1, piece] = load_weight(w3, piece)
-            if piece > 1:
-                load_page(piece - 1)
-        for i in range(PIECES - 1, LAST - 1):
-            load_page(i)
+        for piece in range(1, PIECES + 1):
+            loaded[0, piece] = load_weight(0, piece)
+            loaded[1, piece] = load_weight(1, piece)
+        load_page(1)
+        for t in range(PACK):
+            load_page(2 + t)
+            load_dealt_gain(t)
         for g in range(GROUPS):
             nc.sync.dma_start(
                 out=w4_codes[:, g * N : (g + 1) * N].bitcast(I32),
@@ -176,13 +190,15 @@ def tile_list_clue_memory_triple_kernel(
             quantize_weight(0, which * PIECE, PIECE)
 
         def product(bank, i, h, name):
-            piece, cols = i // 2, slice((i % 2) * P, (i % 2 + 1) * P)
             if name == "b":
-                codes, scales = w2_codes[:, 2 * i * P : 2 * (i + 1) * P].bitcast(FP4X4), w2_scale_tile[:, i * P : (i + 1) * P]
+                codes, scales = (w2_codes, w2_scale_tile) if i < PACK else (w2_dealt_codes, w2_dealt_scales)
+                first = (i % PACK) * P
+                codes, scales = codes[:, 2 * first : 2 * (first + P)].bitcast(FP4X4), scales[:, first : first + P]
             else:
+                piece, first, width = (i // 2, (i % 2) * P, PIECE) if i < PACK else (PIECES, (i - PACK) * P, PASS)
                 if name == "c":
-                    cols = slice(PIECE + cols.start, PIECE + cols.stop)
-                codes, scales = w_codes[piece][:, cols].bitcast(FP8X4), w_scales[piece][:, cols]
+                    first = first + width
+                codes, scales = w_codes[piece][:, first : first + P].bitcast(FP8X4), w_scales[piece][:, first : first + P]
             nc.tensor.matmul_mx(
                 out=bank[:], lhsT=codes, lhsT_scale=scales,
                 rhs=picked_words[h][:].bitcast(FP8X4), rhs_scale=picked_scales[h][:], start=True, stop=True,
@@ -211,7 +227,8 @@ def tile_list_clue_memory_triple_kernel(
                     else:
                         nc.scalar.copy(out=target[:, half(h)], in_=bank[:])
             if i != ON_VECTOR:
-                nc.gpsimd.tensor_tensor(out=values[i][:], in0=values[i][:], in1=gain_whole[:], op=MULT)
+                gain = gain_whole if i < PACK else dealt_gains[i - PACK]
+                nc.gpsimd.tensor_tensor(out=values[i][:], in0=values[i][:], in1=gain[:], op=MULT)
             nc.gpsimd.tensor_tensor(out=values[i][:], in0=values[i][:], in1=a[:], op=MULT)
             if i < LAST:
                 nc.gpsimd.tensor_tensor(out=values[i][:], in0=values[i][:], in1=b[:], op=MULT)
@@ -220,12 +237,30 @@ def tile_list_clue_memory_triple_kernel(
             for which in range(2):
                 round_weight(nc.scalar.copy, loaded[which, piece], piece, which, 0, PIECE)
 
+        def round_dealt(which):
+            width = PACK * PASS
+            nc.scalar.copy(
+                out=woven[1][:, which * width : (which + 1) * width].rearrange("p (t m j) -> p m j t", t=PACK, j=PACK),
+                in_=loaded[which, PIECES][:].rearrange("p j (m t) -> p m j t", t=PACK),
+            )
+
+        def deal_w2():
+            nc.vector.tensor_copy(
+                out=w2_dealt_codes[:].bitcast(U16).rearrange("p (t m) -> p m t", t=PACK),
+                in_=w2_codes[:, 2 * PASS :].bitcast(U16).rearrange("p (m t) -> p m t", t=PACK),
+            )
+            nc.vector.tensor_copy(
+                out=w2_dealt_scales[:].rearrange("p (t m) -> p m t", t=PACK),
+                in_=w2_scale_tile[:, PASS:].rearrange("p (m t) -> p m t", t=PACK),
+            )
+
         def place_values(i):
             if i == LAST:
                 nc.vector.tensor_tensor(out=pages[i][:].indirect(place[:]), in0=values[i][:], in1=b_tiles[i % 2][:], op=MULT)
             else:
                 nc.vector.tensor_copy(out=pages[i][:].indirect(place[:]), in_=values[i][:])
-            nc.sync.dma_start(out=out_1[i * P : (i + 1) * P, :], in_=pages[i][:])
+            rows = out_1[i * P : (i + 1) * P, :] if i < PACK else dealt_out[i - PACK]
+            nc.sync.dma_start(out=rows, in_=pages[i][:])
 
         def chunk_columns(chunk):
             return slice(chunk * BANK, (chunk + 1) * BANK)
@@ -251,6 +286,18 @@ def tile_list_clue_memory_triple_kernel(
                     in_=word_banks[n][:].rearrange("p (b u m) -> p b m u", b=2, u=2),
                 )
 
+        def round_page(i, chunk):
+            u, e = divmod(i - PACK, 2)
+            nc.scalar.copy(
+                out=turned[chunk][:].rearrange("p (u m e) -> p u m e", u=2, e=2)[:, u, :, e], in_=pages[i][:, chunk_columns(chunk)]
+            )
+
+        def weave(chunk):
+            nc.vector.tensor_copy(
+                out=woven_part(chunk).bitcast(F32).rearrange("p (c i u) -> p c u i", i=4, u=2),
+                in_=turned[chunk][:].bitcast(F32).rearrange("p (u c i) -> p c u i", i=4, u=2),
+            )
+
         def quantize_page(g, cols, source):
             nc.vector.quantize_mx(out=page_codes[g][:, cols].bitcast(FP8X4), scales=page_scales[g][:, cols], in_=source)
 
@@ -266,48 +313,57 @@ def tile_list_clue_memory_triple_kernel(
                 out=out_2[g].rearrange("p m t -> p (m t)").bitcast(I32)[:, cols], in_=page_codes[g][:, cols].bitcast(I32)
             )
 
+        def sum_bank(chunk, n):
+            return sum_banks[(chunk % 2) * N_TILES + n]
+
         def read_page(g, chunk):
             cols = chunk_columns(chunk)
             for n in range(N_TILES):
                 w4_cols = slice(g * N + n * P, g * N + (n + 1) * P)
                 nc.tensor.matmul_mx(
-                    out=sum_banks[n][:],
+                    out=sum_bank(chunk, n)[:],
                     lhsT=w4_codes[:, w4_cols].bitcast(FP8X4), lhsT_scale=w4_scale_tile[:, w4_cols],
                     rhs=page_codes[g][:, cols].bitcast(FP8X4), rhs_scale=page_scales[g][:, cols],
                     start=(g == 0), stop=(g == GROUPS - 1),
                 )
 
         def store_features(chunk):
-            for pair in range(N_TILES // 2):
-                features = wide_pool.tile([P, 2, BANK], F32, name="wide")
-                for m in range(2):
-                    n = 2 * pair + m
-                    if m == 1:
-                        nc.vector.tensor_scalar(
-                            out=features[:, m, :], in0=sum_banks[n][:], scalar1=bias[:, n : n + 1], scalar2=None, op0=ADD
-                        )
-                    else:
-                        nc.scalar.activation(
-                            out=features[:, m, :], in_=sum_banks[n][:], func=IDENTITY, bias=bias[:, n : n + 1]
-                        )
-                    nc.sync.dma_start(out=out_0[n * P : (n + 1) * P, chunk_columns(chunk)], in_=features[:, m, :])
+            features = wide_pool.tile([P, N_TILES, BANK], F32, name="features%d" % chunk, offset=4 * N_TILES * BANK * chunk)
+            for n in range(N_TILES):
+                if n == N_TILES - 1:
+                    nc.vector.tensor_scalar(
+                        out=features[:, n, :], in0=sum_bank(chunk, n)[:], scalar1=bias[:, n : n + 1], scalar2=None, op0=ADD
+                    )
+                else:
+                    nc.scalar.activation(
+                        out=features[:, n, :], in_=sum_bank(chunk, n)[:], func=IDENTITY, bias=bias[:, n : n + 1]
+                    )
+                nc.sync.dma_start(out=out_0[n * P : (n + 1) * P, chunk_columns(chunk)], in_=features[:, n, :])
+
+        def turn_tile(i):
+            for chunk in range(CHUNKS):
+                turn_page(i, chunk, next_bank())
 
         first_values()
+        deal_w2()
         make_values(1)
         round_piece(1)
         quantize_weight(1, 0, 2 * PIECE)
         make_values(2)
-        round_piece(2)
+        round_dealt(0)
+        round_dealt(1)
 
         for i in range(LAST):
             place_values(i)
-            if i in (1, 2):
-                w_codes[i + 1] = held("w_codes%d" % (i + 1), [P, 2 * PIECE], U32, value_tags[i])
-                quantize_weight(i + 1, 0, 2 * PIECE)
+            if i == 1:
+                w_codes[PIECES] = held("w_codes_dealt", [P, 2 * PASS], U32, value_tags[i])
+                nc.vector.quantize_mx(out=w_codes[PIECES][:].bitcast(FP8X4), scales=w_scales[PIECES][:], in_=woven[1][:])
             if i + AHEAD < TILES:
                 make_values(i + AHEAD)
-            if i == 0:
-                round_piece(3)
+            if i == 1:
+                turn_tile(0)
+            if 1 <= i < PACK:
+                turn_tile(i)
             if i == PACK:
                 for chunk in range(CHUNKS):
                     turn_back(chunk, [nc.scalar.copy, nc.scalar.copy])
@@ -317,27 +373,25 @@ def tile_list_clue_memory_triple_kernel(
                     quantize_page(0, slice(n * 2 * BANK, (n + 1) * 2 * BANK), woven[n][:])
                 store_page_codes(0, slice(0, T2))
                 store_page_scales(0)
-            for chunk in range(CHUNKS):
-                turn_page(i, chunk, next_bank())
+            if i >= PACK:
+                for chunk in range(CHUNKS):
+                    round_page(i, chunk)
 
-        sum_banks = [next_bank() for n in range(N_TILES)]
-        turn_banks = [next_bank() for n in range(2)]
+        sum_banks = ring + word_banks
         page_codes[1] = held("page_codes1", [P, T2], U32)
         read_page(0, 0)
+        read_page(0, 1)
         place_values(LAST)
-        turn_page(LAST, 0, turn_banks[0])
-        turn_back(0, [nc.scalar.copy, nc.vector.tensor_copy])
-        turn_page(LAST, 1, turn_banks[1])
         for chunk in range(CHUNKS):
+            round_page(LAST, chunk)
+        for chunk in range(CHUNKS):
+            weave(chunk)
             quantize_page(1, chunk_columns(chunk), woven_part(chunk))
-            if chunk + 1 < CHUNKS:
-                turn_back(chunk + 1, [nc.scalar.copy, nc.vector.tensor_copy])
-            store_page_codes(1, chunk_columns(chunk))
+            if chunk % 2 == 1:
+                store_page_codes(1, slice((chunk - 1) * BANK, (chunk + 1) * BANK))
             if chunk == CHUNKS - 1:
                 store_page_scales(1)
             read_page(1, chunk)
-            if chunk + 2 < CHUNKS:
-                turn_page(LAST, chunk + 2, turn_banks[chunk % 2])
             store_features(chunk)
-            if chunk + 1 < CHUNKS:
-                read_page(0, chunk + 1)
+            if chunk + 2 < CHUNKS:
+                read_page(0, chunk + 2)

@@ -33,10 +33,10 @@ QUADRANT = 32
 QUADRANTS = P // QUADRANT
 SCALE_ROWS = 4
 PER_COLUMN = 16
+WIDTHS = (256, 512, 512, 512, 256)
+OPENED = 2
 PIECE = 2 * P
 PIECES = PASS // PIECE
-RING = 6
-ON_VECTOR = 2
 AHEAD = 3
 
 
@@ -48,14 +48,13 @@ def tile_list_clue_memory_triple_kernel(
     with ExitStack() as ctx:
         keep = ctx.enter_context(tc.tile_pool(name="keep", bufs=1))
         wide_pool = ctx.enter_context(tc.tile_pool(name="wide", bufs=1))
+        weave_pool = ctx.enter_context(tc.tile_pool(name="weave", bufs=1))
         psum = ctx.enter_context(tc.psum_pool(name="psum", bufs=1))
-        ring = [psum.tile([P, BANK], F32, name="ring%d" % n) for n in range(RING)]
-        word_banks = [psum.tile([P, BANK], F32, name="word_bank%d" % n) for n in range(2)]
-        ring_turns = []
+        banks = {name: [psum.tile([P, BANK], F32, name="bank_%s%d" % (name, h)) for h in range(2)] for name in "abcw"}
+        turns = ctx.enter_context(tc.tile_pool(name="turns", bufs=1))
 
-        def next_bank():
-            ring_turns.append(0)
-            return ring[(len(ring_turns) - 1) % RING]
+        def placed(name, shape, dtype, kib):
+            return turns.tile(shape, dtype, name=name, align_bytes=64, offset=1024 * kib)
 
         def held(name, shape, dtype, tag=None):
             return keep.tile(shape, dtype, name=name, tag=tag or name, align_bytes=64)
@@ -77,29 +76,25 @@ def tile_list_clue_memory_triple_kernel(
         w2_dealt_scales = held("w2_dealt_scales", [P, PASS], U8)
         identity = held("identity", [P, P], F32)
         pages = [held("page%d" % i, [P, T2], F32) for i in range(TILES)]
-        a_tiles = [held("a%d" % n, [P, S], F32) for n in range(2)]
-        b_tiles = [held("b%d" % n, [P, S], F32) for n in range(2)]
-        woven = [held("woven%d" % n, [P, 2 * PACK * BANK], BF16) for n in range(2)]
-        turned = [held("turned%d" % c, [P, BLOCKS * PASS], BF16) for c in range(CHUNKS)]
+        a_tile = held("a", [P, S], F32)
+        turn_pool = ctx.enter_context(tc.tile_pool(name="turn", bufs=1))
+        turned = [
+            turn_pool.tile([P, PACK * BANK], BF16, name="turned%d" % c, align_bytes=64, offset=2 * PACK * BANK * c)
+            for c in range(CHUNKS)
+        ]
+        spans = [slice(sum(WIDTHS[:n]), sum(WIDTHS[: n + 1])) for n in range(len(WIDTHS))]
         page_scales = [held("page_scales%d" % g, [P, T2], U8) for g in range(GROUPS)]
-        w_scales = [held("w_scales%d" % n, [P, 2 * width], U8) for n, width in enumerate((PIECE, PIECE, PASS))]
-        w_codes = {}
-        page_codes = {}
-        values = {}
-        value_tags = ["values_a", "dealt_codes", "values_b", "values_c", "values_a", "values_b", "page_codes0", "values_c"]
+        w_codes, w_scales, page_codes, values = {}, {}, {}, {}
         dealt_in = page0[PASS:, :].rearrange("(p t) m -> t p m", t=PACK)
         dealt_out = out_1[PASS:, :].rearrange("(p t) m -> t p m", t=PACK)
         gain_rows = wgs.rearrange("(u t) j -> u t j", t=PACK)
 
-        def scale_partitions(q):
-            return slice(QUADRANT * q, QUADRANT * q + SCALE_ROWS)
-
         def load_scale_rows(scale_tile, rows):
             passes = rows.shape[0]
-            for q in range(QUADRANTS):
+            for r in range(SCALE_ROWS):
                 nc.sync.dma_start(
-                    out=scale_tile[scale_partitions(q), :].bitcast(I32).rearrange("r (a c) -> r a c", a=passes),
-                    in_=rows[:, SCALE_ROWS * q : SCALE_ROWS * (q + 1), :].bitcast(I32).rearrange("a r c -> r a c"),
+                    out=scale_tile[r:P:QUADRANT, :].bitcast(I32).rearrange("q (a c) -> q a c", a=passes),
+                    in_=rows.bitcast(I32).rearrange("a (q r) c -> r q a c", r=SCALE_ROWS)[r],
                 )
 
         def load_weight(which, piece):
@@ -120,23 +115,21 @@ def tile_list_clue_memory_triple_kernel(
             for q in (0, 2, 1, 3):
                 nc.sync.dma_start(out=dealt_gains[t][QUADRANT * q : QUADRANT * (q + 1), :], in_=gain_rows[:, t, :])
 
-        def woven_part(n):
-            width = PACK * BANK
-            return woven[n // 2][:, (n % 2) * width : (n % 2 + 1) * width]
+        def woven_tile(name, first, parts, dtype=BF16, width=PACK * BANK):
+            return weave_pool.tile([P, parts * width], dtype, name=name, align_bytes=64, offset=2 * PACK * BANK * first)
 
-        def round_weight(engine_copy, loaded, piece, which, first, count):
-            base = which * PIECE * PACK
-            dst = woven_part(piece)[:, base + first * PACK : base + (first + count) * PACK]
+        def round_weight(engine_copy, source, target):
             engine_copy(
-                out=dst.rearrange("p (c i j) -> p c j i", i=4, j=PACK),
-                in_=loaded[:, :, first : first + count].rearrange("p j (c i) -> p c j i", i=4),
+                out=target.rearrange("p (c i j) -> p c j i", i=4, j=PACK), in_=source.rearrange("p j (c i) -> p c j i", i=4)
             )
 
-        def quantize_weight(piece, first, count):
+        def quantize_weight(key, codes, woven, first, count):
+            if key not in w_codes:
+                w_codes[key] = codes
+                w_scales[key] = held("w_scales%d" % key, [P, codes.shape[1]], U8)
             nc.vector.quantize_mx(
-                out=w_codes[piece][:, first : first + count].bitcast(FP8X4),
-                scales=w_scales[piece][:, first : first + count],
-                in_=woven_part(piece)[:, first * PACK : (first + count) * PACK],
+                out=codes[:, first : first + count].bitcast(FP8X4), scales=w_scales[key][:, first : first + count],
+                in_=woven[:, first * PACK : (first + count) * PACK],
             )
 
         def entries(offsets, first, count):
@@ -159,13 +152,14 @@ def tile_list_clue_memory_triple_kernel(
         nc.sync.dma_start(out=gain_whole[:], in_=wgs)
         nc.sync.dma_start(place[:], offs2)
         load_page(0)
-        for piece in range(1, PIECES + 1):
-            loaded[0, piece] = load_weight(0, piece)
-            loaded[1, piece] = load_weight(1, piece)
+        loaded[0, 1] = load_weight(0, 1)
+        loaded[1, 1] = load_weight(1, 1)
+        loaded[0, 2] = load_weight(0, 2)
         load_page(1)
+        loaded[1, 2] = load_weight(1, 2)
         for t in range(PACK):
-            load_page(2 + t)
             load_dealt_gain(t)
+            load_page(t + 2)
         for g in range(GROUPS):
             nc.sync.dma_start(
                 out=w4_codes[:, g * N : (g + 1) * N].bitcast(I32),
@@ -182,12 +176,13 @@ def tile_list_clue_memory_triple_kernel(
         pick_columns(picked_words, table_words, 0)
         pick_columns(picked_words, table_words, 1)
 
-        w_codes[0] = held("w_codes0", [P, 2 * PIECE], U32)
-        w_codes[1] = held("w_codes1", [P, 2 * PIECE], U32)
+        woven = woven_tile("woven_piece0", 0, 1)
+        codes = held("w_codes0", [P, 2 * PIECE], U32)
         for which in range(2):
-            round_weight(nc.scalar.copy, loaded[which, 0], 0, which, 0, P)
-            round_weight(nc.vector.tensor_copy, loaded[which, 0], 0, which, P, P)
-            quantize_weight(0, which * PIECE, PIECE)
+            for engine_copy, first in ((nc.scalar.copy, 0), (nc.vector.tensor_copy, P)):
+                place_in_woven = (which * PIECE + first) * PACK
+                round_weight(engine_copy, loaded[which, 0][:, :, first : first + P], woven[:, place_in_woven : place_in_woven + PASS])
+            quantize_weight(0, codes, woven, which * PIECE, PIECE)
 
         def product(bank, i, h, name):
             if name == "b":
@@ -209,38 +204,35 @@ def tile_list_clue_memory_triple_kernel(
             return slice(h * BANK, (h + 1) * BANK)
 
         def first_values():
-            values[0] = held("values0", [P, S], F32, value_tags[0])
+            values[0] = placed("values0", [P, S], F32, 16)
             for name in "abc":
                 for h in range(HALVES):
-                    bank = product(next_bank(), 0, h, name)
+                    bank = product(banks[name][h], 0, h, name)
                     other = gain_whole if name == "a" else values[0]
                     nc.vector.tensor_tensor(out=values[0][:, half(h)], in0=bank[:], in1=other[:, half(h)], op=MULT)
 
-        def make_values(i):
-            values[i] = held("values%d" % i, [P, S], F32, value_tags[i])
-            a, b = a_tiles[i % 2], b_tiles[i % 2]
-            for name, target in (("c", values[i]), ("a", a), ("b", b)):
-                for h in range(HALVES):
-                    bank = product(word_banks[h] if i <= ON_VECTOR and name == "c" else next_bank(), i, h, name)
-                    if i == ON_VECTOR and name == "c":
-                        nc.vector.tensor_tensor(out=target[:, half(h)], in0=bank[:], in1=gain_whole[:, half(h)], op=MULT)
-                    else:
-                        nc.scalar.copy(out=target[:, half(h)], in_=bank[:])
-            if i != ON_VECTOR:
-                gain = gain_whole if i < PACK else dealt_gains[i - PACK]
-                nc.gpsimd.tensor_tensor(out=values[i][:], in0=values[i][:], in1=gain[:], op=MULT)
-            nc.gpsimd.tensor_tensor(out=values[i][:], in0=values[i][:], in1=a[:], op=MULT)
-            if i < LAST:
-                nc.gpsimd.tensor_tensor(out=values[i][:], in0=values[i][:], in1=b[:], op=MULT)
+        def copy_product(target, i, name, bank_name):
+            for h in range(HALVES):
+                nc.scalar.copy(out=target[:, half(h)], in_=product(banks[bank_name][h], i, h, name)[:])
 
-        def round_piece(piece):
-            for which in range(2):
-                round_weight(nc.scalar.copy, loaded[which, piece], piece, which, 0, PIECE)
+        def begin_values(i, target):
+            values[i] = target
+            copy_product(b_tile, i, "b", "w" if i == 1 else "b")
+            gain = gain_whole if i < PACK else dealt_gains[i - PACK]
+            nc.gpsimd.tensor_tensor(out=target[:], in0=b_tile[:], in1=gain[:], op=MULT)
 
-        def round_dealt(which):
+        def multiply_by(i, name, target):
+            copy_product(target, i, name, name)
+            nc.gpsimd.tensor_tensor(out=values[i][:], in0=values[i][:], in1=target[:], op=MULT)
+
+        def finish_values(i, a, c):
+            multiply_by(i, "a", a)
+            multiply_by(i, "c", c)
+
+        def round_dealt(woven, which):
             width = PACK * PASS
             nc.scalar.copy(
-                out=woven[1][:, which * width : (which + 1) * width].rearrange("p (t m j) -> p m j t", t=PACK, j=PACK),
+                out=woven[:, which * width : (which + 1) * width].rearrange("p (t m j) -> p m j t", t=PACK, j=PACK),
                 in_=loaded[which, PIECES][:].rearrange("p j (m t) -> p m j t", t=PACK),
             )
 
@@ -256,7 +248,7 @@ def tile_list_clue_memory_triple_kernel(
 
         def place_values(i):
             if i == LAST:
-                nc.vector.tensor_tensor(out=pages[i][:].indirect(place[:]), in0=values[i][:], in1=b_tiles[i % 2][:], op=MULT)
+                nc.vector.tensor_tensor(out=pages[i][:].indirect(place[:]), in0=values[i][:], in1=last_c[:], op=MULT)
             else:
                 nc.vector.tensor_copy(out=pages[i][:].indirect(place[:]), in_=values[i][:])
             rows = out_1[i * P : (i + 1) * P, :] if i < PACK else dealt_out[i - PACK]
@@ -274,38 +266,40 @@ def tile_list_clue_memory_triple_kernel(
                 in_=bank[:].rearrange("p (b w u e) -> p b u w e", b=BLOCKS, u=2, e=2),
             )
 
-        def turn_back(chunk, copies):
+        def turn_back(chunk, target):
             words = turned[chunk][:].bitcast(F32)
-            target = woven_part(chunk).bitcast(F32)
+            target = target.bitcast(F32)
             for n in range(2):
                 for m in range(4):
                     first = (4 * n + m) * P
-                    nc.tensor.transpose(word_banks[n][:, m * P : (m + 1) * P], words[:, first : first + P], identity[:])
-                copies[n](
+                    nc.tensor.transpose(banks["w"][n][:, m * P : (m + 1) * P], words[:, first : first + P], identity[:])
+                nc.scalar.copy(
                     out=target[:, n * BANK : (n + 1) * BANK].rearrange("p (b m u) -> p b m u", b=2, u=2),
-                    in_=word_banks[n][:].rearrange("p (b u m) -> p b m u", b=2, u=2),
+                    in_=banks["w"][n][:].rearrange("p (b u m) -> p b m u", b=2, u=2),
                 )
 
-        def round_page(i, chunk):
+        def round_page(i, n):
             u, e = divmod(i - PACK, 2)
-            nc.scalar.copy(
-                out=turned[chunk][:].rearrange("p (u m e) -> p u m e", u=2, e=2)[:, u, :, e], in_=pages[i][:, chunk_columns(chunk)]
-            )
+            nc.scalar.copy(out=paired[n][:].rearrange("p (u m e) -> p u m e", u=2, e=2)[:, u, :, e], in_=pages[i][:, spans[n]])
 
-        def weave(chunk):
-            nc.vector.tensor_copy(
-                out=woven_part(chunk).bitcast(F32).rearrange("p (c i u) -> p c u i", i=4, u=2),
-                in_=turned[chunk][:].bitcast(F32).rearrange("p (u c i) -> p c u i", i=4, u=2),
+        def weave_and_quantize(n):
+            woven = weave_pool.tile(
+                [P, PACK * WIDTHS[n]], BF16, name="woven_span%d" % n, align_bytes=64, offset=2 * PACK * spans[n].start
             )
+            nc.vector.tensor_copy(
+                out=woven[:].bitcast(F32).rearrange("p (c i u) -> p c u i", i=4, u=2),
+                in_=paired[n][:].bitcast(F32).rearrange("p (u c i) -> p c u i", i=4, u=2),
+            )
+            quantize_page(1, spans[n], woven[:])
 
         def quantize_page(g, cols, source):
             nc.vector.quantize_mx(out=page_codes[g][:, cols].bitcast(FP8X4), scales=page_scales[g][:, cols], in_=source)
 
         def store_page_scales(g):
-            for q in range(QUADRANTS):
+            for r in range(SCALE_ROWS):
                 nc.sync.dma_start(
-                    out=out_3[g, SCALE_ROWS * q : SCALE_ROWS * (q + 1), :].bitcast(I32),
-                    in_=page_scales[g][scale_partitions(q), :].bitcast(I32),
+                    out=out_3[g].bitcast(I32).rearrange("(q r) m -> r q m", r=SCALE_ROWS)[r],
+                    in_=page_scales[g][r:P:QUADRANT, :].bitcast(I32),
                 )
 
         def store_page_codes(g, cols):
@@ -313,85 +307,132 @@ def tile_list_clue_memory_triple_kernel(
                 out=out_2[g].rearrange("p m t -> p (m t)").bitcast(I32)[:, cols], in_=page_codes[g][:, cols].bitcast(I32)
             )
 
-        def sum_bank(chunk, n):
-            return sum_banks[(chunk % 2) * N_TILES + n]
+        def read_page(g, bank, n, cols):
+            w4_cols = slice(g * N + n * P, g * N + (n + 1) * P)
+            nc.tensor.matmul_mx(
+                out=bank[:, : cols.stop - cols.start],
+                lhsT=w4_codes[:, w4_cols].bitcast(FP8X4), lhsT_scale=w4_scale_tile[:, w4_cols],
+                rhs=page_codes[g][:, cols].bitcast(FP8X4), rhs_scale=page_scales[g][:, cols],
+                start=(g == 0), stop=(g == GROUPS - 1),
+            )
 
-        def read_page(g, chunk):
-            cols = chunk_columns(chunk)
-            for n in range(N_TILES):
-                w4_cols = slice(g * N + n * P, g * N + (n + 1) * P)
-                nc.tensor.matmul_mx(
-                    out=sum_bank(chunk, n)[:],
-                    lhsT=w4_codes[:, w4_cols].bitcast(FP8X4), lhsT_scale=w4_scale_tile[:, w4_cols],
-                    rhs=page_codes[g][:, cols].bitcast(FP8X4), rhs_scale=page_scales[g][:, cols],
-                    start=(g == 0), stop=(g == GROUPS - 1),
-                )
+        def add_bias(target, bank, n, on_vector):
+            sums = bank[:, : target.shape[1]]
+            if on_vector:
+                nc.vector.tensor_scalar(out=target, in0=sums, scalar1=bias[:, n : n + 1], scalar2=None, op0=ADD)
+            else:
+                nc.scalar.activation(out=target, in_=sums, func=IDENTITY, bias=bias[:, n : n + 1])
 
-        def store_features(chunk):
-            features = wide_pool.tile([P, N_TILES, BANK], F32, name="features%d" % chunk, offset=4 * N_TILES * BANK * chunk)
-            for n in range(N_TILES):
-                if n == N_TILES - 1:
-                    nc.vector.tensor_scalar(
-                        out=features[:, n, :], in0=sum_bank(chunk, n)[:], scalar1=bias[:, n : n + 1], scalar2=None, op0=ADD
-                    )
-                else:
-                    nc.scalar.activation(
-                        out=features[:, n, :], in_=sum_bank(chunk, n)[:], func=IDENTITY, bias=bias[:, n : n + 1]
-                    )
-                nc.sync.dma_start(out=out_0[n * P : (n + 1) * P, chunk_columns(chunk)], in_=features[:, n, :])
+        def features_tile(n, cols):
+            width = cols.stop - cols.start
+            return wide_pool.tile(
+                [P, width], F32, name="features%d_%d" % (n, cols.start), offset=4 * (N_TILES * cols.start + n * width)
+            )
+
+        def round_tile(i):
+            for n in range(len(WIDTHS)):
+                round_page(i, n)
 
         def turn_tile(i):
             for chunk in range(CHUNKS):
-                turn_page(i, chunk, next_bank())
+                turn_page(i, chunk, banks["c"][chunk % 2])
 
         first_values()
         deal_w2()
-        make_values(1)
-        round_piece(1)
-        quantize_weight(1, 0, 2 * PIECE)
-        make_values(2)
-        round_dealt(0)
-        round_dealt(1)
+        b_tile = wide_pool.tile([P, S], F32, name="b", offset=4 * PACK * PIECE)
+        begin_values(1, placed("values1", [P, S], F32, 0))
+        x1 = placed("x1", [P, S], F32, 4)
+        finish_values(1, a_tile, x1)
+        begin_values(2, x1)
+        woven = placed("woven_piece1", [P, PACK * BANK], BF16, 8)
+        for which in range(2):
+            round_weight(nc.scalar.copy, loaded[which, 1][:], woven[:, which * PIECE * PACK : (which + 1) * PIECE * PACK])
+        woven_dealt = woven_tile("woven_dealt", 1, 2)
+        round_dealt(woven_dealt, 0)
 
-        for i in range(LAST):
-            place_values(i)
-            if i == 1:
-                w_codes[PIECES] = held("w_codes_dealt", [P, 2 * PASS], U32, value_tags[i])
-                nc.vector.quantize_mx(out=w_codes[PIECES][:].bitcast(FP8X4), scales=w_scales[PIECES][:], in_=woven[1][:])
-            if i + AHEAD < TILES:
-                make_values(i + AHEAD)
-            if i == 1:
-                turn_tile(0)
-            if 1 <= i < PACK:
-                turn_tile(i)
-            if i == PACK:
-                for chunk in range(CHUNKS):
-                    turn_back(chunk, [nc.scalar.copy, nc.scalar.copy])
-            if i == LAST - 1:
-                page_codes[0] = held("page_codes0", [P, T2], U32, value_tags[i])
-                for n in range(2):
-                    quantize_page(0, slice(n * 2 * BANK, (n + 1) * 2 * BANK), woven[n][:])
-                store_page_codes(0, slice(0, T2))
-                store_page_scales(0)
-            if i >= PACK:
-                for chunk in range(CHUNKS):
-                    round_page(i, chunk)
+        place_values(0)
+        quantize_weight(1, held("w_codes1", [P, 2 * PIECE], U32), woven, 0, 2 * PIECE)
+        x2 = placed("x2", [P, S], F32, 8)
+        finish_values(2, a_tile, x2)
+        round_dealt(woven_dealt, 1)
+        begin_values(3, x2)
+        turn_tile(0)
 
-        sum_banks = ring + word_banks
-        page_codes[1] = held("page_codes1", [P, T2], U32)
-        read_page(0, 0)
-        read_page(0, 1)
+        place_values(1)
+        quantize_weight(2, placed("w_codes2", [P, 2 * PASS], U32, 0), woven_dealt, 0, 2 * PASS)
+        a_odd = wide_pool.tile([P, S], F32, name="a_odd", offset=4 * PACK * (2 * PASS + PASS))
+        x0 = wide_pool.tile([P, S], F32, name="x0", offset=4 * PACK * (2 * PASS + PASS) + 4 * S)
+        finish_values(3, a_odd, x0)
+        begin_values(4, x0)
+        turn_tile(1)
+
+        place_values(2)
+        finish_values(4, a_tile, x1)
+        begin_values(5, x1)
+        turn_tile(2)
+
+        place_values(3)
+        finish_values(5, a_odd, x2)
+        begin_values(6, x2)
+        turn_tile(3)
+
+        place_values(4)
+        finish_values(6, a_tile, x0)
+        begin_values(7, x0)
+        multiply_by(7, "a", a_odd)
+        woven = [woven_tile("woven_group%d" % n, 2 * n, 2) for n in range(2)]
+        for chunk in range(CHUNKS):
+            turn_back(chunk, woven[chunk // 2][:, (chunk % 2) * PACK * BANK : (chunk % 2 + 1) * PACK * BANK])
+        paired = [
+            turn_pool.tile([P, PACK * width], BF16, name="paired%d" % n, align_bytes=64, offset=2 * PACK * spans[n].start)
+            for n, width in enumerate(WIDTHS)
+        ]
+        round_tile(4)
+
+        place_values(5)
+        last_c = x1
+        copy_product(last_c, LAST, "c", "c")
+        round_tile(5)
+
+        place_values(6)
+        page_codes[0] = placed("page_codes0", [P, T2], U32, 8)
+        for n in range(2):
+            quantize_page(0, slice(n * 2 * BANK, (n + 1) * 2 * BANK), woven[n][:])
+        store_page_codes(0, slice(0, T2))
+        store_page_scales(0)
+        round_tile(6)
+
+        sum_banks = banks["a"] + banks["b"] + banks["c"] + banks["w"]
+        page_codes[1] = placed("page_codes1", [P, T2], U32, 16)
+        for span in range(OPENED):
+            for n in range(N_TILES):
+                read_page(0, sum_banks[span * N_TILES + n], n, spans[span])
         place_values(LAST)
-        for chunk in range(CHUNKS):
-            round_page(LAST, chunk)
-        for chunk in range(CHUNKS):
-            weave(chunk)
-            quantize_page(1, chunk_columns(chunk), woven_part(chunk))
-            if chunk % 2 == 1:
-                store_page_codes(1, slice((chunk - 1) * BANK, (chunk + 1) * BANK))
-            if chunk == CHUNKS - 1:
-                store_page_scales(1)
-            read_page(1, chunk)
-            store_features(chunk)
-            if chunk + 2 < CHUNKS:
-                read_page(0, chunk + 2)
+        round_page(LAST, 0)
+        for span in range(OPENED):
+            round_page(LAST, span + 1)
+            weave_and_quantize(span)
+            store_page_codes(1, spans[span])
+            for n in range(N_TILES):
+                bank = sum_banks[span * N_TILES + n]
+                read_page(1, bank, n, spans[span])
+                features = features_tile(n, spans[span])
+                add_bias(features[:], bank, n, False)
+                nc.sync.dma_start(out=out_0[n * P : (n + 1) * P, spans[span]], in_=features[:])
+        rest = slice(spans[OPENED].start, T2)
+        for span in range(OPENED, len(WIDTHS)):
+            if span + 1 < len(WIDTHS):
+                round_page(LAST, span + 1)
+            weave_and_quantize(span)
+        store_page_codes(1, rest)
+        store_page_scales(1)
+        for n in range(N_TILES):
+            features = features_tile(n, rest)
+            for span in range(OPENED, len(WIDTHS)):
+                turn = n * (len(WIDTHS) - OPENED) + span - OPENED
+                bank = sum_banks[turn % len(sum_banks)]
+                read_page(0, bank, n, spans[span])
+                read_page(1, bank, n, spans[span])
+                target = features[:, spans[span].start - rest.start : spans[span].stop - rest.start]
+                add_bias(target, bank, n, turn % 2 == 1)
+            nc.sync.dma_start(out=out_0[n * P : (n + 1) * P, rest], in_=features[:])

@@ -33,6 +33,7 @@ QUADRANT = 32
 QUADRANTS = P // QUADRANT
 SCALE_ROWS = 4
 PER_COLUMN = 16
+ON_VECTOR = PACK
 WIDTHS = (256, 512, 512, 512, 256)
 OPENED = 2
 PIECE = 2 * P
@@ -217,13 +218,20 @@ def tile_list_clue_memory_triple_kernel(
 
         def begin_values(i, target):
             values[i] = target
-            copy_product(b_tile, i, "b", "w" if i == 1 else "b")
+            b_tile = b_tiles[i in (1, 3)]
             gain = gain_whole if i < PACK else dealt_gains[i - PACK]
-            nc.gpsimd.tensor_tensor(out=target[:], in0=b_tile[:], in1=gain[:], op=MULT)
+            if i == ON_VECTOR:
+                for h in range(HALVES):
+                    bank = product(banks["b"][h], i, h, "b")
+                    nc.vector.tensor_tensor(out=b_tile[:, half(h)], in0=bank[:], in1=gain[:, half(h)], op=MULT)
+            else:
+                copy_product(b_tile, i, "b", "w" if i == 1 else "b")
+                nc.gpsimd.tensor_tensor(out=target[:], in0=b_tile[:], in1=gain[:], op=MULT)
 
         def multiply_by(i, name, target):
             copy_product(target, i, name, name)
-            nc.gpsimd.tensor_tensor(out=values[i][:], in0=values[i][:], in1=target[:], op=MULT)
+            so_far = b_tiles[i in (1, 3)] if i == ON_VECTOR and name == "a" else values[i]
+            nc.gpsimd.tensor_tensor(out=values[i][:], in0=so_far[:], in1=target[:], op=MULT)
 
         def finish_values(i, a, c):
             multiply_by(i, "a", a)
@@ -339,12 +347,12 @@ def tile_list_clue_memory_triple_kernel(
 
         first_values()
         deal_w2()
-        b_tile = wide_pool.tile([P, S], F32, name="b", offset=4 * PACK * PIECE)
+        b_tiles = [wide_pool.tile([P, S], F32, name="b%d" % n, offset=4 * PACK * PIECE * n) for n in range(2)]
         begin_values(1, placed("values1", [P, S], F32, 0))
-        x1 = placed("x1", [P, S], F32, 4)
+        x1 = placed("x1", [P, S], F32, 8)
         finish_values(1, a_tile, x1)
         begin_values(2, x1)
-        woven = placed("woven_piece1", [P, PACK * BANK], BF16, 8)
+        woven = placed("woven_piece1", [P, PACK * BANK], BF16, 4)
         for which in range(2):
             round_weight(nc.scalar.copy, loaded[which, 1][:], woven[:, which * PIECE * PACK : (which + 1) * PIECE * PACK])
         woven_dealt = woven_tile("woven_dealt", 1, 2)
@@ -352,11 +360,11 @@ def tile_list_clue_memory_triple_kernel(
 
         place_values(0)
         quantize_weight(1, held("w_codes1", [P, 2 * PIECE], U32), woven, 0, 2 * PIECE)
-        x2 = placed("x2", [P, S], F32, 8)
-        finish_values(2, a_tile, x2)
-        round_dealt(woven_dealt, 1)
+        x2 = placed("x2", [P, S], F32, 4)
+        x3 = placed("x3", [P, S], F32, 12)
         begin_values(3, x2)
-        turn_tile(0)
+        finish_values(2, a_tile, x3)
+        round_dealt(woven_dealt, 1)
 
         place_values(1)
         quantize_weight(2, placed("w_codes2", [P, 2 * PASS], U32, 0), woven_dealt, 0, 2 * PASS)
@@ -364,22 +372,25 @@ def tile_list_clue_memory_triple_kernel(
         x0 = wide_pool.tile([P, S], F32, name="x0", offset=4 * PACK * (2 * PASS + PASS) + 4 * S)
         finish_values(3, a_odd, x0)
         begin_values(4, x0)
+        turn_tile(0)
+        finish_values(4, a_tile, x3)
+        begin_values(5, x3)
         turn_tile(1)
 
         place_values(2)
-        finish_values(4, a_tile, x1)
-        begin_values(5, x1)
+        finish_values(5, a_odd, x1)
+        begin_values(6, x1)
         turn_tile(2)
 
         place_values(3)
-        finish_values(5, a_odd, x2)
-        begin_values(6, x2)
+        finish_values(6, a_tile, x2)
+        begin_values(7, x2)
+        multiply_by(7, "a", a_odd)
         turn_tile(3)
 
         place_values(4)
-        finish_values(6, a_tile, x0)
-        begin_values(7, x0)
-        multiply_by(7, "a", a_odd)
+        last_c = x0
+        copy_product(last_c, LAST, "c", "c")
         woven = [woven_tile("woven_group%d" % n, 2 * n, 2) for n in range(2)]
         for chunk in range(CHUNKS):
             turn_back(chunk, woven[chunk // 2][:, (chunk % 2) * PACK * BANK : (chunk % 2 + 1) * PACK * BANK])
@@ -390,8 +401,6 @@ def tile_list_clue_memory_triple_kernel(
         round_tile(4)
 
         place_values(5)
-        last_c = x1
-        copy_product(last_c, LAST, "c", "c")
         round_tile(5)
 
         place_values(6)
@@ -435,4 +444,7 @@ def tile_list_clue_memory_triple_kernel(
                 read_page(1, bank, n, spans[span])
                 target = features[:, spans[span].start - rest.start : spans[span].stop - rest.start]
                 add_bias(target, bank, n, turn % 2 == 1)
-            nc.sync.dma_start(out=out_0[n * P : (n + 1) * P, rest], in_=features[:])
+                if n == N_TILES - 1:
+                    nc.sync.dma_start(out=out_0[n * P : (n + 1) * P, spans[span]], in_=target)
+            if n < N_TILES - 1:
+                nc.sync.dma_start(out=out_0[n * P : (n + 1) * P, rest], in_=features[:])

@@ -228,13 +228,14 @@ def tile_list_clue_memory_triple_kernel(
                 copy_product(b_tile, i, "b", "w" if i == 1 else "b")
                 nc.gpsimd.tensor_tensor(out=target[:], in0=b_tile[:], in1=gain[:], op=MULT)
 
-        def multiply_by(i, name, target):
-            copy_product(target, i, name, name)
+        def multiply_by(i, name, target, moved=None):
+            copy_product(target, i, name, "w" if i == 1 and name == "c" else name)
             so_far = b_tiles[i in (1, 3)] if i == ON_VECTOR and name == "a" else values[i]
+            values[i] = values[i] if moved is None else moved
             nc.gpsimd.tensor_tensor(out=values[i][:], in0=so_far[:], in1=target[:], op=MULT)
 
-        def finish_values(i, a, c):
-            multiply_by(i, "a", a)
+        def finish_values(i, a, c, moved=None):
+            multiply_by(i, "a", a, moved)
             multiply_by(i, "c", c)
 
         def round_dealt(woven, which):
@@ -367,11 +368,11 @@ def tile_list_clue_memory_triple_kernel(
         round_dealt(woven_dealt, 1)
 
         place_values(1)
-        quantize_weight(2, placed("w_codes2", [P, 2 * PASS], U32, 0), woven_dealt, 0, 2 * PASS)
         a_odd = wide_pool.tile([P, S], F32, name="a_odd", offset=4 * PACK * (2 * PASS + PASS))
         x0 = wide_pool.tile([P, S], F32, name="x0", offset=4 * PACK * (2 * PASS + PASS) + 4 * S)
-        finish_values(3, a_odd, x0)
         begin_values(4, x0)
+        quantize_weight(2, placed("w_codes2", [P, 2 * PASS], U32, 0), woven_dealt, 0, 2 * PASS)
+        finish_values(3, a_odd, x0, woven_tile("values3", 1, 1, F32, S))
         turn_tile(0)
         finish_values(4, a_tile, x3)
         begin_values(5, x3)

@@ -33,6 +33,7 @@ QUADRANT = 32
 QUADRANTS = P // QUADRANT
 SCALE_ROWS = 4
 PER_COLUMN = 16
+SCALAR_COLUMNS = (256, 192)
 ON_VECTOR = PACK
 WIDTHS = (256, 512, 512, 512, 256)
 OPENED = 2
@@ -150,7 +151,8 @@ def tile_list_clue_memory_triple_kernel(
         nc.sync.dma_start(out=table_words[:].bitcast(I32), in_=tab_words[0].rearrange("p t i -> p (t i)").bitcast(I32))
         load_scale_rows(w2_scale_tile, w2_scales)
         loaded = {(0, 0): load_weight(0, 0), (1, 0): load_weight(1, 0)}
-        nc.sync.dma_start(out=gain_whole[:], in_=wgs)
+        for h in range(HALVES):
+            nc.sync.dma_start(out=gain_whole[:, h * BANK : (h + 1) * BANK], in_=wgs[:, h * BANK : (h + 1) * BANK])
         nc.sync.dma_start(place[:], offs2)
         load_page(0)
         loaded[0, 1] = load_weight(0, 1)
@@ -158,9 +160,11 @@ def tile_list_clue_memory_triple_kernel(
         loaded[0, 2] = load_weight(0, 2)
         load_page(1)
         loaded[1, 2] = load_weight(1, 2)
-        for t in range(PACK):
-            load_dealt_gain(t)
+        load_dealt_gain(0)
+        load_page(2)
+        for t in range(1, PACK):
             load_page(t + 2)
+            load_dealt_gain(t)
         for g in range(GROUPS):
             nc.sync.dma_start(
                 out=w4_codes[:, g * N : (g + 1) * N].bitcast(I32),
@@ -177,12 +181,14 @@ def tile_list_clue_memory_triple_kernel(
         pick_columns(picked_words, table_words, 0)
         pick_columns(picked_words, table_words, 1)
 
-        woven = woven_tile("woven_piece0", 0, 1)
+        woven = placed("woven_piece0", [P, PACK * BANK], BF16, 0)
         codes = held("w_codes0", [P, 2 * PIECE], U32)
         for which in range(2):
-            for engine_copy, first in ((nc.scalar.copy, 0), (nc.vector.tensor_copy, P)):
-                place_in_woven = (which * PIECE + first) * PACK
-                round_weight(engine_copy, loaded[which, 0][:, :, first : first + P], woven[:, place_in_woven : place_in_woven + PASS])
+            split = SCALAR_COLUMNS[which]
+            for engine_copy, cols in ((nc.scalar.copy, slice(0, split)), (nc.vector.tensor_copy, slice(split, PIECE))):
+                if cols.start < cols.stop:
+                    target = woven[:, (which * PIECE + cols.start) * PACK : (which * PIECE + cols.stop) * PACK]
+                    round_weight(engine_copy, loaded[which, 0][:, :, cols], target)
             quantize_weight(0, codes, woven, which * PIECE, PIECE)
 
         def product(bank, i, h, name):
@@ -206,10 +212,10 @@ def tile_list_clue_memory_triple_kernel(
 
         def first_values():
             values[0] = placed("values0", [P, S], F32, 16)
-            for name in "abc":
+            for name in "bac":
                 for h in range(HALVES):
                     bank = product(banks[name][h], 0, h, name)
-                    other = gain_whole if name == "a" else values[0]
+                    other = gain_whole if name == "b" else values[0]
                     nc.vector.tensor_tensor(out=values[0][:, half(h)], in0=bank[:], in1=other[:, half(h)], op=MULT)
 
         def copy_product(target, i, name, bank_name):
@@ -229,7 +235,7 @@ def tile_list_clue_memory_triple_kernel(
                 nc.gpsimd.tensor_tensor(out=target[:], in0=b_tile[:], in1=gain[:], op=MULT)
 
         def multiply_by(i, name, target, moved=None):
-            copy_product(target, i, name, "w" if i == 1 and name == "c" else name)
+            copy_product(target, i, name, {"a": "w", "c": "b"}[name] if i == 1 else name)
             so_far = b_tiles[i in (1, 3)] if i == ON_VECTOR and name == "a" else values[i]
             values[i] = values[i] if moved is None else moved
             nc.gpsimd.tensor_tensor(out=values[i][:], in0=so_far[:], in1=target[:], op=MULT)

@@ -33,9 +33,9 @@ QUADRANT = 32
 QUADRANTS = P // QUADRANT
 SCALE_ROWS = 4
 PER_COLUMN = 16
-SCALAR_COLUMNS = (256, 192)
+SCALAR_COLUMNS = (256, 128)
 ON_VECTOR = PACK
-WIDTHS = (256, 512, 512, 512, 256)
+WIDTHS = (512, 512, 512, 512)
 OPENED = 2
 PIECE = 2 * P
 PIECES = PASS // PIECE
@@ -231,7 +231,8 @@ def tile_list_clue_memory_triple_kernel(
                     bank = product(banks["b"][h], i, h, "b")
                     nc.vector.tensor_tensor(out=b_tile[:, half(h)], in0=bank[:], in1=gain[:, half(h)], op=MULT)
             else:
-                copy_product(b_tile, i, "b", "w" if i == 1 else "b")
+                if i != 3:
+                    copy_product(b_tile, i, "b", "w" if i == 1 else "b")
                 nc.gpsimd.tensor_tensor(out=target[:], in0=b_tile[:], in1=gain[:], op=MULT)
 
         def multiply_by(i, name, target, moved=None):
@@ -307,8 +308,14 @@ def tile_list_clue_memory_triple_kernel(
             )
             quantize_page(1, spans[n], woven[:])
 
+        def codes_of(g, cols):
+            if g == 0:
+                first = cols.start // S * S
+                return page_codes[0][cols.start // S][:, cols.start - first : cols.stop - first]
+            return page_codes[g][:, cols]
+
         def quantize_page(g, cols, source):
-            nc.vector.quantize_mx(out=page_codes[g][:, cols].bitcast(FP8X4), scales=page_scales[g][:, cols], in_=source)
+            nc.vector.quantize_mx(out=codes_of(g, cols).bitcast(FP8X4), scales=page_scales[g][:, cols], in_=source)
 
         def store_page_scales(g):
             for r in range(SCALE_ROWS):
@@ -319,7 +326,7 @@ def tile_list_clue_memory_triple_kernel(
 
         def store_page_codes(g, cols):
             nc.sync.dma_start(
-                out=out_2[g].rearrange("p m t -> p (m t)").bitcast(I32)[:, cols], in_=page_codes[g][:, cols].bitcast(I32)
+                out=out_2[g].rearrange("p m t -> p (m t)").bitcast(I32)[:, cols], in_=codes_of(g, cols).bitcast(I32)
             )
 
         def read_page(g, bank, n, cols):
@@ -327,7 +334,7 @@ def tile_list_clue_memory_triple_kernel(
             nc.tensor.matmul_mx(
                 out=bank[:, : cols.stop - cols.start],
                 lhsT=w4_codes[:, w4_cols].bitcast(FP8X4), lhsT_scale=w4_scale_tile[:, w4_cols],
-                rhs=page_codes[g][:, cols].bitcast(FP8X4), rhs_scale=page_scales[g][:, cols],
+                rhs=codes_of(g, cols).bitcast(FP8X4), rhs_scale=page_scales[g][:, cols],
                 start=(g == 0), stop=(g == GROUPS - 1),
             )
 
@@ -362,6 +369,7 @@ def tile_list_clue_memory_triple_kernel(
         woven = placed("woven_piece1", [P, PACK * BANK], BF16, 4)
         for which in range(2):
             round_weight(nc.scalar.copy, loaded[which, 1][:], woven[:, which * PIECE * PACK : (which + 1) * PIECE * PACK])
+        copy_product(b_tiles[1], 3, "b", "b")
         woven_dealt = woven_tile("woven_dealt", 1, 2)
         round_dealt(woven_dealt, 0)
 
@@ -411,11 +419,9 @@ def tile_list_clue_memory_triple_kernel(
         round_tile(5)
 
         place_values(6)
-        page_codes[0] = placed("page_codes0", [P, T2], U32, 8)
-        for n in range(2):
-            quantize_page(0, slice(n * 2 * BANK, (n + 1) * 2 * BANK), woven[n][:])
-        store_page_codes(0, slice(0, T2))
-        store_page_scales(0)
+        page_codes[0] = [placed("page_codes0a", [P, S], U32, 8)]
+        quantize_page(0, slice(0, S), woven[0][:])
+        store_page_codes(0, slice(0, S))
         round_tile(6)
 
         sum_banks = banks["a"] + banks["b"] + banks["c"] + banks["w"]
@@ -424,34 +430,35 @@ def tile_list_clue_memory_triple_kernel(
             for n in range(N_TILES):
                 read_page(0, sum_banks[span * N_TILES + n], n, spans[span])
         place_values(LAST)
+        page_codes[0].append(placed("page_codes0b", [P, S], U32, 4))
+        quantize_page(0, slice(S, T2), woven[1][:])
+        store_page_codes(0, slice(S, T2))
+        store_page_scales(0)
         round_page(LAST, 0)
-        for span in range(OPENED):
-            round_page(LAST, span + 1)
-            weave_and_quantize(span)
-            store_page_codes(1, spans[span])
-            for n in range(N_TILES):
-                bank = sum_banks[span * N_TILES + n]
-                read_page(1, bank, n, spans[span])
-                features = features_tile(n, spans[span])
-                add_bias(features[:], bank, n, False)
-                nc.sync.dma_start(out=out_0[n * P : (n + 1) * P, spans[span]], in_=features[:])
-        rest = slice(spans[OPENED].start, T2)
-        for span in range(OPENED, len(WIDTHS)):
-            if span + 1 < len(WIDTHS):
+        round_page(LAST, 1)
+        weave_and_quantize(0)
+        store_page_codes(1, spans[0])
+        for n in range(N_TILES):
+            read_page(1, sum_banks[n], n, spans[0])
+            features = features_tile(n, spans[0])
+            add_bias(features[:], sum_banks[n], n, False)
+            nc.sync.dma_start(out=out_0[n * P : (n + 1) * P, spans[0]], in_=features[:])
+        rest = slice(spans[1].start, T2)
+        for span in range(1, CHUNKS):
+            if span + 1 < CHUNKS:
                 round_page(LAST, span + 1)
             weave_and_quantize(span)
         store_page_codes(1, rest)
         store_page_scales(1)
         for n in range(N_TILES):
             features = features_tile(n, rest)
-            for span in range(OPENED, len(WIDTHS)):
-                turn = n * (len(WIDTHS) - OPENED) + span - OPENED
-                bank = sum_banks[turn % len(sum_banks)]
-                read_page(0, bank, n, spans[span])
+            for span in range(1, CHUNKS):
+                if span < OPENED:
+                    bank = sum_banks[N_TILES + n]
+                else:
+                    bank = sum_banks[(2 * n + span - OPENED) % N_TILES]
+                    read_page(0, bank, n, spans[span])
                 read_page(1, bank, n, spans[span])
                 target = features[:, spans[span].start - rest.start : spans[span].stop - rest.start]
-                add_bias(target, bank, n, turn % 2 == 1)
-                if n == N_TILES - 1:
-                    nc.sync.dma_start(out=out_0[n * P : (n + 1) * P, spans[span]], in_=target)
-            if n < N_TILES - 1:
-                nc.sync.dma_start(out=out_0[n * P : (n + 1) * P, rest], in_=features[:])
+                add_bias(target, bank, n, span == CHUNKS - 1 or (span == OPENED and n % 2 == 1))
+            nc.sync.dma_start(out=out_0[n * P : (n + 1) * P, rest], in_=features[:])

@@ -73,7 +73,8 @@ def tile_list_clue_memory_triple_kernel(
         w4_scale_tile = held("w4_scale_tile", [P, GROUPS * N], U8)
         bias = held("bias", [P, N_TILES], F32)
         gain_whole = held("gain_whole", [P, S], F32)
-        dealt_gains = [held("dealt_gain%d" % t, [P, S], F32) for t in range(PACK)]
+        gain_tiles = [held("dealt_gain%d" % t, [P, 2 * S if t in (1, 2) else S], F32) for t in range(PACK)]
+        dealt_gains = [tile[:, :S] for tile in gain_tiles]
         w2_dealt_codes = held("w2_dealt_codes", [P, 2 * PASS], U8)
         w2_dealt_scales = held("w2_dealt_scales", [P, PASS], U8)
         identity = held("identity", [P, P], F32)
@@ -128,7 +129,7 @@ def tile_list_clue_memory_triple_kernel(
         def quantize_weight(key, codes, woven, first, count):
             if key not in w_codes:
                 w_codes[key] = codes
-                w_scales[key] = held("w_scales%d" % key, [P, codes.shape[1]], U8)
+                w_scales[key] = held("w_scales%d" % key, [P, codes.shape[1]], U8, "dealt_gain0" if key == PIECES else None)
             nc.vector.quantize_mx(
                 out=codes[:, first : first + count].bitcast(FP8X4), scales=w_scales[key][:, first : first + count],
                 in_=woven[:, first * PACK : (first + count) * PACK],
@@ -211,7 +212,7 @@ def tile_list_clue_memory_triple_kernel(
             return slice(h * BANK, (h + 1) * BANK)
 
         def first_values():
-            values[0] = placed("values0", [P, S], F32, 16)
+            values[0] = placed("values0", [P, S], F32, 22)
             for name in "bac":
                 for h in range(HALVES):
                     bank = product(banks[name][h], 0, h, name)
@@ -224,20 +225,20 @@ def tile_list_clue_memory_triple_kernel(
 
         def begin_values(i, target):
             values[i] = target
-            b_tile = b_tiles[i in (1, 3)]
+            b_tile = b_tiles[i in (1, 3, 5)]
             gain = gain_whole if i < PACK else dealt_gains[i - PACK]
             if i == ON_VECTOR:
                 for h in range(HALVES):
                     bank = product(banks["b"][h], i, h, "b")
                     nc.vector.tensor_tensor(out=b_tile[:, half(h)], in0=bank[:], in1=gain[:, half(h)], op=MULT)
             else:
-                if i != 3:
+                if i not in (3, 5):
                     copy_product(b_tile, i, "b", "w" if i == 1 else "b")
                 nc.gpsimd.tensor_tensor(out=target[:], in0=b_tile[:], in1=gain[:], op=MULT)
 
         def multiply_by(i, name, target, moved=None):
             copy_product(target, i, name, {"a": "w", "c": "b"}[name] if i == 1 else name)
-            so_far = b_tiles[i in (1, 3)] if i == ON_VECTOR and name == "a" else values[i]
+            so_far = b_tiles[i in (1, 3, 5)] if i == ON_VECTOR and name == "a" else values[i]
             values[i] = values[i] if moved is None else moved
             nc.gpsimd.tensor_tensor(out=values[i][:], in0=so_far[:], in1=target[:], op=MULT)
 
@@ -363,9 +364,12 @@ def tile_list_clue_memory_triple_kernel(
         deal_w2()
         b_tiles = [wide_pool.tile([P, S], F32, name="b%d" % n, offset=4 * PACK * PIECE * n) for n in range(2)]
         begin_values(1, placed("values1", [P, S], F32, 0))
-        x1 = placed("x1", [P, S], F32, 8)
+        x1 = placed("x1", [P, S], F32, 10)
         finish_values(1, a_tile, x1)
-        begin_values(2, x1)
+        values[2] = x1
+        b_half = placed("b_half", [P, BANK], F32, 8)
+        nc.scalar.copy(out=b_half[:], in_=product(banks["b"][0], 2, 0, "b")[:])
+        nc.gpsimd.tensor_tensor(out=x1[:, half(0)], in0=b_half[:], in1=gain_whole[:, half(0)], op=MULT)
         woven = placed("woven_piece1", [P, PACK * BANK], BF16, 4)
         for which in range(2):
             round_weight(nc.scalar.copy, loaded[which, 1][:], woven[:, which * PIECE * PACK : (which + 1) * PIECE * PACK])
@@ -374,9 +378,10 @@ def tile_list_clue_memory_triple_kernel(
         round_dealt(woven_dealt, 0)
 
         place_values(0)
+        nc.vector.tensor_tensor(out=x1[:, half(1)], in0=product(banks["w"][1], 2, 1, "b")[:], in1=gain_whole[:, half(1)], op=MULT)
         quantize_weight(1, held("w_codes1", [P, 2 * PIECE], U32), woven, 0, 2 * PIECE)
-        x2 = placed("x2", [P, S], F32, 4)
-        x3 = placed("x3", [P, S], F32, 12)
+        x2 = placed("x2", [P, S], F32, 6)
+        x3 = placed("x3", [P, S], F32, 14)
         begin_values(3, x2)
         finish_values(2, a_tile, x3)
         round_dealt(woven_dealt, 1)
@@ -389,17 +394,26 @@ def tile_list_clue_memory_triple_kernel(
         finish_values(3, a_odd, x0, woven_tile("values3", 1, 1, F32, S))
         turn_tile(0)
         finish_values(4, a_tile, x3)
-        begin_values(5, x3)
+        pair = placed("pair", [P, 2 * S], F32, 14)
+
+        def merged_values(i, left, target):
+            values[i] = target
+            right = gain_tiles[i - PACK]
+            copy_product(left[:, :S], i, "b", "b")
+            copy_product(left[:, S:], i, "a", "a")
+            copy_product(right[:, S:], i, "c", "c")
+            nc.gpsimd.tensor_tensor(out=pair[:], in0=left[:], in1=right[:], op=MULT)
+            nc.gpsimd.tensor_tensor(out=target[:], in0=pair[:, :S], in1=pair[:, S:], op=MULT)
+
+        merged_values(5, held("left5", [P, 2 * S], F32, "table_words"), x2)
         turn_tile(1)
 
         place_values(2)
-        finish_values(5, a_odd, x1)
-        begin_values(6, x1)
+        merged_values(6, held("left6", [P, 2 * S], F32), x1)
         turn_tile(2)
 
         place_values(3)
-        finish_values(6, a_tile, x2)
-        begin_values(7, x2)
+        begin_values(7, placed("values7", [P, S], F32, 14))
         multiply_by(7, "a", a_odd)
         turn_tile(3)
 
@@ -419,18 +433,18 @@ def tile_list_clue_memory_triple_kernel(
         round_tile(5)
 
         place_values(6)
-        page_codes[0] = [placed("page_codes0a", [P, S], U32, 8)]
+        page_codes[0] = [placed("page_codes0a", [P, S], U32, 10)]
         quantize_page(0, slice(0, S), woven[0][:])
         store_page_codes(0, slice(0, S))
         round_tile(6)
 
         sum_banks = banks["a"] + banks["b"] + banks["c"] + banks["w"]
-        page_codes[1] = placed("page_codes1", [P, T2], U32, 16)
+        page_codes[1] = placed("page_codes1", [P, T2], U32, 22)
         for span in range(OPENED):
             for n in range(N_TILES):
                 read_page(0, sum_banks[span * N_TILES + n], n, spans[span])
         place_values(LAST)
-        page_codes[0].append(placed("page_codes0b", [P, S], U32, 4))
+        page_codes[0].append(placed("page_codes0b", [P, S], U32, 14))
         quantize_page(0, slice(S, T2), woven[1][:])
         store_page_codes(0, slice(S, T2))
         store_page_scales(0)

@@ -33,13 +33,10 @@ QUADRANT = 32
 QUADRANTS = P // QUADRANT
 SCALE_ROWS = 4
 PER_COLUMN = 16
-SCALAR_COLUMNS = (256, 128)
-ON_VECTOR = PACK
-WIDTHS = (512, 512, 512, 512)
-OPENED = 2
 PIECE = 2 * P
-PIECES = PASS // PIECE
-AHEAD = 3
+BANKS = 8
+LEAD = 256
+OPENED = 2
 
 
 def tile_list_clue_memory_triple_kernel(
@@ -49,48 +46,50 @@ def tile_list_clue_memory_triple_kernel(
     nc = tc.nc
     with ExitStack() as ctx:
         keep = ctx.enter_context(tc.tile_pool(name="keep", bufs=1))
-        wide_pool = ctx.enter_context(tc.tile_pool(name="wide", bufs=1))
-        weave_pool = ctx.enter_context(tc.tile_pool(name="weave", bufs=1))
-        psum = ctx.enter_context(tc.psum_pool(name="psum", bufs=1))
-        banks = {name: [psum.tile([P, BANK], F32, name="bank_%s%d" % (name, h)) for h in range(2)] for name in "abcw"}
         turns = ctx.enter_context(tc.tile_pool(name="turns", bufs=1))
+        psum = ctx.enter_context(tc.psum_pool(name="psum", bufs=1))
+        banks = [psum.tile([P, BANK], F32, name="bank%d" % n) for n in range(BANKS)]
+        used = []
+
+        def next_bank():
+            used.append(None)
+            return banks[(len(used) - 1) % BANKS]
+
+        def held(name, shape, dtype):
+            return keep.tile(shape, dtype, name=name, align_bytes=64)
 
         def placed(name, shape, dtype, kib):
             return turns.tile(shape, dtype, name=name, align_bytes=64, offset=1024 * kib)
 
-        def held(name, shape, dtype, tag=None):
-            return keep.tile(shape, dtype, name=name, tag=tag or name, align_bytes=64)
-
         pick = keep.tile([P, S // PER_COLUMN], U16, name="pick")
         place = keep.tile([P, S // PER_COLUMN], U16, name="place")
-        table_words = held("table_words", [P, T], U32)
-        table_scales = held("table_scales", [P, T], U8)
         picked_words = [held("picked_words%d" % h, [P, BANK], U32) for h in range(HALVES)]
         picked_scales = [held("picked_scales%d" % h, [P, BANK], U8) for h in range(HALVES)]
         w2_codes = held("w2_codes", [P, 2 * H], U8)
         w2_scale_tile = held("w2_scale_tile", [P, H], U8)
+        w2_dealt_scales = held("w2_dealt_scales", [P, PASS], U8)
         w4_codes = held("w4_codes", [P, GROUPS * N], U32)
         w4_scale_tile = held("w4_scale_tile", [P, GROUPS * N], U8)
         bias = held("bias", [P, N_TILES], F32)
-        gain_whole = held("gain_whole", [P, S], F32)
-        gain_tiles = [held("dealt_gain%d" % t, [P, 2 * S if t in (1, 2) else S], F32) for t in range(PACK)]
-        dealt_gains = [tile[:, :S] for tile in gain_tiles]
-        w2_dealt_codes = held("w2_dealt_codes", [P, 2 * PASS], U8)
-        w2_dealt_scales = held("w2_dealt_scales", [P, PASS], U8)
+        gain = held("gain", [P, S], F32)
         identity = held("identity", [P, P], F32)
         pages = [held("page%d" % i, [P, T2], F32) for i in range(TILES)]
-        a_tile = held("a", [P, S], F32)
-        turn_pool = ctx.enter_context(tc.tile_pool(name="turn", bufs=1))
-        turned = [
-            turn_pool.tile([P, PACK * BANK], BF16, name="turned%d" % c, align_bytes=64, offset=2 * PACK * BANK * c)
-            for c in range(CHUNKS)
-        ]
-        spans = [slice(sum(WIDTHS[:n]), sum(WIDTHS[: n + 1])) for n in range(len(WIDTHS))]
         page_scales = [held("page_scales%d" % g, [P, T2], U8) for g in range(GROUPS)]
-        w_codes, w_scales, page_codes, values = {}, {}, {}, {}
+        widths = (PIECE, PIECE, PASS)
+        w_scales = [held("w_scales%d" % n, [P, 2 * width], U8) for n, width in enumerate(widths)]
+        turned = [held("turned%d" % c, [P, PACK * BANK], BF16) for c in range(CHUNKS)]
+
+        TABLE, LOADED, LEFT, WOVEN_W, CODES_W, WOVEN_PAGE, PLANES, PAIR, VALUES, SPARE = 0, 8, 40, 48, 64, 72, 88, 104, 112, 124
+        table_words = placed("table_words", [P, T], U32, TABLE)
+        table_scales = placed("table_scales", [P, T], U8, CODES_W)
+        loaded = {}
+        values = {}
         dealt_in = page0[PASS:, :].rearrange("(p t) m -> t p m", t=PACK)
         dealt_out = out_1[PASS:, :].rearrange("(p t) m -> t p m", t=PACK)
         gain_rows = wgs.rearrange("(u t) j -> u t j", t=PACK)
+
+        def half(h):
+            return slice(h * BANK, (h + 1) * BANK)
 
         def load_scale_rows(scale_tile, rows):
             passes = rows.shape[0]
@@ -101,218 +100,140 @@ def tile_list_clue_memory_triple_kernel(
                 )
 
         def load_weight(which, piece):
-            first, width = piece * PIECE, PIECE if piece < PIECES else PASS
-            loaded = wide_pool.tile(
-                [P, PACK, width], F32, name="w_loaded%d_%d" % (which, piece), offset=4 * PACK * (2 * first + which * width)
-            )
+            first, width = piece * PIECE, widths[piece]
+            kib = LOADED + 4 * PACK * (2 * first + (1 - which) * width) // 1024
+            loaded[which, piece] = placed("w_loaded%d_%d" % (which, piece), [P, PACK, width], F32, kib)
             nc.sync.dma_start(
-                out=loaded[:], in_=(w1, w3)[which][:, first : first + width].rearrange("(p j) c -> p j c", j=PACK)
+                out=loaded[which, piece][:],
+                in_=(w1, w3)[which][:, first : first + width].rearrange("(p j) c -> p j c", j=PACK),
             )
-            return loaded
 
         def load_page(i):
             rows = page0[i * P : (i + 1) * P, :] if i < PACK else dealt_in[i - PACK]
             nc.sync.dma_start(out=pages[i][:], in_=rows)
 
+        rights = {}
+
         def load_dealt_gain(t):
+            rights[t] = placed("right%d" % t, [P, 2 * S], F32, TABLE + 8 * t)
             for q in (0, 2, 1, 3):
-                nc.sync.dma_start(out=dealt_gains[t][QUADRANT * q : QUADRANT * (q + 1), :], in_=gain_rows[:, t, :])
-
-        def woven_tile(name, first, parts, dtype=BF16, width=PACK * BANK):
-            return weave_pool.tile([P, parts * width], dtype, name=name, align_bytes=64, offset=2 * PACK * BANK * first)
-
-        def round_weight(engine_copy, source, target):
-            engine_copy(
-                out=target.rearrange("p (c i j) -> p c j i", i=4, j=PACK), in_=source.rearrange("p j (c i) -> p c j i", i=4)
-            )
-
-        def quantize_weight(key, codes, woven, first, count):
-            if key not in w_codes:
-                w_codes[key] = codes
-                w_scales[key] = held("w_scales%d" % key, [P, codes.shape[1]], U8, "dealt_gain0" if key == PIECES else None)
-            nc.vector.quantize_mx(
-                out=codes[:, first : first + count].bitcast(FP8X4), scales=w_scales[key][:, first : first + count],
-                in_=woven[:, first * PACK : (first + count) * PACK],
-            )
-
-        def entries(offsets, first, count):
-            return offsets[:, first // PER_COLUMN : (first + count) // PER_COLUMN]
+                nc.sync.dma_start(out=rights[t][QUADRANT * q : QUADRANT * (q + 1), :S], in_=gain_rows[:, t, :])
 
         def pick_columns(picked, table, h):
-            nc.vector.tensor_copy(out=picked[h][:], in_=table[:].indirect(entries(pick, h * BANK, BANK)))
+            columns = BANK // PER_COLUMN
+            nc.vector.tensor_copy(out=picked[h][:], in_=table[:].indirect(pick[:, h * columns : (h + 1) * columns]))
 
-        nc.vector.memset(table_scales[:].bitcast(I32), 0)
-        nc.vector.memset(w2_scale_tile[:].bitcast(I32), 0)
-        nc.vector.memset(w4_scale_tile[:].bitcast(I32), 0)
-        make_identity(nc, identity[:])
+        woven_w = [placed("woven_w%d" % n, [P, 2 * PACK * width], BF16, (WOVEN_W, SPARE + 4, WOVEN_W + 8)[n]) for n, width in enumerate(widths)]
+        w_codes = [placed("w_codes%d" % n, [P, 2 * width], U32, CODES_W + 2 * n) for n, width in enumerate(widths)]
 
-        nc.sync.dma_start(pick[:], offs)
-        nc.sync.dma_start(out=w2_codes[:].bitcast(I32), in_=w2_words[0].bitcast(I32))
-        load_scale_rows(table_scales, tab_scales)
-        nc.sync.dma_start(out=table_words[:].bitcast(I32), in_=tab_words[0].rearrange("p t i -> p (t i)").bitcast(I32))
-        load_scale_rows(w2_scale_tile, w2_scales)
-        loaded = {(0, 0): load_weight(0, 0), (1, 0): load_weight(1, 0)}
-        for h in range(HALVES):
-            nc.sync.dma_start(out=gain_whole[:, h * BANK : (h + 1) * BANK], in_=wgs[:, h * BANK : (h + 1) * BANK])
-        nc.sync.dma_start(place[:], offs2)
-        load_page(0)
-        loaded[0, 1] = load_weight(0, 1)
-        loaded[1, 1] = load_weight(1, 1)
-        loaded[0, 2] = load_weight(0, 2)
-        load_page(1)
-        loaded[1, 2] = load_weight(1, 2)
-        load_dealt_gain(0)
-        load_page(2)
-        for t in range(1, PACK):
-            load_page(t + 2)
-            load_dealt_gain(t)
-        for g in range(GROUPS):
-            nc.sync.dma_start(
-                out=w4_codes[:, g * N : (g + 1) * N].bitcast(I32),
-                in_=w4_words[g].rearrange("p c i -> p (c i)").bitcast(I32),
+        def round_weight(which, piece):
+            width = PACK * widths[piece]
+            target = woven_w[piece][:, which * width : (which + 1) * width]
+            source = loaded[which, piece][:]
+            if piece < 2:
+                nc.scalar.copy(
+                    out=target.rearrange("p (c i j) -> p c j i", i=4, j=PACK), in_=source.rearrange("p j (c i) -> p c j i", i=4)
+                )
+            else:
+                nc.scalar.copy(
+                    out=target.rearrange("p (t m j) -> p m j t", t=PACK, j=PACK), in_=source.rearrange("p j (m t) -> p m j t", t=PACK)
+                )
+
+        def quantize_weight(piece, first, count):
+            nc.vector.quantize_mx(
+                out=w_codes[piece][:, first : first + count].bitcast(FP8X4), scales=w_scales[piece][:, first : first + count],
+                in_=woven_w[piece][:, first * PACK : (first + count) * PACK],
             )
-        load_page(LAST - 1)
-        load_scale_rows(w4_scale_tile, w4_scales)
-        load_page(LAST)
-        with nc.allow_non_contiguous_dma(reason="one bias value for each partition"):
-            nc.sync.dma_start(out=bias[:], in_=b4.rearrange("(c p) -> p c", p=P))
 
-        pick_columns(picked_scales, table_scales, 0)
-        pick_columns(picked_scales, table_scales, 1)
-        pick_columns(picked_words, table_words, 0)
-        pick_columns(picked_words, table_words, 1)
-
-        woven = placed("woven_piece0", [P, PACK * BANK], BF16, 0)
-        codes = held("w_codes0", [P, 2 * PIECE], U32)
-        for which in range(2):
-            split = SCALAR_COLUMNS[which]
-            for engine_copy, cols in ((nc.scalar.copy, slice(0, split)), (nc.vector.tensor_copy, slice(split, PIECE))):
-                if cols.start < cols.stop:
-                    target = woven[:, (which * PIECE + cols.start) * PACK : (which * PIECE + cols.stop) * PACK]
-                    round_weight(engine_copy, loaded[which, 0][:, :, cols], target)
-            quantize_weight(0, codes, woven, which * PIECE, PIECE)
-
-        def product(bank, i, h, name):
+        def product(i, cols, name):
             if name == "b":
                 codes, scales = (w2_codes, w2_scale_tile) if i < PACK else (w2_dealt_codes, w2_dealt_scales)
                 first = (i % PACK) * P
                 codes, scales = codes[:, 2 * first : 2 * (first + P)].bitcast(FP4X4), scales[:, first : first + P]
             else:
-                piece, first, width = (i // 2, (i % 2) * P, PIECE) if i < PACK else (PIECES, (i - PACK) * P, PASS)
+                piece, first = (i // 2, (i % 2) * P) if i < PACK else (2, (i - PACK) * P)
                 if name == "c":
-                    first = first + width
+                    first = first + widths[piece]
                 codes, scales = w_codes[piece][:, first : first + P].bitcast(FP8X4), w_scales[piece][:, first : first + P]
+            h = cols.start // BANK
+            within = slice(cols.start - h * BANK, cols.stop - h * BANK)
+            sums = next_bank()[:, : cols.stop - cols.start]
             nc.tensor.matmul_mx(
-                out=bank[:], lhsT=codes, lhsT_scale=scales,
-                rhs=picked_words[h][:].bitcast(FP8X4), rhs_scale=picked_scales[h][:], start=True, stop=True,
+                out=sums, lhsT=codes, lhsT_scale=scales,
+                rhs=picked_words[h][:, within].bitcast(FP8X4), rhs_scale=picked_scales[h][:, within], start=True, stop=True,
             )
-            return bank
+            return sums
 
-        def half(h):
-            return slice(h * BANK, (h + 1) * BANK)
+        def copy_product(target, i, name, first=0):
+            for cols in (slice(first, BANK), half(1)):
+                nc.scalar.copy(out=target[:, cols], in_=product(i, cols, name))
 
-        def first_values():
-            values[0] = placed("values0", [P, S], F32, 22)
-            for name in "bac":
-                for h in range(HALVES):
-                    bank = product(banks[name][h], 0, h, name)
-                    other = gain_whole if name == "b" else values[0]
-                    nc.vector.tensor_tensor(out=values[0][:, half(h)], in0=bank[:], in1=other[:, half(h)], op=MULT)
+        def multiply(target, left, right):
+            nc.gpsimd.tensor_tensor(out=target, in0=left, in1=right, op=MULT)
 
-        def copy_product(target, i, name, bank_name):
-            for h in range(HALVES):
-                nc.scalar.copy(out=target[:, half(h)], in_=product(banks[bank_name][h], i, h, name)[:])
+        def entries(cols):
+            return place[:, cols.start // PER_COLUMN : cols.stop // PER_COLUMN]
 
-        def begin_values(i, target):
-            values[i] = target
-            b_tile = b_tiles[i in (1, 3, 5)]
-            gain = gain_whole if i < PACK else dealt_gains[i - PACK]
-            if i == ON_VECTOR:
-                for h in range(HALVES):
-                    bank = product(banks["b"][h], i, h, "b")
-                    nc.vector.tensor_tensor(out=b_tile[:, half(h)], in0=bank[:], in1=gain[:, half(h)], op=MULT)
-            else:
-                if i not in (3, 5):
-                    copy_product(b_tile, i, "b", "w" if i == 1 else "b")
-                nc.gpsimd.tensor_tensor(out=target[:], in0=b_tile[:], in1=gain[:], op=MULT)
-
-        def multiply_by(i, name, target, moved=None):
-            copy_product(target, i, name, {"a": "w", "c": "b"}[name] if i == 1 else name)
-            so_far = b_tiles[i in (1, 3, 5)] if i == ON_VECTOR and name == "a" else values[i]
-            values[i] = values[i] if moved is None else moved
-            nc.gpsimd.tensor_tensor(out=values[i][:], in0=so_far[:], in1=target[:], op=MULT)
-
-        def finish_values(i, a, c, moved=None):
-            multiply_by(i, "a", a, moved)
-            multiply_by(i, "c", c)
-
-        def round_dealt(woven, which):
-            width = PACK * PASS
-            nc.scalar.copy(
-                out=woven[:, which * width : (which + 1) * width].rearrange("p (t m j) -> p m j t", t=PACK, j=PACK),
-                in_=loaded[which, PIECES][:].rearrange("p j (m t) -> p m j t", t=PACK),
-            )
-
-        def deal_w2():
-            nc.vector.tensor_copy(
-                out=w2_dealt_codes[:].bitcast(U16).rearrange("p (t m) -> p m t", t=PACK),
-                in_=w2_codes[:, 2 * PASS :].bitcast(U16).rearrange("p (m t) -> p m t", t=PACK),
-            )
-            nc.vector.tensor_copy(
-                out=w2_dealt_scales[:].rearrange("p (t m) -> p m t", t=PACK),
-                in_=w2_scale_tile[:, PASS:].rearrange("p (m t) -> p m t", t=PACK),
-            )
-
-        def place_values(i):
-            if i == LAST:
-                nc.vector.tensor_tensor(out=pages[i][:].indirect(place[:]), in0=values[i][:], in1=last_c[:], op=MULT)
+        def place_values(i, lead=None):
+            if lead is not None:
+                nc.vector.tensor_copy(out=pages[i][:].indirect(entries(slice(0, LEAD))), in_=lead[:])
+                nc.vector.tensor_copy(out=pages[i][:].indirect(entries(slice(LEAD, S))), in_=values[i][:, LEAD:])
+            elif i == LAST:
+                nc.vector.tensor_tensor(out=pages[i][:].indirect(place[:]), in0=values[i][:, :S], in1=values[i][:, S:], op=MULT)
             else:
                 nc.vector.tensor_copy(out=pages[i][:].indirect(place[:]), in_=values[i][:])
             rows = out_1[i * P : (i + 1) * P, :] if i < PACK else dealt_out[i - PACK]
             nc.sync.dma_start(out=rows, in_=pages[i][:])
 
-        def chunk_columns(chunk):
-            return slice(chunk * BANK, (chunk + 1) * BANK)
-
-        def turn_page(i, chunk, bank):
-            for block in range(BLOCKS):
-                first = chunk * BANK + block * P
-                nc.tensor.transpose(bank[:, block * P : (block + 1) * P], pages[i][:, first : first + P], identity[:])
-            nc.scalar.copy(
-                out=turned[chunk][:].rearrange("p (b u q w e) -> p b u q w e", b=BLOCKS, u=2, q=QUADRANTS, e=2)[:, :, :, i % PACK],
-                in_=bank[:].rearrange("p (b w u e) -> p b u w e", b=BLOCKS, u=2, e=2),
-            )
+        def turn_tile(i):
+            for chunk in range(CHUNKS):
+                bank = next_bank()
+                for block in range(BLOCKS):
+                    first = chunk * BANK + block * P
+                    nc.tensor.transpose(bank[:, block * P : (block + 1) * P], pages[i][:, first : first + P], identity[:])
+                nc.scalar.copy(
+                    out=turned[chunk][:].rearrange("p (b u q w e) -> p b u q w e", b=BLOCKS, u=2, q=QUADRANTS, e=2)[:, :, :, i],
+                    in_=bank[:].rearrange("p (b w u e) -> p b u w e", b=BLOCKS, u=2, e=2),
+                )
 
         def turn_back(chunk, target):
             words = turned[chunk][:].bitcast(F32)
             target = target.bitcast(F32)
             for n in range(2):
+                bank = next_bank()
                 for m in range(4):
                     first = (4 * n + m) * P
-                    nc.tensor.transpose(banks["w"][n][:, m * P : (m + 1) * P], words[:, first : first + P], identity[:])
+                    nc.tensor.transpose(bank[:, m * P : (m + 1) * P], words[:, first : first + P], identity[:])
                 nc.scalar.copy(
                     out=target[:, n * BANK : (n + 1) * BANK].rearrange("p (b m u) -> p b m u", b=2, u=2),
-                    in_=banks["w"][n][:].rearrange("p (b u m) -> p b m u", b=2, u=2),
+                    in_=bank[:].rearrange("p (b u m) -> p b m u", b=2, u=2),
                 )
 
-        def round_page(i, n):
-            u, e = divmod(i - PACK, 2)
-            nc.scalar.copy(out=paired[n][:].rearrange("p (u m e) -> p u m e", u=2, e=2)[:, u, :, e], in_=pages[i][:, spans[n]])
+        def chunk_columns(chunk):
+            return slice(chunk * BANK, (chunk + 1) * BANK)
 
-        def weave_and_quantize(n):
-            woven = weave_pool.tile(
-                [P, PACK * WIDTHS[n]], BF16, name="woven_span%d" % n, align_bytes=64, offset=2 * PACK * spans[n].start
-            )
+        def round_page(i, chunk):
+            u, e = divmod(i - PACK, 2)
+            nc.scalar.copy(out=planes[chunk][:].rearrange("p (u m e) -> p u m e", u=2, e=2)[:, u, :, e], in_=pages[i][:, chunk_columns(chunk)])
+
+        def round_tile(i):
+            for chunk in range(CHUNKS):
+                round_page(i, chunk)
+
+        def weave_and_quantize(chunk):
+            woven = placed("woven_chunk%d" % chunk, [P, PACK * BANK], BF16, WOVEN_PAGE + 4 * chunk)
             nc.vector.tensor_copy(
                 out=woven[:].bitcast(F32).rearrange("p (c i u) -> p c u i", i=4, u=2),
-                in_=paired[n][:].bitcast(F32).rearrange("p (u c i) -> p c u i", i=4, u=2),
+                in_=planes[chunk][:].bitcast(F32).rearrange("p (u c i) -> p c u i", i=4, u=2),
             )
-            quantize_page(1, spans[n], woven[:])
+            quantize_page(1, chunk_columns(chunk), woven[:])
+
+        page_codes = {}
 
         def codes_of(g, cols):
             if g == 0:
                 first = cols.start // S * S
-                return page_codes[0][cols.start // S][:, cols.start - first : cols.stop - first]
+                return page_codes[0, cols.start // S][:, cols.start - first : cols.stop - first]
             return page_codes[g][:, cols]
 
         def quantize_page(g, cols, source):
@@ -333,146 +254,196 @@ def tile_list_clue_memory_triple_kernel(
         def read_page(g, bank, n, cols):
             w4_cols = slice(g * N + n * P, g * N + (n + 1) * P)
             nc.tensor.matmul_mx(
-                out=bank[:, : cols.stop - cols.start],
+                out=bank[:],
                 lhsT=w4_codes[:, w4_cols].bitcast(FP8X4), lhsT_scale=w4_scale_tile[:, w4_cols],
                 rhs=codes_of(g, cols).bitcast(FP8X4), rhs_scale=page_scales[g][:, cols],
                 start=(g == 0), stop=(g == GROUPS - 1),
             )
 
         def add_bias(target, bank, n, on_vector):
-            sums = bank[:, : target.shape[1]]
             if on_vector:
-                nc.vector.tensor_scalar(out=target, in0=sums, scalar1=bias[:, n : n + 1], scalar2=None, op0=ADD)
+                nc.vector.tensor_scalar(out=target, in0=bank[:], scalar1=bias[:, n : n + 1], scalar2=None, op0=ADD)
             else:
-                nc.scalar.activation(out=target, in_=sums, func=IDENTITY, bias=bias[:, n : n + 1])
+                nc.scalar.activation(out=target, in_=bank[:], func=IDENTITY, bias=bias[:, n : n + 1])
 
         def features_tile(n, cols):
             width = cols.stop - cols.start
-            return wide_pool.tile(
-                [P, width], F32, name="features%d_%d" % (n, cols.start), offset=4 * (N_TILES * cols.start + n * width)
-            )
+            return placed("features%d_%d" % (n, cols.start), [P, width], F32, TABLE + 4 * (N_TILES * cols.start + n * width) // 1024)
 
-        def round_tile(i):
-            for n in range(len(WIDTHS)):
-                round_page(i, n)
+        nc.gpsimd.memset(table_scales[:].bitcast(I32), 0)
+        nc.vector.memset(w2_scale_tile[:].bitcast(I32), 0)
+        nc.vector.memset(w4_scale_tile[:].bitcast(I32), 0)
+        make_identity(nc, identity[:])
 
-        def turn_tile(i):
-            for chunk in range(CHUNKS):
-                turn_page(i, chunk, banks["c"][chunk % 2])
+        nc.sync.dma_start(pick[:], offs)
+        load_weight(0, 0)
+        load_scale_rows(table_scales, tab_scales)
+        nc.sync.dma_start(out=table_words[:].bitcast(I32), in_=tab_words[0].rearrange("p t i -> p (t i)").bitcast(I32))
+        load_scale_rows(w2_scale_tile, w2_scales)
+        load_weight(1, 0)
+        for h in range(HALVES):
+            nc.sync.dma_start(out=gain[:, half(h)], in_=wgs[:, half(h)])
+        nc.sync.dma_start(out=w2_codes[:].bitcast(I32), in_=w2_words[0].bitcast(I32))
+        nc.sync.dma_start(place[:], offs2)
+        load_page(0)
+        load_weight(0, 1)
+        load_weight(1, 1)
+        load_weight(0, 2)
+        load_page(1)
+        load_weight(1, 2)
 
-        first_values()
-        deal_w2()
-        b_tiles = [wide_pool.tile([P, S], F32, name="b%d" % n, offset=4 * PACK * PIECE * n) for n in range(2)]
-        begin_values(1, placed("values1", [P, S], F32, 0))
-        x1 = placed("x1", [P, S], F32, 10)
-        finish_values(1, a_tile, x1)
-        values[2] = x1
-        b_half = placed("b_half", [P, BANK], F32, 8)
-        nc.scalar.copy(out=b_half[:], in_=product(banks["b"][0], 2, 0, "b")[:])
-        nc.gpsimd.tensor_tensor(out=x1[:, half(0)], in0=b_half[:], in1=gain_whole[:, half(0)], op=MULT)
-        woven = placed("woven_piece1", [P, PACK * BANK], BF16, 4)
+        pick_columns(picked_scales, table_scales, 0)
+        pick_columns(picked_scales, table_scales, 1)
+        pick_columns(picked_words, table_words, 0)
+        pick_columns(picked_words, table_words, 1)
+        nc.gpsimd.tensor_copy(
+            out=w2_dealt_scales[:].rearrange("p (t m) -> p t m", t=PACK),
+            in_=w2_scale_tile[:, PASS:].rearrange("p (m t) -> p t m", t=PACK),
+        )
         for which in range(2):
-            round_weight(nc.scalar.copy, loaded[which, 1][:], woven[:, which * PIECE * PACK : (which + 1) * PIECE * PACK])
-        copy_product(b_tiles[1], 3, "b", "b")
-        woven_dealt = woven_tile("woven_dealt", 1, 2)
-        round_dealt(woven_dealt, 0)
+            round_weight(which, 0)
+            quantize_weight(0, which * PIECE, PIECE)
+
+        values[0] = placed("values0", [P, S], F32, LOADED + 2)
+        a1 = placed("a1", [P, S], F32, LOADED - 2)
+        for h in range(HALVES):
+            nc.vector.tensor_tensor(out=values[0][:, half(h)], in0=product(0, half(h), "a"), in1=gain[:, half(h)], op=MULT)
+            nc.scalar.copy(out=a1[:, half(h)], in_=product(1, half(h), "a"))
+        c1 = placed("c1", [P, S], F32, SPARE)
+        b1 = placed("b1", [P, S], F32, VALUES + 4)
+        for name in "cb":
+            for h in range(HALVES):
+                nc.vector.tensor_tensor(out=values[0][:, half(h)], in0=product(0, half(h), name), in1=values[0][:, half(h)], op=MULT)
+            copy_product(c1 if name == "c" else b1, 1, name)
+        values[1] = placed("values1", [P, S], F32, WOVEN_W)
+        for h in range(HALVES):
+            multiply(values[1][:, half(h)], a1[:, half(h)], gain[:, half(h)])
+        multiply(values[1][:], values[1][:], c1[:])
+        multiply(values[1][:], values[1][:], b1[:])
+        b2 = placed("b2", [P, S], F32, PLANES + 4)
+        copy_product(b2, 2, "b")
+        values[2] = placed("values2", [P, S], F32, VALUES + 4)
+        multiply(values[2][:], b2[:], gain[:])
+        for which in range(2):
+            round_weight(which, 1)
+        b3 = placed("b3", [P, S], F32, LEFT)
+        copy_product(b3, 3, "b")
+        w2_dealt_codes = placed("w2_dealt_codes", [P, 2 * PASS], U8, SPARE)
+        nc.scalar.copy(
+            out=w2_dealt_codes[:].bitcast(U16).rearrange("p (t m) -> p t m", t=PACK),
+            in_=w2_codes[:, 2 * PASS :].bitcast(U16).rearrange("p (m t) -> p t m", t=PACK),
+        )
+        round_weight(0, 2)
+        load_dealt_gain(0)
+        load_page(2)
+        load_page(3)
+        load_dealt_gain(1)
+        load_page(4)
+        load_dealt_gain(2)
+        load_page(5)
+        load_dealt_gain(3)
+        for g in range(GROUPS):
+            nc.sync.dma_start(
+                out=w4_codes[:, g * N : (g + 1) * N].bitcast(I32),
+                in_=w4_words[g].rearrange("p c i -> p (c i)").bitcast(I32),
+            )
+        load_page(LAST - 1)
+        load_scale_rows(w4_scale_tile, w4_scales)
+        load_page(LAST)
+        with nc.allow_non_contiguous_dma(reason="one bias value for each partition"):
+            nc.sync.dma_start(out=bias[:], in_=b4.rearrange("(c p) -> p c", p=P))
 
         place_values(0)
-        nc.vector.tensor_tensor(out=x1[:, half(1)], in0=product(banks["w"][1], 2, 1, "b")[:], in1=gain_whole[:, half(1)], op=MULT)
-        quantize_weight(1, held("w_codes1", [P, 2 * PIECE], U32), woven, 0, 2 * PIECE)
-        x2 = placed("x2", [P, S], F32, 6)
-        x3 = placed("x3", [P, S], F32, 14)
-        begin_values(3, x2)
-        finish_values(2, a_tile, x3)
-        round_dealt(woven_dealt, 1)
+        quantize_weight(1, 0, 2 * PIECE)
+        begun3 = placed("begun3", [P, S], F32, SPARE + 5)
+        multiply(begun3[:], b3[:], gain[:])
+        a2, c2 = placed("a2", [P, S], F32, PLANES), placed("c2", [P, S], F32, PLANES + 4)
+        copy_product(a2, 2, "a")
+        copy_product(c2, 2, "c")
+        multiply(values[2][:], values[2][:], a2[:])
+        multiply(values[2][:], values[2][:], c2[:])
+        round_weight(1, 2)
+        a3, c3 = placed("a3", [P, S], F32, PLANES + 8), placed("c3", [P, S], F32, PLANES + 12)
+        copy_product(a3, 3, "a")
+        copy_product(c3, 3, "c")
 
         place_values(1)
-        a_odd = wide_pool.tile([P, S], F32, name="a_odd", offset=4 * PACK * (2 * PASS + PASS))
-        x0 = wide_pool.tile([P, S], F32, name="x0", offset=4 * PACK * (2 * PASS + PASS) + 4 * S)
-        begin_values(4, x0)
-        quantize_weight(2, placed("w_codes2", [P, 2 * PASS], U32, 0), woven_dealt, 0, 2 * PASS)
-        finish_values(3, a_odd, x0, woven_tile("values3", 1, 1, F32, S))
+        quantize_weight(2, 0, 2 * PASS)
+        values[3] = placed("values3", [P, S], F32, WOVEN_W + 8)
+        multiply(values[3][:], begun3[:], a3[:])
+        multiply(values[3][:], values[3][:], c3[:])
+
+        def merged_values(i):
+            left = placed("left%d" % i, [P, 2 * S], F32, LEFT - 8 * (i % 2))
+            right = rights[i - PACK]
+            copy_product(left[:, :S], i, "b")
+            copy_product(left[:, S:], i, "a")
+            copy_product(right[:, S:], i, "c")
+            pair = placed("pair%d" % i, [P, 2 * S], F32, PAIR)
+            multiply(pair[:], left[:], right[:])
+            values[i] = pair
+            if i < LAST:
+                values[i] = placed("values%d" % i, [P, S], F32, VALUES + 4 * (i % 3))
+                multiply(values[i][:], pair[:, :S], pair[:, S:])
+
+        merged_values(4)
         turn_tile(0)
-        finish_values(4, a_tile, x3)
-        pair = placed("pair", [P, 2 * S], F32, 14)
-
-        def merged_values(i, left, target):
-            values[i] = target
-            right = gain_tiles[i - PACK]
-            copy_product(left[:, :S], i, "b", "b")
-            copy_product(left[:, S:], i, "a", "a")
-            copy_product(right[:, S:], i, "c", "c")
-            nc.gpsimd.tensor_tensor(out=pair[:], in0=left[:], in1=right[:], op=MULT)
-            nc.gpsimd.tensor_tensor(out=target[:], in0=pair[:, :S], in1=pair[:, S:], op=MULT)
-
-        merged_values(5, held("left5", [P, 2 * S], F32, "table_words"), x2)
-        turn_tile(1)
-
         place_values(2)
-        merged_values(6, held("left6", [P, 2 * S], F32), x1)
-        turn_tile(2)
-
+        merged_values(5)
+        turn_tile(1)
         place_values(3)
-        begin_values(7, placed("values7", [P, S], F32, 14))
-        multiply_by(7, "a", a_odd)
-        turn_tile(3)
-
+        merged_values(6)
+        turn_tile(2)
         place_values(4)
-        last_c = x0
-        copy_product(last_c, LAST, "c", "c")
-        woven = [woven_tile("woven_group%d" % n, 2 * n, 2) for n in range(2)]
+        merged_values(7)
+        turn_tile(3)
+        woven = [placed("woven_group%d" % n, [P, 2 * PACK * BANK], BF16, WOVEN_PAGE + 8 * n) for n in range(2)]
+        planes = [placed("planes%d" % c, [P, PACK * BANK], BF16, PLANES + 4 * c) for c in range(CHUNKS)]
         for chunk in range(CHUNKS):
             turn_back(chunk, woven[chunk // 2][:, (chunk % 2) * PACK * BANK : (chunk % 2 + 1) * PACK * BANK])
-        paired = [
-            turn_pool.tile([P, PACK * width], BF16, name="paired%d" % n, align_bytes=64, offset=2 * PACK * spans[n].start)
-            for n, width in enumerate(WIDTHS)
-        ]
         round_tile(4)
-
         place_values(5)
         round_tile(5)
-
         place_values(6)
-        page_codes[0] = [placed("page_codes0a", [P, S], U32, 10)]
+        page_codes[0, 0] = placed("page_codes0a", [P, S], U32, VALUES)
         quantize_page(0, slice(0, S), woven[0][:])
         store_page_codes(0, slice(0, S))
         round_tile(6)
 
-        sum_banks = banks["a"] + banks["b"] + banks["c"] + banks["w"]
-        page_codes[1] = placed("page_codes1", [P, T2], U32, 22)
-        for span in range(OPENED):
+        page_codes[1] = placed("page_codes1", [P, T2], U32, WOVEN_W)
+        for chunk in range(OPENED):
             for n in range(N_TILES):
-                read_page(0, sum_banks[span * N_TILES + n], n, spans[span])
+                read_page(0, banks[chunk * N_TILES + n], n, chunk_columns(chunk))
         place_values(LAST)
-        page_codes[0].append(placed("page_codes0b", [P, S], U32, 14))
+        page_codes[0, 1] = placed("page_codes0b", [P, S], U32, PAIR)
         quantize_page(0, slice(S, T2), woven[1][:])
         store_page_codes(0, slice(S, T2))
         store_page_scales(0)
         round_page(LAST, 0)
         round_page(LAST, 1)
         weave_and_quantize(0)
-        store_page_codes(1, spans[0])
+        store_page_codes(1, chunk_columns(0))
         for n in range(N_TILES):
-            read_page(1, sum_banks[n], n, spans[0])
-            features = features_tile(n, spans[0])
-            add_bias(features[:], sum_banks[n], n, False)
-            nc.sync.dma_start(out=out_0[n * P : (n + 1) * P, spans[0]], in_=features[:])
-        rest = slice(spans[1].start, T2)
-        for span in range(1, CHUNKS):
-            if span + 1 < CHUNKS:
-                round_page(LAST, span + 1)
-            weave_and_quantize(span)
+            read_page(1, banks[n], n, chunk_columns(0))
+            features = features_tile(n, chunk_columns(0))
+            add_bias(features[:], banks[n], n, False)
+            nc.sync.dma_start(out=out_0[n * P : (n + 1) * P, chunk_columns(0)], in_=features[:])
+        rest = slice(BANK, T2)
+        for chunk in range(1, CHUNKS):
+            if chunk + 1 < CHUNKS:
+                round_page(LAST, chunk + 1)
+            weave_and_quantize(chunk)
         store_page_codes(1, rest)
         store_page_scales(1)
         for n in range(N_TILES):
             features = features_tile(n, rest)
-            for span in range(1, CHUNKS):
-                if span < OPENED:
-                    bank = sum_banks[N_TILES + n]
+            for chunk in range(1, CHUNKS):
+                if chunk < OPENED:
+                    bank = banks[N_TILES + n]
                 else:
-                    bank = sum_banks[(2 * n + span - OPENED) % N_TILES]
-                    read_page(0, bank, n, spans[span])
-                read_page(1, bank, n, spans[span])
-                target = features[:, spans[span].start - rest.start : spans[span].stop - rest.start]
-                add_bias(target, bank, n, span == CHUNKS - 1 or (span == OPENED and n % 2 == 1))
+                    bank = banks[(2 * n + chunk - OPENED) % N_TILES]
+                    read_page(0, bank, n, chunk_columns(chunk))
+                read_page(1, bank, n, chunk_columns(chunk))
+                target = features[:, chunk * BANK - rest.start : (chunk + 1) * BANK - rest.start]
+                add_bias(target, bank, n, chunk == CHUNKS - 1)
             nc.sync.dma_start(out=out_0[n * P : (n + 1) * P, rest], in_=features[:])

@@ -296,9 +296,9 @@ def tile_list_clue_memory_triple_kernel(
         pick_columns(picked_scales, table_scales, 1)
         pick_columns(picked_words, table_words, 0)
         pick_columns(picked_words, table_words, 1)
-        nc.gpsimd.tensor_copy(
-            out=w2_dealt_scales[:].rearrange("p (t m) -> p t m", t=PACK),
-            in_=w2_scale_tile[:, PASS:].rearrange("p (m t) -> p t m", t=PACK),
+        nc.vector.tensor_copy(
+            out=w2_dealt_scales[:].rearrange("p (t m) -> p m t", t=PACK),
+            in_=w2_scale_tile[:, PASS:].rearrange("p (m t) -> p m t", t=PACK),
         )
         for which in range(2):
             round_weight(which, 0)

@@ -36,6 +36,7 @@ PER_COLUMN = 16
 PIECE = 2 * P
 BANKS = 8
 LEAD = 256
+SHARE = 256
 OPENED = 2
 
 
@@ -64,7 +65,7 @@ def tile_list_clue_memory_triple_kernel(
         pick = keep.tile([P, S // PER_COLUMN], U16, name="pick")
         place = keep.tile([P, S // PER_COLUMN], U16, name="place")
         picked_words = [held("picked_words%d" % h, [P, BANK], U32) for h in range(HALVES)]
-        picked_scales = [held("picked_scales%d" % h, [P, BANK], U8) for h in range(HALVES)]
+        picked_scales = held("picked_scales", [P, S], U8)
         w2_codes = held("w2_codes", [P, 2 * H], U8)
         w2_scale_tile = held("w2_scale_tile", [P, H], U8)
         w2_dealt_scales = held("w2_dealt_scales", [P, PASS], U8)
@@ -74,7 +75,7 @@ def tile_list_clue_memory_triple_kernel(
         gain = held("gain", [P, S], F32)
         identity = held("identity", [P, P], F32)
         pages = [held("page%d" % i, [P, T2], F32) for i in range(TILES)]
-        page_scales = [held("page_scales%d" % g, [P, T2], U8) for g in range(GROUPS)]
+        page_scales = {(g, n): held("page_scales%d_%d" % (g, n), [P, S], U8) for g in range(GROUPS) for n in range(2)}
         widths = (PIECE, PIECE, PASS)
         w_scales = [held("w_scales%d" % n, [P, 2 * width], U8) for n, width in enumerate(widths)]
         turned = [held("turned%d" % c, [P, PACK * BANK], BF16) for c in range(CHUNKS)]
@@ -119,11 +120,7 @@ def tile_list_clue_memory_triple_kernel(
             for q in (0, 2, 1, 3):
                 nc.sync.dma_start(out=rights[t][QUADRANT * q : QUADRANT * (q + 1), :S], in_=gain_rows[:, t, :])
 
-        def pick_columns(picked, table, h):
-            columns = BANK // PER_COLUMN
-            nc.vector.tensor_copy(out=picked[h][:], in_=table[:].indirect(pick[:, h * columns : (h + 1) * columns]))
-
-        woven_w = [placed("woven_w%d" % n, [P, 2 * PACK * width], BF16, (WOVEN_W, SPARE + 4, WOVEN_W + 8)[n]) for n, width in enumerate(widths)]
+        woven_w = [placed("woven_w%d" % n, [P, 2 * PACK * width], BF16, (WOVEN_W, SPARE, WOVEN_W + 8)[n]) for n, width in enumerate(widths)]
         w_codes = [placed("w_codes%d" % n, [P, 2 * width], U32, CODES_W + 2 * n) for n, width in enumerate(widths)]
 
         def round_weight(which, piece):
@@ -160,7 +157,7 @@ def tile_list_clue_memory_triple_kernel(
             sums = next_bank()[:, : cols.stop - cols.start]
             nc.tensor.matmul_mx(
                 out=sums, lhsT=codes, lhsT_scale=scales,
-                rhs=picked_words[h][:, within].bitcast(FP8X4), rhs_scale=picked_scales[h][:, within], start=True, stop=True,
+                rhs=picked_words[h][:, within].bitcast(FP8X4), rhs_scale=picked_scales[:, cols], start=True, stop=True,
             )
             return sums
 
@@ -236,15 +233,23 @@ def tile_list_clue_memory_triple_kernel(
                 return page_codes[0, cols.start // S][:, cols.start - first : cols.stop - first]
             return page_codes[g][:, cols]
 
-        def quantize_page(g, cols, source):
-            nc.vector.quantize_mx(out=codes_of(g, cols).bitcast(FP8X4), scales=page_scales[g][:, cols], in_=source)
+        def first_row(g, n):
+            return SCALE_ROWS * g * (n + 1)
 
-        def store_page_scales(g):
+        def scales_of(g, cols):
+            n = cols.start // S
+            return page_scales[g, n][first_row(g, n) :, cols.start - n * S : cols.stop - n * S]
+
+        def quantize_page(g, cols, source):
+            nc.vector.quantize_mx(out=codes_of(g, cols).bitcast(FP8X4), scales=scales_of(g, cols), in_=source)
+
+        def store_page_scales(g, halves):
             for r in range(SCALE_ROWS):
-                nc.sync.dma_start(
-                    out=out_3[g].bitcast(I32).rearrange("(q r) m -> r q m", r=SCALE_ROWS)[r],
-                    in_=page_scales[g][r:P:QUADRANT, :].bitcast(I32),
-                )
+                for n in halves:
+                    nc.sync.dma_start(
+                        out=out_3[g][:, n * S : (n + 1) * S].bitcast(I32).rearrange("(q r) m -> r q m", r=SCALE_ROWS)[r],
+                        in_=page_scales[g, n][first_row(g, n) + r : P : QUADRANT, :].bitcast(I32),
+                    )
 
         def store_page_codes(g, cols):
             nc.sync.dma_start(
@@ -256,7 +261,7 @@ def tile_list_clue_memory_triple_kernel(
             nc.tensor.matmul_mx(
                 out=bank[:],
                 lhsT=w4_codes[:, w4_cols].bitcast(FP8X4), lhsT_scale=w4_scale_tile[:, w4_cols],
-                rhs=codes_of(g, cols).bitcast(FP8X4), rhs_scale=page_scales[g][:, cols],
+                rhs=codes_of(g, cols).bitcast(FP8X4), rhs_scale=scales_of(g, cols),
                 start=(g == 0), stop=(g == GROUPS - 1),
             )
 
@@ -292,10 +297,10 @@ def tile_list_clue_memory_triple_kernel(
         load_page(1)
         load_weight(1, 2)
 
-        pick_columns(picked_scales, table_scales, 0)
-        pick_columns(picked_scales, table_scales, 1)
-        pick_columns(picked_words, table_words, 0)
-        pick_columns(picked_words, table_words, 1)
+        nc.vector.tensor_copy(out=picked_scales[:], in_=table_scales[:].indirect(pick[:]))
+        for h in range(HALVES):
+            columns = BANK // PER_COLUMN
+            nc.vector.tensor_copy(out=picked_words[h][:], in_=table_words[:].indirect(pick[:, h * columns : (h + 1) * columns]))
         nc.vector.tensor_copy(
             out=w2_dealt_scales[:].rearrange("p (t m) -> p m t", t=PACK),
             in_=w2_scale_tile[:, PASS:].rearrange("p (m t) -> p m t", t=PACK),
@@ -309,7 +314,7 @@ def tile_list_clue_memory_triple_kernel(
         for h in range(HALVES):
             nc.vector.tensor_tensor(out=values[0][:, half(h)], in0=product(0, half(h), "a"), in1=gain[:, half(h)], op=MULT)
             nc.scalar.copy(out=a1[:, half(h)], in_=product(1, half(h), "a"))
-        c1 = placed("c1", [P, S], F32, SPARE)
+        c1 = placed("c1", [P, S], F32, WOVEN_W + 4)
         b1 = placed("b1", [P, S], F32, VALUES + 4)
         for name in "cb":
             for h in range(HALVES):
@@ -320,7 +325,7 @@ def tile_list_clue_memory_triple_kernel(
             multiply(values[1][:, half(h)], a1[:, half(h)], gain[:, half(h)])
         multiply(values[1][:], values[1][:], c1[:])
         multiply(values[1][:], values[1][:], b1[:])
-        b2 = placed("b2", [P, S], F32, PLANES + 4)
+        b2 = placed("b2", [P, S], F32, SPARE + 4)
         copy_product(b2, 2, "b")
         values[2] = placed("values2", [P, S], F32, VALUES + 4)
         multiply(values[2][:], b2[:], gain[:])
@@ -328,7 +333,7 @@ def tile_list_clue_memory_triple_kernel(
             round_weight(which, 1)
         b3 = placed("b3", [P, S], F32, LEFT)
         copy_product(b3, 3, "b")
-        w2_dealt_codes = placed("w2_dealt_codes", [P, 2 * PASS], U8, SPARE)
+        w2_dealt_codes = placed("w2_dealt_codes", [P, 2 * PASS], U8, WOVEN_W + 4)
         nc.scalar.copy(
             out=w2_dealt_codes[:].bitcast(U16).rearrange("p (t m) -> p t m", t=PACK),
             in_=w2_codes[:, 2 * PASS :].bitcast(U16).rearrange("p (m t) -> p t m", t=PACK),
@@ -355,19 +360,21 @@ def tile_list_clue_memory_triple_kernel(
 
         place_values(0)
         quantize_weight(1, 0, 2 * PIECE)
-        begun3 = placed("begun3", [P, S], F32, SPARE + 5)
+        begun3 = placed("begun3", [P, S], F32, SPARE + 2)
         multiply(begun3[:], b3[:], gain[:])
         a2, c2 = placed("a2", [P, S], F32, PLANES), placed("c2", [P, S], F32, PLANES + 4)
         copy_product(a2, 2, "a")
-        copy_product(c2, 2, "c")
+        for cols in (slice(SHARE, BANK), half(1)):
+            nc.scalar.copy(out=c2[:, cols], in_=product(2, cols, "c"))
         multiply(values[2][:], values[2][:], a2[:])
-        multiply(values[2][:], values[2][:], c2[:])
+        multiply(values[2][:, SHARE:], values[2][:, SHARE:], c2[:, SHARE:])
         round_weight(1, 2)
         a3, c3 = placed("a3", [P, S], F32, PLANES + 8), placed("c3", [P, S], F32, PLANES + 12)
         copy_product(a3, 3, "a")
         copy_product(c3, 3, "c")
 
         place_values(1)
+        nc.vector.tensor_tensor(out=values[2][:, :SHARE], in0=product(2, slice(0, SHARE), "c"), in1=values[2][:, :SHARE], op=MULT)
         quantize_weight(2, 0, 2 * PASS)
         values[3] = placed("values3", [P, S], F32, WOVEN_W + 8)
         multiply(values[3][:], begun3[:], a3[:])
@@ -408,6 +415,7 @@ def tile_list_clue_memory_triple_kernel(
         page_codes[0, 0] = placed("page_codes0a", [P, S], U32, VALUES)
         quantize_page(0, slice(0, S), woven[0][:])
         store_page_codes(0, slice(0, S))
+        store_page_scales(0, (0,))
         round_tile(6)
 
         page_codes[1] = placed("page_codes1", [P, T2], U32, WOVEN_W)
@@ -418,32 +426,31 @@ def tile_list_clue_memory_triple_kernel(
         page_codes[0, 1] = placed("page_codes0b", [P, S], U32, PAIR)
         quantize_page(0, slice(S, T2), woven[1][:])
         store_page_codes(0, slice(S, T2))
-        store_page_scales(0)
-        round_page(LAST, 0)
-        round_page(LAST, 1)
-        weave_and_quantize(0)
-        store_page_codes(1, chunk_columns(0))
+        store_page_scales(0, (1,))
+        round_tile(LAST)
+        for chunk in range(OPENED):
+            weave_and_quantize(chunk)
+        store_page_codes(1, slice(0, S))
         for n in range(N_TILES):
             read_page(1, banks[n], n, chunk_columns(0))
             features = features_tile(n, chunk_columns(0))
             add_bias(features[:], banks[n], n, False)
             nc.sync.dma_start(out=out_0[n * P : (n + 1) * P, chunk_columns(0)], in_=features[:])
+        store_page_scales(1, (0,))
         rest = slice(BANK, T2)
-        for chunk in range(1, CHUNKS):
-            if chunk + 1 < CHUNKS:
-                round_page(LAST, chunk + 1)
+        features = [features_tile(n, rest) for n in range(N_TILES)]
+        for chunk in range(OPENED, CHUNKS):
             weave_and_quantize(chunk)
-        store_page_codes(1, rest)
-        store_page_scales(1)
+        store_page_codes(1, slice(S, T2))
         for n in range(N_TILES):
-            features = features_tile(n, rest)
-            for chunk in range(1, CHUNKS):
-                if chunk < OPENED:
-                    bank = banks[N_TILES + n]
-                else:
-                    bank = banks[(2 * n + chunk - OPENED) % N_TILES]
-                    read_page(0, bank, n, chunk_columns(chunk))
-                read_page(1, bank, n, chunk_columns(chunk))
-                target = features[:, chunk * BANK - rest.start : (chunk + 1) * BANK - rest.start]
-                add_bias(target, bank, n, chunk == CHUNKS - 1)
-            nc.sync.dma_start(out=out_0[n * P : (n + 1) * P, rest], in_=features[:])
+            read_page(1, banks[N_TILES + n], n, chunk_columns(1))
+            add_bias(features[n][:, :BANK], banks[N_TILES + n], n, False)
+            for chunk in range(OPENED, CHUNKS):
+                bank = banks[(2 * n + chunk - OPENED) % 6]
+                for g in range(GROUPS):
+                    read_page(g, bank, n, chunk_columns(chunk))
+                target = features[n][:, chunk * BANK - rest.start : (chunk + 1) * BANK - rest.start]
+                add_bias(target, bank, n, chunk == CHUNKS - 1 or n % 2 == 1)
+            nc.sync.dma_start(out=out_0[n * P : (n + 1) * P, rest], in_=features[n][:])
+            if n == 0:
+                store_page_scales(1, (1,))

@@ -37,6 +37,7 @@ PIECE = 2 * P
 BANKS = 8
 LEAD = 256
 SHARE = 256
+VECTOR_COLUMNS = 160
 OPENED = 2
 
 
@@ -82,7 +83,7 @@ def tile_list_clue_memory_triple_kernel(
 
         TABLE, LOADED, LEFT, WOVEN_W, CODES_W, WOVEN_PAGE, PLANES, PAIR, VALUES, SPARE = 0, 8, 40, 48, 64, 72, 88, 104, 112, 124
         table_words = placed("table_words", [P, T], U32, TABLE)
-        table_scales = placed("table_scales", [P, T], U8, CODES_W)
+        table_scales = placed("table_scales", [P, T], U8, PAIR)
         loaded = {}
         values = {}
         dealt_in = page0[PASS:, :].rearrange("(p t) m -> t p m", t=PACK)
@@ -123,12 +124,13 @@ def tile_list_clue_memory_triple_kernel(
         woven_w = [placed("woven_w%d" % n, [P, 2 * PACK * width], BF16, (WOVEN_W, SPARE, WOVEN_W + 8)[n]) for n, width in enumerate(widths)]
         w_codes = [placed("w_codes%d" % n, [P, 2 * width], U32, CODES_W + 2 * n) for n, width in enumerate(widths)]
 
-        def round_weight(which, piece):
+        def round_weight(which, piece, engine_copy=nc.scalar.copy, cols=slice(0, PIECE)):
             width = PACK * widths[piece]
             target = woven_w[piece][:, which * width : (which + 1) * width]
             source = loaded[which, piece][:]
             if piece < 2:
-                nc.scalar.copy(
+                target, source = target[:, PACK * cols.start : PACK * cols.stop], source[:, :, cols]
+                engine_copy(
                     out=target.rearrange("p (c i j) -> p c j i", i=4, j=PACK), in_=source.rearrange("p j (c i) -> p c j i", i=4)
                 )
             else:
@@ -280,8 +282,8 @@ def tile_list_clue_memory_triple_kernel(
         nc.vector.memset(w4_scale_tile[:].bitcast(I32), 0)
         make_identity(nc, identity[:])
 
-        nc.sync.dma_start(pick[:], offs)
         load_weight(0, 0)
+        nc.sync.dma_start(pick[:], offs)
         load_scale_rows(table_scales, tab_scales)
         nc.sync.dma_start(out=table_words[:].bitcast(I32), in_=tab_words[0].rearrange("p t i -> p (t i)").bitcast(I32))
         load_scale_rows(w2_scale_tile, w2_scales)
@@ -297,6 +299,9 @@ def tile_list_clue_memory_triple_kernel(
         load_page(1)
         load_weight(1, 2)
 
+        round_weight(0, 0, nc.vector.tensor_copy, slice(0, VECTOR_COLUMNS))
+        round_weight(0, 0, nc.scalar.copy, slice(VECTOR_COLUMNS, PIECE))
+        quantize_weight(0, 0, PIECE)
         nc.vector.tensor_copy(out=picked_scales[:], in_=table_scales[:].indirect(pick[:]))
         for h in range(HALVES):
             columns = BANK // PER_COLUMN
@@ -305,9 +310,8 @@ def tile_list_clue_memory_triple_kernel(
             out=w2_dealt_scales[:].rearrange("p (t m) -> p m t", t=PACK),
             in_=w2_scale_tile[:, PASS:].rearrange("p (m t) -> p m t", t=PACK),
         )
-        for which in range(2):
-            round_weight(which, 0)
-            quantize_weight(0, which * PIECE, PIECE)
+        round_weight(1, 0)
+        quantize_weight(0, PIECE, PIECE)
 
         values[0] = placed("values0", [P, S], F32, LOADED + 2)
         a1 = placed("a1", [P, S], F32, LOADED - 2)
@@ -439,18 +443,19 @@ def tile_list_clue_memory_triple_kernel(
         store_page_scales(1, (0,))
         rest = slice(BANK, T2)
         features = [features_tile(n, rest) for n in range(N_TILES)]
+        for n in range(N_TILES):
+            read_page(1, banks[N_TILES + n], n, chunk_columns(1))
+            add_bias(features[n][:, :BANK], banks[N_TILES + n], n, False)
         for chunk in range(OPENED, CHUNKS):
             weave_and_quantize(chunk)
         store_page_codes(1, slice(S, T2))
         for n in range(N_TILES):
-            read_page(1, banks[N_TILES + n], n, chunk_columns(1))
-            add_bias(features[n][:, :BANK], banks[N_TILES + n], n, False)
             for chunk in range(OPENED, CHUNKS):
                 bank = banks[(2 * n + chunk - OPENED) % 6]
                 for g in range(GROUPS):
                     read_page(g, bank, n, chunk_columns(chunk))
                 target = features[n][:, chunk * BANK - rest.start : (chunk + 1) * BANK - rest.start]
-                add_bias(target, bank, n, chunk == CHUNKS - 1 or n % 2 == 1)
+                add_bias(target, bank, n, n < N_TILES - 1)
             nc.sync.dma_start(out=out_0[n * P : (n + 1) * P, rest], in_=features[n][:])
             if n == 0:
                 store_page_scales(1, (1,))

@@ -73,15 +73,16 @@ def tile_list_clue_memory_triple_kernel(
         w4_codes = held("w4_codes", [P, GROUPS * N], U32)
         w4_scale_tile = held("w4_scale_tile", [P, GROUPS * N], U8)
         bias = held("bias", [P, N_TILES], F32)
-        gain = held("gain", [P, S], F32)
         identity = held("identity", [P, P], F32)
         pages = [held("page%d" % i, [P, T2], F32) for i in range(TILES)]
         page_scales = {(g, n): held("page_scales%d_%d" % (g, n), [P, S], U8) for g in range(GROUPS) for n in range(2)}
         widths = (PIECE, PIECE, PASS)
         w_scales = [held("w_scales%d" % n, [P, 2 * width], U8) for n, width in enumerate(widths)]
-        turned = [held("turned%d" % c, [P, PACK * BANK], BF16) for c in range(CHUNKS)]
 
-        TABLE, LOADED, LEFT, WOVEN_W, CODES_W, WOVEN_PAGE, PLANES, PAIR, VALUES, SPARE = 0, 8, 40, 48, 64, 72, 88, 104, 112, 124
+        TABLE, LOADED, LEFT, WOVEN_W, CODES_W, WOVEN_PAGE, PLANES, PAIR, VALUES, GAIN, SPARE, TURNED = 0, 8, 40, 48, 64, 72, 88, 104, 112, 120, 128, 136
+        turned = [placed("turned%d" % c, [P, PACK * BANK], BF16, TURNED + 4 * c) for c in range(CHUNKS)]
+        b1_gain = placed("b1_gain", [P, 2 * S], F32, GAIN)
+        b1, gain = b1_gain[:, :S], b1_gain[:, S:]
         table_words = placed("table_words", [P, T], U32, TABLE)
         table_scales = placed("table_scales", [P, T], U8, PAIR)
         loaded = {}
@@ -117,7 +118,7 @@ def tile_list_clue_memory_triple_kernel(
         rights = {}
 
         def load_dealt_gain(t):
-            rights[t] = placed("right%d" % t, [P, 2 * S], F32, TABLE + 8 * t)
+            rights[t] = placed("right%d" % t, [P, 2 * S], F32, TABLE + 8 * t if t < 2 else PLANES + 8 * (t - 2))
             for q in (0, 2, 1, 3):
                 nc.sync.dma_start(out=rights[t][QUADRANT * q : QUADRANT * (q + 1), :S], in_=gain_rows[:, t, :])
 
@@ -186,7 +187,7 @@ def tile_list_clue_memory_triple_kernel(
 
         def turn_tile(i):
             for chunk in range(CHUNKS):
-                bank = next_bank()
+                bank = banks[(len(used) - CHUNKS + chunk) % BANKS]
                 for block in range(BLOCKS):
                     first = chunk * BANK + block * P
                     nc.tensor.transpose(bank[:, block * P : (block + 1) * P], pages[i][:, first : first + P], identity[:])
@@ -286,8 +287,8 @@ def tile_list_clue_memory_triple_kernel(
         nc.sync.dma_start(pick[:], offs)
         load_scale_rows(table_scales, tab_scales)
         nc.sync.dma_start(out=table_words[:].bitcast(I32), in_=tab_words[0].rearrange("p t i -> p (t i)").bitcast(I32))
-        load_scale_rows(w2_scale_tile, w2_scales)
         load_weight(1, 0)
+        load_scale_rows(w2_scale_tile, w2_scales)
         for h in range(HALVES):
             nc.sync.dma_start(out=gain[:, half(h)], in_=wgs[:, half(h)])
         nc.sync.dma_start(out=w2_codes[:].bitcast(I32), in_=w2_words[0].bitcast(I32))
@@ -306,38 +307,35 @@ def tile_list_clue_memory_triple_kernel(
         for h in range(HALVES):
             columns = BANK // PER_COLUMN
             nc.vector.tensor_copy(out=picked_words[h][:], in_=table_words[:].indirect(pick[:, h * columns : (h + 1) * columns]))
+        round_weight(1, 0)
+        quantize_weight(0, PIECE, PIECE)
         nc.vector.tensor_copy(
             out=w2_dealt_scales[:].rearrange("p (t m) -> p m t", t=PACK),
             in_=w2_scale_tile[:, PASS:].rearrange("p (m t) -> p m t", t=PACK),
         )
-        round_weight(1, 0)
-        quantize_weight(0, PIECE, PIECE)
 
         values[0] = placed("values0", [P, S], F32, LOADED + 2)
         a1 = placed("a1", [P, S], F32, LOADED - 2)
         for h in range(HALVES):
             nc.vector.tensor_tensor(out=values[0][:, half(h)], in0=product(0, half(h), "a"), in1=gain[:, half(h)], op=MULT)
             nc.scalar.copy(out=a1[:, half(h)], in_=product(1, half(h), "a"))
-        c1 = placed("c1", [P, S], F32, WOVEN_W + 4)
-        b1 = placed("b1", [P, S], F32, VALUES + 4)
+        c1 = placed("c1", [P, S], F32, SPARE + 4)
         for name in "cb":
             for h in range(HALVES):
                 nc.vector.tensor_tensor(out=values[0][:, half(h)], in0=product(0, half(h), name), in1=values[0][:, half(h)], op=MULT)
             copy_product(c1 if name == "c" else b1, 1, name)
-        values[1] = placed("values1", [P, S], F32, WOVEN_W)
+        both = placed("values1_2", [P, 2 * S], F32, WOVEN_W)
+        values[1], values[2] = both[:, :S], both[:, S:]
         for h in range(HALVES):
             multiply(values[1][:, half(h)], a1[:, half(h)], gain[:, half(h)])
         multiply(values[1][:], values[1][:], c1[:])
-        multiply(values[1][:], values[1][:], b1[:])
-        b2 = placed("b2", [P, S], F32, SPARE + 4)
-        copy_product(b2, 2, "b")
-        values[2] = placed("values2", [P, S], F32, VALUES + 4)
-        multiply(values[2][:], b2[:], gain[:])
+        copy_product(values[2], 2, "b")
+        multiply(both[:], both[:], b1_gain[:])
         for which in range(2):
             round_weight(which, 1)
         b3 = placed("b3", [P, S], F32, LEFT)
         copy_product(b3, 3, "b")
-        w2_dealt_codes = placed("w2_dealt_codes", [P, 2 * PASS], U8, WOVEN_W + 4)
+        w2_dealt_codes = placed("w2_dealt_codes", [P, 2 * PASS], U8, SPARE + 6)
         nc.scalar.copy(
             out=w2_dealt_codes[:].bitcast(U16).rearrange("p (t m) -> p t m", t=PACK),
             in_=w2_codes[:, 2 * PASS :].bitcast(U16).rearrange("p (m t) -> p t m", t=PACK),
@@ -362,41 +360,45 @@ def tile_list_clue_memory_triple_kernel(
         with nc.allow_non_contiguous_dma(reason="one bias value for each partition"):
             nc.sync.dma_start(out=bias[:], in_=b4.rearrange("(c p) -> p c", p=P))
 
+
         place_values(0)
         quantize_weight(1, 0, 2 * PIECE)
         begun3 = placed("begun3", [P, S], F32, SPARE + 2)
         multiply(begun3[:], b3[:], gain[:])
-        a2, c2 = placed("a2", [P, S], F32, PLANES), placed("c2", [P, S], F32, PLANES + 4)
+        a2, c2 = placed("a2", [P, S], F32, LEFT - 8), placed("c2", [P, S], F32, LEFT - 4)
         copy_product(a2, 2, "a")
         for cols in (slice(SHARE, BANK), half(1)):
             nc.scalar.copy(out=c2[:, cols], in_=product(2, cols, "c"))
         multiply(values[2][:], values[2][:], a2[:])
         multiply(values[2][:, SHARE:], values[2][:, SHARE:], c2[:, SHARE:])
         round_weight(1, 2)
-        a3, c3 = placed("a3", [P, S], F32, PLANES + 8), placed("c3", [P, S], F32, PLANES + 12)
-        copy_product(a3, 3, "a")
+        a3, c3 = placed("a3", [P, S], F32, LEFT - 16), placed("c3", [P, S], F32, LEFT - 12)
+        for cols in (slice(SHARE, BANK), half(1)):
+            nc.scalar.copy(out=a3[:, cols], in_=product(3, cols, "a"))
         copy_product(c3, 3, "c")
 
         place_values(1)
         nc.vector.tensor_tensor(out=values[2][:, :SHARE], in0=product(2, slice(0, SHARE), "c"), in1=values[2][:, :SHARE], op=MULT)
         quantize_weight(2, 0, 2 * PASS)
         values[3] = placed("values3", [P, S], F32, WOVEN_W + 8)
-        multiply(values[3][:], begun3[:], a3[:])
+        nc.vector.tensor_tensor(out=values[3][:, :SHARE], in0=product(3, slice(0, SHARE), "a"), in1=begun3[:, :SHARE], op=MULT)
+        multiply(values[3][:, SHARE:], begun3[:, SHARE:], a3[:, SHARE:])
         multiply(values[3][:], values[3][:], c3[:])
 
         def merged_values(i):
-            left = placed("left%d" % i, [P, 2 * S], F32, LEFT - 8 * (i % 2))
+            left = placed("left%d" % i, [P, 2 * S], F32, WOVEN_W + 8 if i == LAST else LEFT - 8 * (i % 2))
             right = rights[i - PACK]
-            copy_product(left[:, :S], i, "b")
-            copy_product(left[:, S:], i, "a")
-            copy_product(right[:, S:], i, "c")
+            targets = {"a": left[:, S:], "b": left[:, :S], "c": right[:, S:]}
+            for name in "bac" if i == PACK else "acb":
+                copy_product(targets[name], i, name)
             pair = placed("pair%d" % i, [P, 2 * S], F32, PAIR)
             multiply(pair[:], left[:], right[:])
             values[i] = pair
             if i < LAST:
-                values[i] = placed("values%d" % i, [P, S], F32, VALUES + 4 * (i % 3))
+                values[i] = placed("values%d" % i, [P, S], F32, VALUES + 4 * (i % 2))
                 multiply(values[i][:], pair[:, :S], pair[:, S:])
 
+        used.extend([None] * 2)
         merged_values(4)
         turn_tile(0)
         place_values(2)
@@ -409,7 +411,7 @@ def tile_list_clue_memory_triple_kernel(
         merged_values(7)
         turn_tile(3)
         woven = [placed("woven_group%d" % n, [P, 2 * PACK * BANK], BF16, WOVEN_PAGE + 8 * n) for n in range(2)]
-        planes = [placed("planes%d" % c, [P, PACK * BANK], BF16, PLANES + 4 * c) for c in range(CHUNKS)]
+        planes = [placed("planes%d" % c, [P, PACK * BANK], BF16, TURNED + 4 * c) for c in range(CHUNKS)]
         for chunk in range(CHUNKS):
             turn_back(chunk, woven[chunk // 2][:, (chunk % 2) * PACK * BANK : (chunk % 2 + 1) * PACK * BANK])
         round_tile(4)

@@ -37,7 +37,6 @@ PIECE = 2 * P
 BANKS = 8
 LEAD = 256
 SHARE = 256
-VECTOR_COLUMNS = 160
 OPENED = 2
 
 
@@ -81,8 +80,8 @@ def tile_list_clue_memory_triple_kernel(
 
         TABLE, LOADED, LEFT, WOVEN_W, CODES_W, WOVEN_PAGE, PLANES, PAIR, VALUES, GAIN, SPARE, TURNED = 0, 8, 40, 48, 64, 72, 88, 104, 112, 120, 128, 136
         turned = [placed("turned%d" % c, [P, PACK * BANK], BF16, TURNED + 4 * c) for c in range(CHUNKS)]
-        b1_gain = placed("b1_gain", [P, 2 * S], F32, GAIN)
-        b1, gain = b1_gain[:, :S], b1_gain[:, S:]
+        c1_gain = placed("c1_gain", [P, 2 * S], F32, GAIN)
+        c1, gain = c1_gain[:, :S], c1_gain[:, S:]
         table_words = placed("table_words", [P, T], U32, TABLE)
         table_scales = placed("table_scales", [P, T], U8, PAIR)
         loaded = {}
@@ -283,15 +282,15 @@ def tile_list_clue_memory_triple_kernel(
         nc.vector.memset(w4_scale_tile[:].bitcast(I32), 0)
         make_identity(nc, identity[:])
 
-        load_weight(0, 0)
+        nc.sync.dma_start(out=w2_codes[:].bitcast(I32), in_=w2_words[0].bitcast(I32))
         nc.sync.dma_start(pick[:], offs)
         load_scale_rows(table_scales, tab_scales)
         nc.sync.dma_start(out=table_words[:].bitcast(I32), in_=tab_words[0].rearrange("p t i -> p (t i)").bitcast(I32))
-        load_weight(1, 0)
         load_scale_rows(w2_scale_tile, w2_scales)
+        load_weight(0, 0)
+        load_weight(1, 0)
         for h in range(HALVES):
             nc.sync.dma_start(out=gain[:, half(h)], in_=wgs[:, half(h)])
-        nc.sync.dma_start(out=w2_codes[:].bitcast(I32), in_=w2_words[0].bitcast(I32))
         nc.sync.dma_start(place[:], offs2)
         load_page(0)
         load_weight(0, 1)
@@ -300,37 +299,36 @@ def tile_list_clue_memory_triple_kernel(
         load_page(1)
         load_weight(1, 2)
 
-        round_weight(0, 0, nc.vector.tensor_copy, slice(0, VECTOR_COLUMNS))
-        round_weight(0, 0, nc.scalar.copy, slice(VECTOR_COLUMNS, PIECE))
-        quantize_weight(0, 0, PIECE)
         nc.vector.tensor_copy(out=picked_scales[:], in_=table_scales[:].indirect(pick[:]))
         for h in range(HALVES):
             columns = BANK // PER_COLUMN
             nc.vector.tensor_copy(out=picked_words[h][:], in_=table_words[:].indirect(pick[:, h * columns : (h + 1) * columns]))
-        round_weight(1, 0)
-        quantize_weight(0, PIECE, PIECE)
         nc.vector.tensor_copy(
             out=w2_dealt_scales[:].rearrange("p (t m) -> p m t", t=PACK),
             in_=w2_scale_tile[:, PASS:].rearrange("p (m t) -> p m t", t=PACK),
         )
+        round_weight(0, 0)
+        quantize_weight(0, 0, PIECE)
+        round_weight(1, 0)
+        quantize_weight(0, PIECE, PIECE)
 
-        values[0] = placed("values0", [P, S], F32, LOADED + 2)
-        a1 = placed("a1", [P, S], F32, LOADED - 2)
-        for h in range(HALVES):
-            nc.vector.tensor_tensor(out=values[0][:, half(h)], in0=product(0, half(h), "a"), in1=gain[:, half(h)], op=MULT)
-            nc.scalar.copy(out=a1[:, half(h)], in_=product(1, half(h), "a"))
-        c1 = placed("c1", [P, S], F32, SPARE + 4)
-        for name in "cb":
-            for h in range(HALVES):
-                nc.vector.tensor_tensor(out=values[0][:, half(h)], in0=product(0, half(h), name), in1=values[0][:, half(h)], op=MULT)
-            copy_product(c1 if name == "c" else b1, 1, name)
+        values[0] = placed("values0", [P, S], F32, VALUES)
+        b1 = placed("b1", [P, S], F32, LOADED)
         both = placed("values1_2", [P, 2 * S], F32, WOVEN_W)
         values[1], values[2] = both[:, :S], both[:, S:]
         for h in range(HALVES):
-            multiply(values[1][:, half(h)], a1[:, half(h)], gain[:, half(h)])
-        multiply(values[1][:], values[1][:], c1[:])
+            nc.vector.tensor_tensor(out=values[0][:, half(h)], in0=product(0, half(h), "b"), in1=gain[:, half(h)], op=MULT)
+            nc.scalar.copy(out=b1[:, half(h)], in_=product(1, half(h), "b"))
+        for h in range(HALVES):
+            multiply(values[1][:, half(h)], b1[:, half(h)], gain[:, half(h)])
+        a1 = placed("a1", [P, S], F32, VALUES + 4)
+        for name in "ac":
+            for h in range(HALVES):
+                nc.vector.tensor_tensor(out=values[0][:, half(h)], in0=product(0, half(h), name), in1=values[0][:, half(h)], op=MULT)
+            copy_product(a1 if name == "a" else c1, 1, name)
+        multiply(values[1][:], values[1][:], a1[:])
         copy_product(values[2], 2, "b")
-        multiply(both[:], both[:], b1_gain[:])
+        multiply(both[:], both[:], c1_gain[:])
         for which in range(2):
             round_weight(which, 1)
         b3 = placed("b3", [P, S], F32, LEFT)

@@ -35,7 +35,7 @@ SCALE_ROWS = 4
 PER_COLUMN = 16
 PIECE = 2 * P
 BANKS = 8
-LEAD = 256
+FUSED = 256
 SHARE = 256
 OPENED = 2
 
@@ -173,10 +173,11 @@ def tile_list_clue_memory_triple_kernel(
         def entries(cols):
             return place[:, cols.start // PER_COLUMN : cols.stop // PER_COLUMN]
 
-        def place_values(i, lead=None):
-            if lead is not None:
-                nc.vector.tensor_copy(out=pages[i][:].indirect(entries(slice(0, LEAD))), in_=lead[:])
-                nc.vector.tensor_copy(out=pages[i][:].indirect(entries(slice(LEAD, S))), in_=values[i][:, LEAD:])
+        def place_values(i):
+            if i == LAST - 1:
+                nc.vector.tensor_copy(out=pages[i][:].indirect(entries(slice(0, S - FUSED))), in_=values[i][:])
+                rest = values[i, 1]
+                nc.vector.tensor_tensor(out=pages[i][:].indirect(entries(slice(S - FUSED, S))), in0=rest[:, 0], in1=rest[:, 1], op=MULT)
             elif i == LAST:
                 nc.vector.tensor_tensor(out=pages[i][:].indirect(place[:]), in0=values[i][:, :S], in1=values[i][:, S:], op=MULT)
             else:
@@ -371,16 +372,14 @@ def tile_list_clue_memory_triple_kernel(
         multiply(values[2][:, SHARE:], values[2][:, SHARE:], c2[:, SHARE:])
         round_weight(1, 2)
         a3, c3 = placed("a3", [P, S], F32, LEFT - 16), placed("c3", [P, S], F32, LEFT - 12)
-        for cols in (slice(SHARE, BANK), half(1)):
-            nc.scalar.copy(out=a3[:, cols], in_=product(3, cols, "a"))
+        copy_product(a3, 3, "a")
         copy_product(c3, 3, "c")
 
         place_values(1)
         nc.vector.tensor_tensor(out=values[2][:, :SHARE], in0=product(2, slice(0, SHARE), "c"), in1=values[2][:, :SHARE], op=MULT)
         quantize_weight(2, 0, 2 * PASS)
         values[3] = placed("values3", [P, S], F32, WOVEN_W + 8)
-        nc.vector.tensor_tensor(out=values[3][:, :SHARE], in0=product(3, slice(0, SHARE), "a"), in1=begun3[:, :SHARE], op=MULT)
-        multiply(values[3][:, SHARE:], begun3[:, SHARE:], a3[:, SHARE:])
+        multiply(values[3][:], begun3[:], a3[:])
         multiply(values[3][:], values[3][:], c3[:])
 
         def merged_values(i):
@@ -389,14 +388,23 @@ def tile_list_clue_memory_triple_kernel(
             targets = {"a": left[:, S:], "b": left[:, :S], "c": right[:, S:]}
             for name in "bac" if i == PACK else "acb":
                 copy_product(targets[name], i, name)
-            pair = placed("pair%d" % i, [P, 2 * S], F32, PAIR)
+            if i == LAST - 1:
+                left, right = (tile[:].rearrange("p (k c) -> p k c", k=2) for tile in (left, right))
+                pair = placed("pair_first", [P, 2, S - FUSED], F32, PAIR)
+                multiply(pair[:], left[:, :, : S - FUSED], right[:, :, : S - FUSED])
+                values[i] = placed("values%d" % i, [P, S - FUSED], F32, GAIN)
+                multiply(values[i][:], pair[:, 0], pair[:, 1])
+                values[i, 1] = placed("pair_rest", [P, 2, FUSED], F32, PAIR)
+                multiply(values[i, 1][:], left[:, :, S - FUSED :], right[:, :, S - FUSED :])
+                return
+            pair = placed("pair%d" % i, [P, 2 * S], F32, PAIR + 2 if i == LAST else PAIR)
             multiply(pair[:], left[:], right[:])
             values[i] = pair
             if i < LAST:
                 values[i] = placed("values%d" % i, [P, S], F32, VALUES + 4 * (i % 2))
                 multiply(values[i][:], pair[:, :S], pair[:, S:])
 
-        used.extend([None] * 2)
+        used.extend([None] * 3)
         merged_values(4)
         turn_tile(0)
         place_values(2)
@@ -416,7 +424,7 @@ def tile_list_clue_memory_triple_kernel(
         place_values(5)
         round_tile(5)
         place_values(6)
-        page_codes[0, 0] = placed("page_codes0a", [P, S], U32, VALUES)
+        page_codes[0, 0] = placed("page_codes0a", [P, S], U32, PAIR - 2)
         quantize_page(0, slice(0, S), woven[0][:])
         store_page_codes(0, slice(0, S))
         store_page_scales(0, (0,))
@@ -427,7 +435,7 @@ def tile_list_clue_memory_triple_kernel(
             for n in range(N_TILES):
                 read_page(0, banks[chunk * N_TILES + n], n, chunk_columns(chunk))
         place_values(LAST)
-        page_codes[0, 1] = placed("page_codes0b", [P, S], U32, PAIR)
+        page_codes[0, 1] = placed("page_codes0b", [P, S], U32, PAIR + 2)
         quantize_page(0, slice(S, T2), woven[1][:])
         store_page_codes(0, slice(S, T2))
         store_page_scales(0, (1,))

@@ -319,9 +319,12 @@ def tile_list_clue_memory_triple_kernel(
         values[1], values[2] = both[:, :S], both[:, S:]
         for h in range(HALVES):
             nc.vector.tensor_tensor(out=values[0][:, half(h)], in0=product(0, half(h), "b"), in1=gain[:, half(h)], op=MULT)
-            nc.scalar.copy(out=b1[:, half(h)], in_=product(1, half(h), "b"))
-        for h in range(HALVES):
-            multiply(values[1][:, half(h)], b1[:, half(h)], gain[:, half(h)])
+            sums = product(1, half(h), "b")
+            cols = slice(SHARE, BANK) if h == 0 else half(h)
+            nc.scalar.copy(out=b1[:, cols], in_=sums[:, cols.start - h * BANK :])
+            multiply(values[1][:, cols], b1[:, cols], gain[:, cols])
+            if h == 0:
+                nc.vector.tensor_tensor(out=values[1][:, :SHARE], in0=sums[:, :SHARE], in1=gain[:, :SHARE], op=MULT)
         a1 = placed("a1", [P, S], F32, VALUES + 4)
         for name in "ac":
             for h in range(HALVES):

from contextlib import ExitStack

import concourse.mybir as mybir
from concourse.masks import make_identity

K, H, N, T, S, T2 = 512, 1024, 512, 2048, 1024, 2048
FLOPS = 2 * (3 * K * H * S + H * N * T2)

F32 = mybir.dt.float32
BF16 = mybir.dt.bfloat16
I32 = mybir.dt.int32
U32 = mybir.dt.uint32
U16 = mybir.dt.uint16
U8 = mybir.dt.uint8
FP8X4 = mybir.dt.float8_e4m3fn_x4
FP4X4 = mybir.dt.float4_e2m1fn_x4
MULT = mybir.AluOpType.mult
ADD = mybir.AluOpType.add
IDENTITY = mybir.ActivationFunctionType.Identity

P = 128
PACK = 4
PASS = P * PACK
BANK = 512
GROUPS = H // PASS
TILES = H // P
LAST = TILES - 1
HALVES = S // BANK
CHUNKS = T2 // BANK
BLOCKS = BANK // P
N_TILES = N // P
QUADRANT = 32
QUADRANTS = P // QUADRANT
SCALE_ROWS = 4
PER_COLUMN = 16
PIECE = 2 * P
BANKS = 8
FUSED = 256
SHARE = 256
OPENED = 2


def tile_list_clue_memory_triple_kernel(
    tc, tab_words, tab_scales, offs, offs2, w1, w2_words, w2_scales, w3, wgs, page0,
    w4_words, w4_scales, b4, out_0, out_1, out_2, out_3,
):
    nc = tc.nc
    with ExitStack() as ctx:
        keep = ctx.enter_context(tc.tile_pool(name="keep", bufs=1))
        turns = ctx.enter_context(tc.tile_pool(name="turns", bufs=1))
        psum = ctx.enter_context(tc.psum_pool(name="psum", bufs=1))
        banks = [psum.tile([P, BANK], F32, name="bank%d" % n) for n in range(BANKS)]
        used = []

        def next_bank():
            used.append(None)
            return banks[(len(used) - 1) % BANKS]

        def held(name, shape, dtype):
            return keep.tile(shape, dtype, name=name, align_bytes=64)

        def placed(name, shape, dtype, kib):
            return turns.tile(shape, dtype, name=name, align_bytes=64, offset=1024 * kib)

        pick = keep.tile([P, S // PER_COLUMN], U16, name="pick")
        place = keep.tile([P, S // PER_COLUMN], U16, name="place")
        picked_words = [held("picked_words%d" % h, [P, BANK], U32) for h in range(HALVES)]
        picked_scales = held("picked_scales", [P, S], U8)
        w2_codes = held("w2_codes", [P, 2 * H], U8)
        w2_scale_tile = held("w2_scale_tile", [P, H], U8)
        w2_dealt_scales = held("w2_dealt_scales", [P, PASS], U8)
        w4_codes = held("w4_codes", [P, GROUPS * N], U32)
        w4_scale_tile = held("w4_scale_tile", [P, GROUPS * N], U8)
        bias = held("bias", [P, N_TILES], F32)
        identity = held("identity", [P, P], F32)
        pages = [held("page%d" % i, [P, T2], F32) for i in range(TILES)]
        page_scales = {(g, n): held("page_scales%d_%d" % (g, n), [P, S], U8) for g in range(GROUPS) for n in range(2)}
        widths = (PIECE, PIECE, PASS)
        w_scales = [held("w_scales%d" % n, [P, 2 * width], U8) for n, width in enumerate(widths)]

        TABLE, LOADED, LEFT, WOVEN_W, CODES_W, WOVEN_PAGE, PLANES, PAIR, VALUES, GAIN, SPARE, TURNED = 0, 8, 40, 48, 64, 72, 88, 104, 112, 120, 128, 136
        turned = [placed("turned%d" % c, [P, PACK * BANK], BF16, TURNED + 4 * c) for c in range(CHUNKS)]
        c1_gain = placed("c1_gain", [P, 2 * S], F32, GAIN)
        c1, gain = c1_gain[:, :S], c1_gain[:, S:]
        table_words = placed("table_words", [P, T], U32, TABLE)
        table_scales = placed("table_scales", [P, T], U8, PAIR)
        loaded = {}
        values = {}
        dealt_in = page0[PASS:, :].rearrange("(p t) m -> t p m", t=PACK)
        dealt_out = out_1[PASS:, :].rearrange("(p t) m -> t p m", t=PACK)
        gain_rows = wgs.rearrange("(u t) j -> u t j", t=PACK)

        def half(h):
            return slice(h * BANK, (h + 1) * BANK)

        def load_scale_rows(scale_tile, rows):
            passes = rows.shape[0]
            for r in range(SCALE_ROWS):
                nc.sync.dma_start(
                    out=scale_tile[r:P:QUADRANT, :].bitcast(I32).rearrange("q (a c) -> q a c", a=passes),
                    in_=rows.bitcast(I32).rearrange("a (q r) c -> r q a c", r=SCALE_ROWS)[r],
                )

        def load_weight(which, piece):
            first, width = piece * PIECE, widths[piece]
            kib = LOADED + 4 * PACK * (2 * first + (1 - which) * width) // 1024
            loaded[which, piece] = placed("w_loaded%d_%d" % (which, piece), [P, PACK, width], F32, kib)
            nc.sync.dma_start(
                out=loaded[which, piece][:],
                in_=(w1, w3)[which][:, first : first + width].rearrange("(p j) c -> p j c", j=PACK),
            )

        def load_page(i):
            rows = page0[i * P : (i + 1) * P, :] if i < PACK else dealt_in[i - PACK]
            nc.sync.dma_start(out=pages[i][:], in_=rows)

        rights = {}

        def load_dealt_gain(t):
            rights[t] = placed("right%d" % t, [P, 2 * S], F32, TABLE + 8 * t if t < 2 else PLANES + 8 * (t - 2))
            for q in (0, 2, 1, 3):
                nc.sync.dma_start(out=rights[t][QUADRANT * q : QUADRANT * (q + 1), :S], in_=gain_rows[:, t, :])

        woven_w = [placed("woven_w%d" % n, [P, 2 * PACK * width], BF16, (WOVEN_W, SPARE, WOVEN_W + 8)[n]) for n, width in enumerate(widths)]
        w_codes = [placed("w_codes%d" % n, [P, 2 * width], U32, CODES_W + 2 * n) for n, width in enumerate(widths)]

        def round_weight(which, piece, engine_copy=nc.scalar.copy, cols=slice(0, PIECE)):
            width = PACK * widths[piece]
            target = woven_w[piece][:, which * width : (which + 1) * width]
            source = loaded[which, piece][:]
            if piece < 2:
                target, source = target[:, PACK * cols.start : PACK * cols.stop], source[:, :, cols]
                engine_copy(
                    out=target.rearrange("p (c i j) -> p c j i", i=4, j=PACK), in_=source.rearrange("p j (c i) -> p c j i", i=4)
                )
            else:
                nc.scalar.copy(
                    out=target.rearrange("p (t m j) -> p m j t", t=PACK, j=PACK), in_=source.rearrange("p j (m t) -> p m j t", t=PACK)
                )

        def quantize_weight(piece, first, count):
            nc.vector.quantize_mx(
                out=w_codes[piece][:, first : first + count].bitcast(FP8X4), scales=w_scales[piece][:, first : first + count],
                in_=woven_w[piece][:, first * PACK : (first + count) * PACK],
            )

        def product(i, cols, name):
            if name == "b":
                codes, scales = (w2_codes, w2_scale_tile) if i < PACK else (w2_dealt_codes, w2_dealt_scales)
                first = (i % PACK) * P
                codes, scales = codes[:, 2 * first : 2 * (first + P)].bitcast(FP4X4), scales[:, first : first + P]
            else:
                piece, first = (i // 2, (i % 2) * P) if i < PACK else (2, (i - PACK) * P)
                if name == "c":
                    first = first + widths[piece]
                codes, scales = w_codes[piece][:, first : first + P].bitcast(FP8X4), w_scales[piece][:, first : first + P]
            h = cols.start // BANK
            within = slice(cols.start - h * BANK, cols.stop - h * BANK)
            sums = next_bank()[:, : cols.stop - cols.start]
            nc.tensor.matmul_mx(
                out=sums, lhsT=codes, lhsT_scale=scales,
                rhs=picked_words[h][:, within].bitcast(FP8X4), rhs_scale=picked_scales[:, cols], start=True, stop=True,
            )
            return sums

        def copy_product(target, i, name, first=0):
            for cols in (slice(first, BANK), half(1)):
                nc.scalar.copy(out=target[:, cols], in_=product(i, cols, name))

        def multiply(target, left, right):
            nc.gpsimd.tensor_tensor(out=target, in0=left, in1=right, op=MULT)

        def entries(cols):
            return place[:, cols.start // PER_COLUMN : cols.stop // PER_COLUMN]

        def place_values(i):
            if i == LAST - 1:
                nc.vector.tensor_copy(out=pages[i][:].indirect(entries(slice(0, S - FUSED))), in_=values[i][:])
                rest = values[i, 1]
                nc.vector.tensor_tensor(out=pages[i][:].indirect(entries(slice(S - FUSED, S))), in0=rest[:, 0], in1=rest[:, 1], op=MULT)
            elif i == LAST:
                nc.vector.tensor_tensor(out=pages[i][:].indirect(place[:]), in0=values[i][:, :S], in1=values[i][:, S:], op=MULT)
            else:
                nc.vector.tensor_copy(out=pages[i][:].indirect(place[:]), in_=values[i][:])
            rows = out_1[i * P : (i + 1) * P, :] if i < PACK else dealt_out[i - PACK]
            nc.sync.dma_start(out=rows, in_=pages[i][:])

        def turn_tile(i):
            for chunk in range(CHUNKS):
                bank = banks[(len(used) - CHUNKS + chunk) % BANKS]
                for block in range(BLOCKS):
                    first = chunk * BANK + block * P
                    nc.tensor.transpose(bank[:, block * P : (block + 1) * P], pages[i][:, first : first + P], identity[:])
                nc.scalar.copy(
                    out=turned[chunk][:].rearrange("p (b u q w e) -> p b u q w e", b=BLOCKS, u=2, q=QUADRANTS, e=2)[:, :, :, i],
                    in_=bank[:].rearrange("p (b w u e) -> p b u w e", b=BLOCKS, u=2, e=2),
                )

        def turn_back(chunk, target):
            words = turned[chunk][:].bitcast(F32)
            target = target.bitcast(F32)
            for n in range(2):
                bank = next_bank()
                for m in range(4):
                    first = (4 * n + m) * P
                    nc.tensor.transpose(bank[:, m * P : (m + 1) * P], words[:, first : first + P], identity[:])
                nc.scalar.copy(
                    out=target[:, n * BANK : (n + 1) * BANK].rearrange("p (b m u) -> p b m u", b=2, u=2),
                    in_=bank[:].rearrange("p (b u m) -> p b m u", b=2, u=2),
                )

        def chunk_columns(chunk):
            return slice(chunk * BANK, (chunk + 1) * BANK)

        def round_page(i, chunk):
            u, e = divmod(i - PACK, 2)
            nc.scalar.copy(out=planes[chunk][:].rearrange("p (u m e) -> p u m e", u=2, e=2)[:, u, :, e], in_=pages[i][:, chunk_columns(chunk)])

        def round_tile(i):
            for chunk in range(CHUNKS):
                round_page(i, chunk)

        def weave_and_quantize(chunk):
            woven = placed("woven_chunk%d" % chunk, [P, PACK * BANK], BF16, WOVEN_PAGE + 4 * chunk)
            nc.vector.tensor_copy(
                out=woven[:].bitcast(F32).rearrange("p (c i u) -> p c u i", i=4, u=2),
                in_=planes[chunk][:].bitcast(F32).rearrange("p (u c i) -> p c u i", i=4, u=2),
            )
            quantize_page(1, chunk_columns(chunk), woven[:])

        page_codes = {}

        def codes_of(g, cols):
            if g == 0:
                first = cols.start // S * S
                return page_codes[0, cols.start // S][:, cols.start - first : cols.stop - first]
            return page_codes[g][:, cols]

        def first_row(g, n):
            return SCALE_ROWS * g * (n + 1)

        def scales_of(g, cols):
            n = cols.start // S
            return page_scales[g, n][first_row(g, n) :, cols.start - n * S : cols.stop - n * S]

        def quantize_page(g, cols, source):
            nc.vector.quantize_mx(out=codes_of(g, cols).bitcast(FP8X4), scales=scales_of(g, cols), in_=source)

        def store_page_scales(g, halves):
            for r in range(SCALE_ROWS):
                for n in halves:
                    nc.sync.dma_start(
                        out=out_3[g][:, n * S : (n + 1) * S].bitcast(I32).rearrange("(q r) m -> r q m", r=SCALE_ROWS)[r],
                        in_=page_scales[g, n][first_row(g, n) + r : P : QUADRANT, :].bitcast(I32),
                    )

        def store_page_codes(g, cols):
            nc.sync.dma_start(
                out=out_2[g].rearrange("p m t -> p (m t)").bitcast(I32)[:, cols], in_=codes_of(g, cols).bitcast(I32)
            )

        def read_page(g, bank, n, cols):
            w4_cols = slice(g * N + n * P, g * N + (n + 1) * P)
            nc.tensor.matmul_mx(
                out=bank[:],
                lhsT=w4_codes[:, w4_cols].bitcast(FP8X4), lhsT_scale=w4_scale_tile[:, w4_cols],
                rhs=codes_of(g, cols).bitcast(FP8X4), rhs_scale=scales_of(g, cols),
                start=(g == 0), stop=(g == GROUPS - 1),
            )

        def add_bias(target, bank, n, on_vector):
            if on_vector:
                nc.vector.tensor_scalar(out=target, in0=bank[:], scalar1=bias[:, n : n + 1], scalar2=None, op0=ADD)
            else:
                nc.scalar.activation(out=target, in_=bank[:], func=IDENTITY, bias=bias[:, n : n + 1])

        def features_tile(n, cols):
            width = cols.stop - cols.start
            return placed("features%d_%d" % (n, cols.start), [P, width], F32, TABLE + 4 * (N_TILES * cols.start + n * width) // 1024)

        nc.gpsimd.memset(table_scales[:].bitcast(I32), 0)
        nc.vector.memset(w2_scale_tile[:].bitcast(I32), 0)
        nc.vector.memset(w4_scale_tile[:].bitcast(I32), 0)
        make_identity(nc, identity[:])

        nc.sync.dma_start(out=w2_codes[:].bitcast(I32), in_=w2_words[0].bitcast(I32))
        nc.sync.dma_start(pick[:], offs)
        load_scale_rows(table_scales, tab_scales)
        nc.sync.dma_start(out=table_words[:].bitcast(I32), in_=tab_words[0].rearrange("p t i -> p (t i)").bitcast(I32))
        load_scale_rows(w2_scale_tile, w2_scales)
        load_weight(0, 0)
        load_weight(1, 0)
        for h in range(HALVES):
            nc.sync.dma_start(out=gain[:, half(h)], in_=wgs[:, half(h)])
        nc.sync.dma_start(place[:], offs2)
        load_page(0)
        load_weight(0, 1)
        load_weight(1, 1)
        load_weight(0, 2)
        load_page(1)
        load_weight(1, 2)

        nc.vector.tensor_copy(out=picked_scales[:], in_=table_scales[:].indirect(pick[:]))
        for h in range(HALVES):
            columns = BANK // PER_COLUMN
            nc.vector.tensor_copy(out=picked_words[h][:], in_=table_words[:].indirect(pick[:, h * columns : (h + 1) * columns]))
        nc.vector.tensor_copy(
            out=w2_dealt_scales[:].rearrange("p (t m) -> p m t", t=PACK),
            in_=w2_scale_tile[:, PASS:].rearrange("p (m t) -> p m t", t=PACK),
        )
        round_weight(0, 0)
        quantize_weight(0, 0, PIECE)
        round_weight(1, 0)
        quantize_weight(0, PIECE, PIECE)

        values[0] = placed("values0", [P, S], F32, VALUES)
        b1 = placed("b1", [P, S], F32, LOADED)
        both = placed("values1_2", [P, 2 * S], F32, WOVEN_W)
        values[1], values[2] = both[:, :S], both[:, S:]
        for h in range(HALVES):
            nc.vector.tensor_tensor(out=values[0][:, half(h)], in0=product(0, half(h), "b"), in1=gain[:, half(h)], op=MULT)
            sums = product(1, half(h), "b")
            cols = slice(SHARE, BANK) if h == 0 else half(h)
            nc.scalar.copy(out=b1[:, cols], in_=sums[:, cols.start - h * BANK :])
            multiply(values[1][:, cols], b1[:, cols], gain[:, cols])
            if h == 0:
                nc.vector.tensor_tensor(out=values[1][:, :SHARE], in0=sums[:, :SHARE], in1=gain[:, :SHARE], op=MULT)
        a1 = placed("a1", [P, S], F32, VALUES + 4)
        for name in "ac":
            for h in range(HALVES):
                nc.vector.tensor_tensor(out=values[0][:, half(h)], in0=product(0, half(h), name), in1=values[0][:, half(h)], op=MULT)
            copy_product(a1 if name == "a" else c1, 1, name)
        multiply(values[1][:], values[1][:], a1[:])
        copy_product(values[2], 2, "b")
        multiply(both[:], both[:], c1_gain[:])
        for which in range(2):
            round_weight(which, 1)
        b3 = placed("b3", [P, S], F32, LEFT)
        copy_product(b3, 3, "b")
        w2_dealt_codes = placed("w2_dealt_codes", [P, 2 * PASS], U8, SPARE + 6)
        nc.scalar.copy(
            out=w2_dealt_codes[:].bitcast(U16).rearrange("p (t m) -> p t m", t=PACK),
            in_=w2_codes[:, 2 * PASS :].bitcast(U16).rearrange("p (m t) -> p t m", t=PACK),
        )
        round_weight(0, 2)
        load_dealt_gain(0)
        load_page(2)
        load_page(3)
        load_dealt_gain(1)
        load_page(4)
        load_dealt_gain(2)
        load_page(5)
        load_dealt_gain(3)
        for g in range(GROUPS):
            nc.sync.dma_start(
                out=w4_codes[:, g * N : (g + 1) * N].bitcast(I32),
                in_=w4_words[g].rearrange("p c i -> p (c i)").bitcast(I32),
            )
        load_page(LAST - 1)
        load_scale_rows(w4_scale_tile, w4_scales)
        load_page(LAST)
        with nc.allow_non_contiguous_dma(reason="one bias value for each partition"):
            nc.sync.dma_start(out=bias[:], in_=b4.rearrange("(c p) -> p c", p=P))


        place_values(0)
        quantize_weight(1, 0, 2 * PIECE)
        begun3 = placed("begun3", [P, S], F32, SPARE + 2)
        multiply(begun3[:], b3[:], gain[:])
        a2, c2 = placed("a2", [P, S], F32, LEFT - 8), placed("c2", [P, S], F32, LEFT - 4)
        copy_product(a2, 2, "a")
        for cols in (slice(SHARE, BANK), half(1)):
            nc.scalar.copy(out=c2[:, cols], in_=product(2, cols, "c"))
        multiply(values[2][:], values[2][:], a2[:])
        multiply(values[2][:, SHARE:], values[2][:, SHARE:], c2[:, SHARE:])
        round_weight(1, 2)
        a3, c3 = placed("a3", [P, S], F32, LEFT - 16), placed("c3", [P, S], F32, LEFT - 12)
        copy_product(a3, 3, "a")
        copy_product(c3, 3, "c")

        place_values(1)
        nc.vector.tensor_tensor(out=values[2][:, :SHARE], in0=product(2, slice(0, SHARE), "c"), in1=values[2][:, :SHARE], op=MULT)
        quantize_weight(2, 0, 2 * PASS)
        values[3] = placed("values3", [P, S], F32, WOVEN_W + 8)
        multiply(values[3][:], begun3[:], a3[:])
        multiply(values[3][:], values[3][:], c3[:])

        def merged_values(i):
            left = placed("left%d" % i, [P, 2 * S], F32, WOVEN_W + 8 if i == LAST else LEFT - 8 * (i % 2))
            right = rights[i - PACK]
            targets = {"a": left[:, S:], "b": left[:, :S], "c": right[:, S:]}
            for name in "bac" if i == PACK else "acb":
                copy_product(targets[name], i, name)
            if i == LAST - 1:
                left, right = (tile[:].rearrange("p (k c) -> p k c", k=2) for tile in (left, right))
                pair = placed("pair_first", [P, 2, S - FUSED], F32, PAIR)
                multiply(pair[:], left[:, :, : S - FUSED], right[:, :, : S - FUSED])
                values[i] = placed("values%d" % i, [P, S - FUSED], F32, GAIN)
                multiply(values[i][:], pair[:, 0], pair[:, 1])
                values[i, 1] = placed("pair_rest", [P, 2, FUSED], F32, PAIR)
                multiply(values[i, 1][:], left[:, :, S - FUSED :], right[:, :, S - FUSED :])
                return
            pair = placed("pair%d" % i, [P, 2 * S], F32, PAIR + 2 if i == LAST else PAIR)
            multiply(pair[:], left[:], right[:])
            values[i] = pair
            if i < LAST:
                values[i] = placed("values%d" % i, [P, S], F32, VALUES + 4 * (i % 2))
                multiply(values[i][:], pair[:, :S], pair[:, S:])

        used.extend([None] * 3)
        merged_values(4)
        turn_tile(0)
        place_values(2)
        merged_values(5)
        turn_tile(1)
        place_values(3)
        merged_values(6)
        turn_tile(2)
        place_values(4)
        merged_values(7)
        turn_tile(3)
        woven = [placed("woven_group%d" % n, [P, 2 * PACK * BANK], BF16, WOVEN_PAGE + 8 * n) for n in range(2)]
        planes = [placed("planes%d" % c, [P, PACK * BANK], BF16, TURNED + 4 * c) for c in range(CHUNKS)]
        for chunk in range(CHUNKS):
            turn_back(chunk, woven[chunk // 2][:, (chunk % 2) * PACK * BANK : (chunk % 2 + 1) * PACK * BANK])
        round_tile(4)
        place_values(5)
        round_tile(5)
        place_values(6)
        page_codes[0, 0] = placed("page_codes0a", [P, S], U32, PAIR - 2)
        quantize_page(0, slice(0, S), woven[0][:])
        store_page_codes(0, slice(0, S))
        store_page_scales(0, (0,))
        round_tile(6)

        page_codes[1] = placed("page_codes1", [P, T2], U32, WOVEN_W)
        for chunk in range(OPENED):
            for n in range(N_TILES):
                read_page(0, banks[chunk * N_TILES + n], n, chunk_columns(chunk))
        place_values(LAST)
        page_codes[0, 1] = placed("page_codes0b", [P, S], U32, PAIR + 2)
        quantize_page(0, slice(S, T2), woven[1][:])
        store_page_codes(0, slice(S, T2))
        store_page_scales(0, (1,))
        round_tile(LAST)
        for chunk in range(OPENED):
            weave_and_quantize(chunk)
        store_page_codes(1, slice(0, S))
        for n in range(N_TILES):
            read_page(1, banks[n], n, chunk_columns(0))
            features = features_tile(n, chunk_columns(0))
            add_bias(features[:], banks[n], n, False)
            nc.sync.dma_start(out=out_0[n * P : (n + 1) * P, chunk_columns(0)], in_=features[:])
        store_page_scales(1, (0,))
        rest = slice(BANK, T2)
        features = [features_tile(n, rest) for n in range(N_TILES)]
        for n in range(N_TILES):
            read_page(1, banks[N_TILES + n], n, chunk_columns(1))
            add_bias(features[n][:, :BANK], banks[N_TILES + n], n, False)
        for chunk in range(OPENED, CHUNKS):
            weave_and_quantize(chunk)
        store_page_codes(1, slice(S, T2))
        for n in range(N_TILES):
            for chunk in range(OPENED, CHUNKS):
                bank = banks[(2 * n + chunk - OPENED) % 6]
                for g in range(GROUPS):
                    read_page(g, bank, n, chunk_columns(chunk))
                target = features[n][:, chunk * BANK - rest.start : (chunk + 1) * BANK - rest.start]
                add_bias(target, bank, n, n < N_TILES - 1)
            nc.sync.dma_start(out=out_0[n * P : (n + 1) * P, rest], in_=features[n][:])
            if n == 0:
                store_page_scales(1, (1,))
